import numpy as np
import ml_dtypes


def mxq(x, axis, fmt="e4m3"):
    dtype, down = {"e4m3": (ml_dtypes.float8_e4m3fn, 7), "e5m2": (ml_dtypes.float8_e5m2, 14)}[fmt]
    v = np.moveaxis(np.asarray(x, np.float32).astype(ml_dtypes.bfloat16).astype(np.float64), axis, -1)
    blocks = v.reshape(v.shape[:-1] + (-1, 32))
    amax = np.abs(blocks).max(-1, keepdims=True)
    byte = np.maximum(np.where(amax > 0, np.frexp(amax)[1] - 1 + 127, 0) - down, 1)
    scale = np.exp2(byte - 127.0)
    codes = (blocks / scale).astype(np.float32).astype(dtype).astype(np.float64)
    return np.moveaxis((codes * scale).reshape(v.shape), -1, axis)


WIDE = False


def mx_kscale(k):
    if not WIDE:
        return np.ones(k)
    levels = np.array([10, -10, 5, -5, 0])
    if k % 512:
        return np.exp2(np.random.permutation(np.resize(levels, k // 32))).repeat(32)
    a = np.empty((k // 512, 16))
    for p in range(k // 512):
        a[p, :8] = np.random.permutation(np.resize(levels, 8))
        for g in range(8):
            far = levels[np.abs(levels - a[p, g]) >= 10]
            a[p, g + 8] = far[np.random.randint(len(far))]
    return np.exp2(a.ravel()).repeat(32)


def f64(x):
    return np.asarray(x).astype(np.float64)


def striped(idx):
    return np.tile(idx.reshape(-1, 16).T, (8, 1)).astype(np.uint16)


def unstriped(offs):
    return offs[:16].T.reshape(-1).astype(np.int64)


E2M1 = np.array([0.0, 0.5, 1.0, 1.5, 2.0, 3.0, 4.0, 6.0, -0.0, -0.5, -1.0, -1.5, -2.0, -3.0, -4.0, -6.0])


def pack_weight(w, fmt):
    k, n = w.shape
    w = f64(np.asarray(w, np.float32).astype(ml_dtypes.bfloat16)).reshape(k // 32, 32, n)
    amax = np.abs(w).max(1)
    if fmt == "e4m3":
        byte = np.frexp(amax)[1] - 1 + 127 - 7
    else:
        mant, ex = np.frexp(amax / 6.0)
        byte = np.where(mant > 0.5, ex, ex - 1) + 127
    byte = np.clip(np.where(amax > 0, byte, 1), 1, 254)
    scaled = (w * np.exp2(127.0 - byte)[:, None, :]).reshape(k, n).astype(np.float32)
    by_word = np.ascontiguousarray(scaled.reshape(k // 512, 128, 4, n).transpose(0, 1, 3, 2))
    if fmt == "e4m3":
        words = by_word.astype(ml_dtypes.float8_e4m3fn).view(np.uint8)
    else:
        c = by_word.astype(ml_dtypes.float4_e2m1fn).view(np.uint8) & 0xF
        words = (c[..., 0::2] | (c[..., 1::2] << 4)).reshape(k // 512, 128, 2 * n)
    return np.ascontiguousarray(words), np.ascontiguousarray(byte.astype(np.uint8).reshape(k // 512, 16, n))


def unpack_weight(words, scales, fmt):
    g, _, n = scales.shape
    words = np.ascontiguousarray(words).reshape(g, 128, n, -1)
    if fmt == "e4m3":
        vals = words.view(ml_dtypes.float8_e4m3fn).astype(np.float64)
    else:
        nib = np.empty((g, 128, n, 4), np.uint8)
        nib[..., 0::2] = words & 0xF
        nib[..., 1::2] = words >> 4
        vals = E2M1[nib]
    vals = vals * np.repeat(np.exp2(scales.astype(np.float64) - 127.0), 8, axis=1)[..., None]
    return vals.transpose(0, 1, 3, 2).reshape(g * 512, n)


def gelu(v):
    return 0.5 * v * (1.0 + np.tanh(np.sqrt(2.0 / np.pi) * (v + 0.044715 * v**3)))


K, T, S, P, H, N = 1024, 2048, 1024, 512, 1024, 512

def setup_inputs():
    n = np.random.standard_normal
    s = mx_kscale(K)[:, None]
    u = mx_kscale(H)[:, None]
    tab_words, tab_scales = pack_weight(n((K, T)) * s, "e4m3")
    w1_words, w1_scales = pack_weight(0.7 * n((K, H)) / np.sqrt(K) / s, "e2m1")
    w3_words, w3_scales = pack_weight(n((H, N)) / np.sqrt(H) / u, "e4m3")
    perm = np.random.permutation(S)
    return {
        "tab_words": tab_words, "tab_scales": tab_scales,
        "offs": striped(np.random.permutation(T)[:S]),
        "pos1": striped(np.random.permutation(S)[:P]),
        "pos2": striped(perm[:P]),
        "pos3": striped(perm[-P:]),
        "w1_words": w1_words, "w1_scales": w1_scales,
        "w2": (0.8 * n((K, H)) / np.sqrt(K) / s).astype(np.float32),
        "gain": (np.exp(0.3 * n(H)) * u[:, 0]).astype(np.float32),
        "w3_words": w3_words, "w3_scales": w3_scales,
        "guide": (n((K, P)) * s).astype(np.float32),
        "w4": (0.7 * n((K, N)) / np.sqrt(K) / s).astype(np.float32),
    }

def reference(tab_words, tab_scales, offs, pos1, pos2, pos3, w1_words, w1_scales,
              w2, gain, w3_words, w3_scales, guide, w4):
    v = unpack_weight(tab_words, tab_scales, "e4m3")[:, unstriped(offs)]
    head = unpack_weight(w1_words, w1_scales, "e2m1").T @ v
    ann = mxq(f64(w2), 0, "e4m3").T @ v
    d = ann[:, unstriped(pos2)] - ann[:, unstriped(pos3)]
    den = 1.0 + np.exp(head[:, unstriped(pos1)])
    z = f64(gain)[:, None] * np.square(d) / den
    zq = mxq(z, 0, "e4m3")
    gq = mxq(f64(guide), 0, "e4m3")
    return (unpack_weight(w3_words, w3_scales, "e4m3").T @ zq
                 + mxq(f64(w4), 0, "e4m3").T @ gq)

@@ -1,0 +1,347 @@
+from contextlib import ExitStack
+
+import concourse.mybir as mybir
+
+K, T, S, PAIRS, H, N = 1024, 2048, 1024, 512, 1024, 512
+FLOPS = 2 * K * H * S * 2 + 2 * H * N * PAIRS + 2 * K * N * PAIRS
+
+F32 = mybir.dt.float32
+BF16 = mybir.dt.bfloat16
+I32 = mybir.dt.int32
+U32 = mybir.dt.uint32
+U16 = mybir.dt.uint16
+U8 = mybir.dt.uint8
+FP8X4 = mybir.dt.float8_e4m3fn_x4
+FP4X4 = mybir.dt.float4_e2m1fn_x4
+MULT = mybir.AluOpType.mult
+SUBTRACT = mybir.AluOpType.subtract
+SIGMOID = mybir.ActivationFunctionType.Sigmoid
+
+P = 128
+PACK = 4
+K_PASS = P * PACK
+BANK = 512
+BANKS = 8
+HALF = PAIRS // 2
+
+
+def tile_list_annotation_disagreement_kernel(
+    tc, tab_words, tab_scales, offs, pos1, pos2, pos3, w1_words, w1_scales,
+    w2, gain, w3_words, w3_scales, guide, w4, out,
+):
+    nc = tc.nc
+    with ExitStack() as ctx:
+        keep = ctx.enter_context(tc.tile_pool(name="keep", bufs=1))
+        ring = ctx.enter_context(tc.tile_pool(name="ring", bufs=3))
+        psum = ctx.enter_context(tc.psum_pool(name="psum", bufs=1))
+
+        def held(shape, dtype, name):
+            return keep.tile(shape, dtype, name=name, align_bytes=64)
+
+        bank_uses = []
+
+        def next_bank(width):
+            name = "bank%d" % (len(bank_uses) % BANKS)
+            bank_uses.append(name)
+            return psum.tile([P, width], F32, name=name)
+
+        def zeroed_plane(width, name):
+            plane = held([P, width], U8, name)
+            nc.vector.memset(plane[:].bitcast(I32), 0)
+            return plane
+
+        def load_scale_rows(plane, scales):
+            for q in range(4):
+                nc.sync.dma_start(
+                    out=plane[32 * q : 32 * q + 8, :].bitcast(I32),
+                    in_=scales[:, 4 * q : 4 * q + 4, :].bitcast(I32),
+                )
+
+        def load_list(src, name):
+            tile = held(list(src.shape), U16, name)
+            nc.sync.dma_start(tile[:], src)
+            return tile
+
+        def load_rows(src, k_pass, cols, name):
+            raw = held([P, PACK, BANK], F32, name)
+            rows = src[k_pass * K_PASS : (k_pass + 1) * K_PASS, cols]
+            nc.sync.dma_start(out=raw[:], in_=rows.rearrange("(p j) c -> p j c", j=PACK))
+            return raw
+
+        warm = held([P, 16], F32, "warm")
+        nc.vector.memset(warm[:, 0:1], 0.0)
+        nc.scalar.activation(warm[:, 8:9], warm[:, 0:1], SIGMOID, scale=-1.0)
+        tab_plane = zeroed_plane(T, "tab_plane")
+        w1_plane = zeroed_plane(2 * H, "w1_plane")
+        picked_plane1 = zeroed_plane(S, "picked_plane1")
+        w3_plane = zeroed_plane(N, "w3_plane")
+
+        offs_sb = load_list(offs, "offs_sb")
+        pos3_sb = load_list(pos3, "pos3_sb")
+        pos2_sb = load_list(pos2, "pos2_sb")
+        pos1_sb = load_list(pos1, "pos1_sb")
+        tab_sb = [held([P, T], U32, "tab%d" % a) for a in range(2)]
+
+        def load_tab(a, pieces):
+            words = tab_words[a].rearrange("p t i -> p (t i)").bitcast(I32)
+            width = T // pieces
+            for c in range(0, T, width):
+                nc.sync.dma_start(out=tab_sb[a][:, c : c + width].bitcast(I32), in_=words[:, c : c + width])
+
+        load_tab(0, 4)
+        load_scale_rows(tab_plane, tab_scales)
+        w2_raw = {}
+        w2_raw[0, 0] = load_rows(w2, 0, slice(0, BANK), "w2_raw00")
+        w2_raw[1, 0] = load_rows(w2, 1, slice(0, BANK), "w2_raw10")
+        load_tab(1, 1)
+        w1_sb = held([P, 2, 2 * H], U8, "w1_sb")
+        nc.sync.dma_start(
+            out=w1_sb[:].bitcast(I32), in_=w1_words.rearrange("a p c -> p a c").bitcast(I32)
+        )
+        for q in range(4):
+            nc.sync.dma_start(
+                out=w1_plane[32 * q : 32 * q + 4, :].rearrange("r (a c) -> r a c", a=2).bitcast(I32),
+                in_=w1_scales[:, 4 * q : 4 * q + 4, :].rearrange("a r c -> r a c").bitcast(I32),
+            )
+        picked_plane0 = held([P, S], U8, "picked_plane0")
+        nc.vector.tensor_copy(picked_plane0[:], tab_plane[:].indirect(offs_sb[:]))
+        nc.gpsimd.dma_start(
+            out=picked_plane1[0:100, :].bitcast(I32), in_=picked_plane0[4:104, :].bitcast(I32)
+        )
+        gain_sb = held([P, 2, PACK], F32, "gain_sb")
+        nc.sync.dma_start(out=gain_sb[:], in_=gain.rearrange("(b p t) -> p b t", b=2, t=PACK))
+        for a in range(2):
+            w2_raw[a, 1] = load_rows(w2, a, slice(BANK, 2 * BANK), "w2_raw%d1" % a)
+        guide_raw = [load_rows(guide, a, slice(0, PAIRS), "guide_raw%d" % a) for a in range(2)]
+        w4_raw = [load_rows(w4, a, slice(0, N), "w4_raw%d" % a) for a in range(2)]
+        w3_sb = held([P, 2, N], U32, "w3_sb")
+        nc.sync.dma_start(
+            out=w3_sb[:].bitcast(I32),
+            in_=w3_words.rearrange("a p c i -> p a (c i)").bitcast(I32),
+        )
+        load_scale_rows(w3_plane, w3_scales)
+
+        w1_sorted = [held([P, 2, 2 * BANK], U8, "w1_sorted%d" % b) for b in range(2)]
+        w1_sorted_plane = [held([P, 2, BANK], U8, "w1_sorted_plane%d" % b) for b in range(2)]
+
+        def sort_w1(b):
+            cols = slice(b * BANK, (b + 1) * BANK)
+            nc.vector.tensor_copy(
+                w1_sorted[b][:].bitcast(U16).rearrange("p a (t g m) -> p a g t m", t=PACK, m=8),
+                w1_sb[:].bitcast(U16)[:, :, cols].rearrange("p a (g m t) -> p a g t m", t=PACK, m=8),
+            )
+            nc.vector.tensor_copy(
+                w1_sorted_plane[b][:].rearrange("p a (t g m) -> p a g t m", t=PACK, m=16),
+                w1_plane[:].rearrange("p (a c) -> p a c", a=2)[:, :, cols].rearrange(
+                    "p a (g m t) -> p a g t m", t=PACK, m=16
+                ),
+            )
+
+        picked = {}
+
+        def pick_words(a, pieces):
+            picked[a] = held([P, S], U32, "picked%d" % a)
+            width = S // pieces
+            for c in range(0, S, width):
+                nc.vector.tensor_copy(
+                    picked[a][:, c : c + width],
+                    tab_sb[a][:].indirect(offs_sb[:, c // 16 : (c + width) // 16]),
+                )
+
+        def cast(engine, dst, src):
+            if engine == "vector":
+                nc.vector.tensor_copy(dst, src)
+            else:
+                nc.scalar.copy(dst, src)
+
+        def weave(engine, raw):
+            woven = ring.tile([P, BANK, PACK], BF16, name="woven", align_bytes=64)
+            cast(
+                engine,
+                woven[:].rearrange("p (g i) j -> p g j i", i=4),
+                raw[:].rearrange("p j (g i) -> p g j i", i=4),
+            )
+            return woven
+
+        def weave_sorted(engines, raw):
+            woven = ring.tile([P, BANK, PACK], BF16, name="woven", align_bytes=64)
+            dst = woven[:].rearrange("p (t m) j -> p m j t", t=PACK)
+            src = raw[:].rearrange("p j (m t) -> p m j t", t=PACK)
+            share = P // len(engines)
+            for e, engine in enumerate(engines):
+                part = slice(e * share, (e + 1) * share)
+                cast(engine, dst[:, part], src[:, part])
+            return woven
+
+        def quantize(values, width, name):
+            codes = held([P, width], U32, name + "_codes")
+            plane = held([P, width], U8, name + "_plane")
+            nc.vector.quantize_mx(out=codes[:].bitcast(FP8X4), scales=plane[:], in_=values)
+            return codes, plane
+
+        def flat(woven):
+            return woven[:].rearrange("p c j -> p (c j)")
+
+        w2_mx = {}
+
+        def first_stage(i, stationary, moving_planes, window):
+            for h in range(2):
+                acc = next_bank(BANK)
+                for a in range(2):
+                    codes, plane = stationary(a, i)
+                    nc.tensor.matmul_mx(
+                        out=acc[:],
+                        lhsT=codes,
+                        lhsT_scale=plane,
+                        rhs=picked[a][:, h * BANK : (h + 1) * BANK].bitcast(FP8X4),
+                        rhs_scale=moving_planes[a][:, h * BANK : (h + 1) * BANK],
+                        start=(a == 0),
+                        stop=(a == 1),
+                    )
+                nc.scalar.copy(window[:, h * BANK : (h + 1) * BANK], acc[:])
+
+        def w1_columns(a, i):
+            b, t = divmod(i, PACK)
+            codes = w1_sorted[b][:, a, 2 * P * t : 2 * P * (t + 1)].bitcast(FP4X4)
+            return codes, w1_sorted_plane[b][:, a, P * t : P * (t + 1)]
+
+        def w2_columns(a, i):
+            b, t = divmod(i, PACK)
+            codes, plane = w2_mx[a, b]
+            return codes[:, P * t : P * (t + 1)].bitcast(FP8X4), plane[:, P * t : P * (t + 1)]
+
+        gate = {}
+
+        def head_tile(i):
+            window = ring.tile([P, S], F32, name="head", bufs=2)
+            first_stage(i, w1_columns, [picked_plane0[:], picked_plane1[:]], window)
+            gate[i] = held([P, PAIRS], F32, "gate%d" % i)
+            nc.scalar.activation(gate[i][:], window[:].indirect(pos1_sb[:]), SIGMOID, scale=-1.0)
+
+        ann = {}
+        second = {}
+        diff = {}
+        scaled = {}
+
+        def ann_tile(i):
+            ann[i] = held([P, S], F32, "ann%d" % i)
+            first_stage(i, w2_columns, [picked_plane0[:], picked_plane0[4:P, :]], ann[i])
+
+        def pick_second(i):
+            second[i] = ring.tile([P, PAIRS], F32, name="second")
+            nc.vector.tensor_copy(second[i][:], ann[i][:].indirect(pos3_sb[:]))
+
+        def subtract(i):
+            b, t = divmod(i, PACK)
+            if t == 0:
+                diff[b] = held([P, PACK, PAIRS], F32, "w2_raw0%d" % b)
+            nc.vector.tensor_tensor(
+                diff[b][:, t, :], ann[i][:].indirect(pos2_sb[:]), second[i][:], SUBTRACT
+            )
+
+        def scale(i):
+            b, t = divmod(i, PACK)
+            if t == 0:
+                scaled[b] = held([P, PACK, PAIRS], F32, "w2_raw1%d" % b)
+            nc.vector.scalar_tensor_tensor(
+                scaled[b][:, t, :], diff[b][:, t, :], gain_sb[:, b, t : t + 1], gate[i][:], MULT, MULT
+            )
+
+        z_woven = {}
+        z_mx = {}
+
+        def make_z(b, half):
+            cols = slice(half * HALF, (half + 1) * HALF)
+            z_woven[b, half] = ring.tile([P, HALF, PACK], BF16, name="z_woven", bufs=2, align_bytes=64)
+            nc.vector.tensor_tensor(
+                z_woven[b, half][:].rearrange("p (g i) t -> p g t i", i=4),
+                diff[b][:, :, cols].rearrange("p t (g i) -> p g t i", i=4),
+                scaled[b][:, :, cols].rearrange("p t (g i) -> p g t i", i=4),
+                MULT,
+            )
+
+        def quantize_z(b, half):
+            z_mx[b, half] = quantize(flat(z_woven[b, half]), HALF, "z%d%d" % (b, half))
+
+        def make_w2(a, b, engines):
+            woven = weave_sorted(engines, w2_raw[a, b])
+            w2_mx[a, b] = quantize(flat(woven), BANK, "w2_%d%d" % (a, b))
+
+        pick_words(0, 1)
+        make_w2(0, 0, ["scalar"])
+        make_w2(1, 0, ["scalar", "vector"])
+        pick_words(1, 2)
+        sort_w1(0)
+        ann_tile(0)
+        ann_tile(1)
+        ann_tile(2)
+        head_tile(0)
+        ann_tile(3)
+        pick_second(0)
+        pick_second(1)
+        sort_w1(1)
+        head_tile(1)
+
+        tiles = 2 * PACK
+        for i in range(tiles):
+            subtract(i)
+            if i < 2:
+                make_w2(i, 1, ["vector"])
+            if i >= 1:
+                scale(i - 1)
+            if PACK <= i + 3 < tiles:
+                ann_tile(i + 3)
+            if i + 2 < tiles:
+                head_tile(i + 2)
+            if i + 2 < tiles:
+                pick_second(i + 2)
+            if i == PACK:
+                make_z(0, 0)
+                make_z(0, 1)
+                quantize_z(0, 0)
+                quantize_z(0, 1)
+
+        guide_mx = []
+        w4_mx = []
+        for a in range(2):
+            guide_mx.append(quantize(flat(weave("scalar", guide_raw[a])), PAIRS, "guide%d" % a))
+            w4_mx.append(quantize(flat(weave("vector" if a == 0 else "scalar", w4_raw[a])), N, "w4_%d" % a))
+        scale(tiles - 1)
+        make_z(1, 0)
+        make_z(1, 1)
+        quantize_z(1, 0)
+        quantize_z(1, 1)
+
+        for half in range(2):
+            cols = slice(half * HALF, (half + 1) * HALF)
+            result = held([P, N // P, HALF], F32, "result%d" % half)
+            for n in range(N // P):
+                rows = slice(n * P, (n + 1) * P)
+                acc = next_bank(HALF)
+                guide_passes = [
+                    (w4_mx[a][0][:, rows], w4_mx[a][1][:, rows], guide_mx[a][0][:, cols], guide_mx[a][1][:, cols])
+                    for a in range(2)
+                ]
+                z_passes = [
+                    (w3_sb[:, b, rows], w3_plane[4 * b : P, rows], z_mx[b, half][0][:], z_mx[b, half][1][:])
+                    for b in range(2)
+                ]
+                passes = [z_passes[0]] + guide_passes + [z_passes[1]]
+                for j, (lhs, lhs_plane, rhs, rhs_plane) in enumerate(passes):
+                    nc.tensor.matmul_mx(
+                        out=acc[:],
+                        lhsT=lhs.bitcast(FP8X4),
+                        lhsT_scale=lhs_plane,
+                        rhs=rhs.bitcast(FP8X4),
+                        rhs_scale=rhs_plane,
+                        start=(j == 0),
+                        stop=(j == len(passes) - 1),
+                    )
+                engine = "vector" if half == 1 and n % 2 == 1 else "scalar"
+                cast(engine, result[:, n, :], acc[:])
+                if half == 1:
+                    nc.sync.dma_start(out=out[rows, cols], in_=result[:, n, :])
+            if half == 0:
+                nc.sync.dma_start(
+                    out=out[:, cols].rearrange("(n p) m -> p n m", p=P), in_=result[:]
+                )

@@ -154,17 +154,18 @@ def tile_list_annotation_disagreement_kernel(
             else:
                 nc.scalar.copy(dst, src)
 
-        def weave(engine, raw):
-            woven = ring.tile([P, BANK, PACK], BF16, name="woven", align_bytes=64)
+        def weave(engine, raw, cols):
+            width = cols.stop - cols.start
+            woven = ring.tile([P, width, PACK], BF16, name="woven", bufs=4, align_bytes=64)
             cast(
                 engine,
                 woven[:].rearrange("p (g i) j -> p g j i", i=4),
-                raw[:].rearrange("p j (g i) -> p g j i", i=4),
+                raw[:, :, cols].rearrange("p j (g i) -> p g j i", i=4),
             )
             return woven
 
         def weave_sorted(engines, raw):
-            woven = ring.tile([P, BANK, PACK], BF16, name="woven", align_bytes=64)
+            woven = ring.tile([P, BANK, PACK], BF16, name="woven", bufs=4, align_bytes=64)
             dst = woven[:].rearrange("p (t m) j -> p m j t", t=PACK)
             src = raw[:].rearrange("p j (m t) -> p m j t", t=PACK)
             share = P // len(engines)
@@ -252,7 +253,7 @@ def tile_list_annotation_disagreement_kernel(
 
         def make_z(b, half):
             cols = slice(half * HALF, (half + 1) * HALF)
-            z_woven[b, half] = ring.tile([P, HALF, PACK], BF16, name="z_woven", bufs=2, align_bytes=64)
+            z_woven[b, half] = ring.tile([P, HALF, PACK], BF16, name="z_woven%d" % b, bufs=2 - b, align_bytes=64)
             nc.vector.tensor_tensor(
                 z_woven[b, half][:].rearrange("p (g i) t -> p g t i", i=4),
                 diff[b][:, :, cols].rearrange("p t (g i) -> p g t i", i=4),
@@ -267,32 +268,42 @@ def tile_list_annotation_disagreement_kernel(
             woven = weave_sorted(engines, w2_raw[a, b])
             w2_mx[a, b] = quantize(flat(woven), BANK, "w2_%d%d" % (a, b))
 
+        guide_mx = {}
+        w4_mx = {}
+
+        def make_w4(a, engine):
+            w4_mx[a] = quantize(flat(weave(engine, w4_raw[a], slice(0, N))), N, "w4_%d" % a)
+
+        def make_guide(a, half, engine):
+            cols = slice(half * HALF, (half + 1) * HALF)
+            guide_mx[a, half] = quantize(flat(weave(engine, guide_raw[a], cols)), HALF, "guide%d%d" % (a, half))
+
         pick_words(0, 1)
         make_w2(0, 0, ["scalar"])
-        make_w2(1, 0, ["scalar", "vector"])
+        make_w2(1, 0, ["vector"])
         pick_words(1, 2)
         sort_w1(0)
         ann_tile(0)
         ann_tile(1)
-        ann_tile(2)
         head_tile(0)
+        ann_tile(2)
         ann_tile(3)
         pick_second(0)
+        make_w2(0, 1, ["vector"])
         pick_second(1)
+        make_w2(1, 1, ["vector"])
         sort_w1(1)
         head_tile(1)
 
         tiles = 2 * PACK
         for i in range(tiles):
             subtract(i)
-            if i < 2:
-                make_w2(i, 1, ["vector"])
             if i >= 1:
                 scale(i - 1)
-            if PACK <= i + 3 < tiles:
-                ann_tile(i + 3)
             if i + 2 < tiles:
                 head_tile(i + 2)
+            if PACK <= i + 4 < tiles:
+                ann_tile(i + 4)
             if i + 2 < tiles:
                 pick_second(i + 2)
             if i == PACK:
@@ -300,16 +311,20 @@ def tile_list_annotation_disagreement_kernel(
                 make_z(0, 1)
                 quantize_z(0, 0)
                 quantize_z(0, 1)
-
-        guide_mx = []
-        w4_mx = []
-        for a in range(2):
-            guide_mx.append(quantize(flat(weave("scalar", guide_raw[a])), PAIRS, "guide%d" % a))
-            w4_mx.append(quantize(flat(weave("vector" if a == 0 else "scalar", w4_raw[a])), N, "w4_%d" % a))
+            if i == 3:
+                make_w4(0, "scalar")
+            if i == 2:
+                make_guide(0, 0, "vector")
+                make_guide(0, 1, "scalar")
+            if i == 5:
+                make_w4(1, "scalar")
+            if i == 5:
+                make_guide(1, 0, "scalar")
         scale(tiles - 1)
         make_z(1, 0)
-        make_z(1, 1)
         quantize_z(1, 0)
+        make_guide(1, 1, "scalar")
+        make_z(1, 1)
         quantize_z(1, 1)
 
         for half in range(2):
@@ -319,7 +334,7 @@ def tile_list_annotation_disagreement_kernel(
                 rows = slice(n * P, (n + 1) * P)
                 acc = next_bank(HALF)
                 guide_passes = [
-                    (w4_mx[a][0][:, rows], w4_mx[a][1][:, rows], guide_mx[a][0][:, cols], guide_mx[a][1][:, cols])
+                    (w4_mx[a][0][:, rows], w4_mx[a][1][:, rows], guide_mx[a, half][0][:], guide_mx[a, half][1][:])
                     for a in range(2)
                 ]
                 z_passes = [

@@ -105,13 +105,13 @@ def tile_list_annotation_disagreement_kernel(
             )
         picked_plane0 = held([P, S], U8, "picked_plane0")
         nc.vector.tensor_copy(picked_plane0[:], tab_plane[:].indirect(offs_sb[:]))
-        nc.gpsimd.dma_start(
+        nc.sync.dma_start(
             out=picked_plane1[0:100, :].bitcast(I32), in_=picked_plane0[4:104, :].bitcast(I32)
         )
-        gain_sb = held([P, 2, PACK], F32, "gain_sb")
-        nc.sync.dma_start(out=gain_sb[:], in_=gain.rearrange("(b p t) -> p b t", b=2, t=PACK))
         for a in range(2):
             w2_raw[a, 1] = load_rows(w2, a, slice(BANK, 2 * BANK), "w2_raw%d1" % a)
+        gain_sb = held([P, 2, PACK], F32, "gain_sb")
+        nc.sync.dma_start(out=gain_sb[:], in_=gain.rearrange("(b p t) -> p b t", b=2, t=PACK))
         guide_raw = [load_rows(guide, a, slice(0, PAIRS), "guide_raw%d" % a) for a in range(2)]
         w4_raw = [load_rows(w4, a, slice(0, N), "w4_raw%d" % a) for a in range(2)]
         w3_sb = held([P, 2, N], U32, "w3_sb")

@@ -68,9 +68,6 @@ def tile_list_annotation_disagreement_kernel(
             nc.sync.dma_start(out=raw[:], in_=rows.rearrange("(p j) c -> p j c", j=PACK))
             return raw
 
-        warm = held([P, 16], F32, "warm")
-        nc.vector.memset(warm[:, 0:1], 0.0)
-        nc.scalar.activation(warm[:, 8:9], warm[:, 0:1], SIGMOID, scale=-1.0)
         tab_plane = zeroed_plane(T, "tab_plane")
         w1_plane = zeroed_plane(2 * H, "w1_plane")
         picked_plane1 = zeroed_plane(S, "picked_plane1")

@@ -16,6 +16,7 @@ FP4X4 = mybir.dt.float4_e2m1fn_x4
 MULT = mybir.AluOpType.mult
 SUBTRACT = mybir.AluOpType.subtract
 SIGMOID = mybir.ActivationFunctionType.Sigmoid
+COPY = mybir.ActivationFunctionType.Copy
 
 P = 128
 PACK = 4
@@ -23,6 +24,8 @@ K_PASS = P * PACK
 BANK = 512
 BANKS = 8
 HALF = PAIRS // 2
+TILES = H // P
+SLOT = 4 * T
 
 
 def tile_list_annotation_disagreement_kernel(
@@ -32,97 +35,94 @@ def tile_list_annotation_disagreement_kernel(
     nc = tc.nc
     with ExitStack() as ctx:
         keep = ctx.enter_context(tc.tile_pool(name="keep", bufs=1))
-        ring = ctx.enter_context(tc.tile_pool(name="ring", bufs=3))
+        stage = ctx.enter_context(tc.tile_pool(name="stage", bufs=1))
+        ring = ctx.enter_context(tc.tile_pool(name="ring", bufs=4))
         psum = ctx.enter_context(tc.psum_pool(name="psum", bufs=1))
 
         def held(shape, dtype, name):
             return keep.tile(shape, dtype, name=name, align_bytes=64)
 
-        bank_uses = []
+        def staged(shape, dtype, name, offset):
+            return stage.tile(shape, dtype, name=name, align_bytes=64, offset=offset)
 
-        def next_bank(width):
-            name = "bank%d" % (len(bank_uses) % BANKS)
-            bank_uses.append(name)
-            return psum.tile([P, width], F32, name=name)
-
-        def zeroed_plane(width, name):
-            plane = held([P, width], U8, name)
+        def zeroed(shape, name):
+            plane = held(shape, U8, name)
             nc.vector.memset(plane[:].bitcast(I32), 0)
             return plane
-
-        def load_scale_rows(plane, scales):
-            for q in range(4):
-                nc.sync.dma_start(
-                    out=plane[32 * q : 32 * q + 8, :].bitcast(I32),
-                    in_=scales[:, 4 * q : 4 * q + 4, :].bitcast(I32),
-                )
 
         def load_list(src, name):
             tile = held(list(src.shape), U16, name)
             nc.sync.dma_start(tile[:], src)
             return tile
 
-        def load_rows(src, k_pass, cols, name):
-            raw = held([P, PACK, BANK], F32, name)
+        def load_rows(src, k_pass, cols, name, slot):
+            raw = staged([P, PACK, BANK], F32, name, slot * SLOT)
             rows = src[k_pass * K_PASS : (k_pass + 1) * K_PASS, cols]
             nc.sync.dma_start(out=raw[:], in_=rows.rearrange("(p j) c -> p j c", j=PACK))
             return raw
 
-        tab_plane = zeroed_plane(T, "tab_plane")
-        w1_plane = zeroed_plane(2 * H, "w1_plane")
-        picked_plane1 = zeroed_plane(S, "picked_plane1")
-        w3_plane = zeroed_plane(N, "w3_plane")
+        def load_tab(a, slot):
+            words = staged([P, T], U32, "tab%d" % a, slot * SLOT)
+            nc.sync.dma_start(
+                out=words[:].bitcast(I32), in_=tab_words[a].rearrange("p t i -> p (t i)").bitcast(I32)
+            )
+            return words
 
         offs_sb = load_list(offs, "offs_sb")
+        tab_rows = staged([P, T], U8, "tab_rows", SLOT - T // 2)
+        nc.sync.dma_start(
+            out=tab_rows[0:32, :].bitcast(I32), in_=tab_scales.rearrange("a q t -> q a t").bitcast(I32)
+        )
+        w1_plane = zeroed([P, 2 * H], "w1_plane")
+        nc.vector.memset(tab_rows[32:64, :].bitcast(I32), 0)
+        nc.vector.memset(tab_rows[64:128, :].bitcast(I32), 0)
+        picked_plane = zeroed([P, 2 * S], "picked_plane")
+        w3_plane = zeroed([P, N], "w3_plane")
+        pos1_sb = load_list(pos1, "pos1_sb")
         pos3_sb = load_list(pos3, "pos3_sb")
         pos2_sb = load_list(pos2, "pos2_sb")
-        pos1_sb = load_list(pos1, "pos1_sb")
-        tab_sb = [held([P, T], U32, "tab%d" % a) for a in range(2)]
-
-        def load_tab(a, pieces):
-            words = tab_words[a].rearrange("p t i -> p (t i)").bitcast(I32)
-            width = T // pieces
-            for c in range(0, T, width):
-                nc.sync.dma_start(out=tab_sb[a][:, c : c + width].bitcast(I32), in_=words[:, c : c + width])
-
-        load_tab(0, 4)
-        load_scale_rows(tab_plane, tab_scales)
-        w2_raw = {}
-        w2_raw[0, 0] = load_rows(w2, 0, slice(0, BANK), "w2_raw00")
-        w2_raw[1, 0] = load_rows(w2, 1, slice(0, BANK), "w2_raw10")
-        load_tab(1, 1)
-        w1_sb = held([P, 2, 2 * H], U8, "w1_sb")
+        w1_sb = held([P, 2, 2 * H], U8, "slot_e")
         nc.sync.dma_start(
             out=w1_sb[:].bitcast(I32), in_=w1_words.rearrange("a p c -> p a c").bitcast(I32)
         )
+        tab_sb = [load_tab(0, 3)]
         for q in range(4):
-            nc.sync.dma_start(
+            nc.scalar.dma_start(
                 out=w1_plane[32 * q : 32 * q + 4, :].rearrange("r (a c) -> r a c", a=2).bitcast(I32),
                 in_=w1_scales[:, 4 * q : 4 * q + 4, :].rearrange("a r c -> r a c").bitcast(I32),
             )
-        picked_plane0 = held([P, S], U8, "picked_plane0")
-        nc.vector.tensor_copy(picked_plane0[:], tab_plane[:].indirect(offs_sb[:]))
-        nc.sync.dma_start(
-            out=picked_plane1[0:100, :].bitcast(I32), in_=picked_plane0[4:104, :].bitcast(I32)
-        )
-        for a in range(2):
-            w2_raw[a, 1] = load_rows(w2, a, slice(BANK, 2 * BANK), "w2_raw%d1" % a)
         gain_sb = held([P, 2, PACK], F32, "gain_sb")
-        nc.sync.dma_start(out=gain_sb[:], in_=gain.rearrange("(b p t) -> p b t", b=2, t=PACK))
-        guide_raw = [load_rows(guide, a, slice(0, PAIRS), "guide_raw%d" % a) for a in range(2)]
-        w4_raw = [load_rows(w4, a, slice(0, N), "w4_raw%d" % a) for a in range(2)]
-        w3_sb = held([P, 2, N], U32, "w3_sb")
-        nc.sync.dma_start(
-            out=w3_sb[:].bitcast(I32),
-            in_=w3_words.rearrange("a p c i -> p a (c i)").bitcast(I32),
-        )
-        load_scale_rows(w3_plane, w3_scales)
+        nc.gpsimd.dma_start(out=gain_sb[:], in_=gain.rearrange("(b p t) -> p b t", b=2, t=PACK))
+        for q in range(4):
+            nc.gpsimd.dma_start(
+                out=w3_plane[32 * q : 32 * q + 8, :].bitcast(I32),
+                in_=w3_scales[:, 4 * q : 4 * q + 4, :].bitcast(I32),
+            )
 
-        w1_sorted = [held([P, 2, 2 * BANK], U8, "w1_sorted%d" % b) for b in range(2)]
-        w1_sorted_plane = [held([P, 2, BANK], U8, "w1_sorted_plane%d" % b) for b in range(2)]
+        picked_rows = staged([P, S], U8, "picked_rows", 2 * SLOT)
+        nc.vector.tensor_copy(picked_rows[:], tab_rows[:].indirect(offs_sb[:]))
+        for q in range(4):
+            nc.sync.dma_start(
+                out=picked_plane[32 * q : 32 * q + 4, :].bitcast(I32),
+                in_=picked_rows[8 * q : 8 * q + 8, :].bitcast(I32),
+            )
 
-        def sort_w1(b):
+        tab_sb.append(load_tab(1, 0))
+        picked = [held([P, S], U32, "picked%d" % a) for a in range(2)]
+
+        def pick_words(a, h):
+            nc.vector.tensor_copy(
+                picked[a][:, h * BANK : (h + 1) * BANK],
+                tab_sb[a][:].indirect(offs_sb[:, h * BANK // 16 : (h + 1) * BANK // 16]),
+            )
+
+        w1_sorted = {}
+        w1_sorted_plane = {}
+
+        def sort_w1(b, words_slot, plane_slot):
             cols = slice(b * BANK, (b + 1) * BANK)
+            w1_sorted[b] = held([P, 2, 2 * BANK], U8, words_slot)
+            w1_sorted_plane[b] = held([P, 2, BANK], U8, plane_slot)
             nc.vector.tensor_copy(
                 w1_sorted[b][:].bitcast(U16).rearrange("p a (t g m) -> p a g t m", t=PACK, m=8),
                 w1_sb[:].bitcast(U16)[:, :, cols].rearrange("p a (g m t) -> p a g t m", t=PACK, m=8),
@@ -134,211 +134,173 @@ def tile_list_annotation_disagreement_kernel(
                 ),
             )
 
-        picked = {}
-
-        def pick_words(a, pieces):
-            picked[a] = held([P, S], U32, "picked%d" % a)
-            width = S // pieces
-            for c in range(0, S, width):
-                nc.vector.tensor_copy(
-                    picked[a][:, c : c + width],
-                    tab_sb[a][:].indirect(offs_sb[:, c // 16 : (c + width) // 16]),
-                )
-
-        def cast(engine, dst, src):
-            if engine == "vector":
-                nc.vector.tensor_copy(dst, src)
-            else:
-                nc.scalar.copy(dst, src)
-
-        def weave(engine, raw, cols):
-            width = cols.stop - cols.start
-            woven = ring.tile([P, width, PACK], BF16, name="woven", bufs=4, align_bytes=64)
-            cast(
-                engine,
+        def weave(raw, woven):
+            nc.vector.tensor_copy(
                 woven[:].rearrange("p (g i) j -> p g j i", i=4),
-                raw[:, :, cols].rearrange("p j (g i) -> p g j i", i=4),
+                raw[:].rearrange("p j (g i) -> p g j i", i=4),
             )
-            return woven
 
-        def weave_sorted(engines, raw):
-            woven = ring.tile([P, BANK, PACK], BF16, name="woven", bufs=4, align_bytes=64)
-            dst = woven[:].rearrange("p (t m) j -> p m j t", t=PACK)
-            src = raw[:].rearrange("p j (m t) -> p m j t", t=PACK)
-            share = P // len(engines)
-            for e, engine in enumerate(engines):
-                part = slice(e * share, (e + 1) * share)
-                cast(engine, dst[:, part], src[:, part])
-            return woven
+        def weave_sorted(raw, woven):
+            nc.vector.tensor_copy(
+                woven[:].rearrange("p (t m) j -> p m j t", t=PACK),
+                raw[:].rearrange("p j (m t) -> p m j t", t=PACK),
+            )
 
-        def quantize(values, width, name):
+        def quantize(woven, name):
+            width = woven.shape[1]
             codes = held([P, width], U32, name + "_codes")
             plane = held([P, width], U8, name + "_plane")
-            nc.vector.quantize_mx(out=codes[:].bitcast(FP8X4), scales=plane[:], in_=values)
+            nc.vector.quantize_mx(
+                out=codes[:].bitcast(FP8X4), scales=plane[:], in_=woven[:].rearrange("p c j -> p (c j)")
+            )
             return codes, plane
 
-        def flat(woven):
-            return woven[:].rearrange("p c j -> p (c j)")
-
-        w2_mx = {}
-
-        def first_stage(i, stationary, moving_planes, window):
-            for h in range(2):
-                acc = next_bank(BANK)
-                for a in range(2):
-                    codes, plane = stationary(a, i)
-                    nc.tensor.matmul_mx(
-                        out=acc[:],
-                        lhsT=codes,
-                        lhsT_scale=plane,
-                        rhs=picked[a][:, h * BANK : (h + 1) * BANK].bitcast(FP8X4),
-                        rhs_scale=moving_planes[a][:, h * BANK : (h + 1) * BANK],
-                        start=(a == 0),
-                        stop=(a == 1),
-                    )
-                nc.scalar.copy(window[:, h * BANK : (h + 1) * BANK], acc[:])
+        def product_half(stationary, i, h, bank, window):
+            acc = psum.tile([P, BANK], F32, name="bank%d" % (bank % BANKS))
+            cols = slice(h * BANK, (h + 1) * BANK)
+            order = (0, 1) if i < 2 else (1, 0)
+            for a in order:
+                codes, plane = stationary(a, i)
+                nc.tensor.matmul_mx(
+                    out=acc[:],
+                    lhsT=codes,
+                    lhsT_scale=plane,
+                    rhs=picked[a][:, cols].bitcast(FP8X4),
+                    rhs_scale=picked_plane[:, a * S + h * BANK : a * S + (h + 1) * BANK],
+                    start=(a == order[0]),
+                    stop=(a == order[1]),
+                )
+            nc.scalar.copy(window[:, cols], acc[:])
 
         def w1_columns(a, i):
             b, t = divmod(i, PACK)
             codes = w1_sorted[b][:, a, 2 * P * t : 2 * P * (t + 1)].bitcast(FP4X4)
             return codes, w1_sorted_plane[b][:, a, P * t : P * (t + 1)]
 
+        w2_mx = {}
+
         def w2_columns(a, i):
             b, t = divmod(i, PACK)
             codes, plane = w2_mx[a, b]
             return codes[:, P * t : P * (t + 1)].bitcast(FP8X4), plane[:, P * t : P * (t + 1)]
 
-        gate = {}
+        head = {}
+        gate = [held([P, PACK, PAIRS], F32, "gate0")]
+        gate_half = [held([P, PACK, HALF], F32, "gate1%d" % h) for h in range(2)]
 
-        def head_tile(i):
-            window = ring.tile([P, S], F32, name="head", bufs=2)
-            first_stage(i, w1_columns, [picked_plane0[:], picked_plane1[:]], window)
-            gate[i] = held([P, PAIRS], F32, "gate%d" % i)
-            nc.scalar.activation(gate[i][:], window[:].indirect(pos1_sb[:]), SIGMOID, scale=-1.0)
+        def head_block(b, first_bank):
+            for t in range(PACK):
+                head[b, t] = ring.tile([P, S], F32, name="head")
+            for h in range(2):
+                for t in range(PACK):
+                    product_half(w1_columns, PACK * b + t, h, first_bank + t, head[b, t])
 
         ann = {}
         second = {}
         diff = {}
-        scaled = {}
+        weighted = [held([P, PACK, PAIRS], F32, "weighted%d" % b) for b in range(2)]
 
         def ann_tile(i):
             ann[i] = held([P, S], F32, "ann%d" % i)
-            first_stage(i, w2_columns, [picked_plane0[:], picked_plane0[4:P, :]], ann[i])
+            for h in range(2):
+                product_half(w2_columns, i, h, 4 + 2 * i + h, ann[i])
 
         def pick_second(i):
             second[i] = ring.tile([P, PAIRS], F32, name="second")
-            nc.vector.tensor_copy(second[i][:], ann[i][:].indirect(pos3_sb[:]))
+            if i < TILES - 1:
+                nc.scalar.activation(second[i][:], ann[i][:].indirect(pos3_sb[:]), COPY)
+            else:
+                nc.vector.tensor_copy(second[i][:], ann[i][:].indirect(pos3_sb[:]))
 
         def subtract(i):
-            b, t = divmod(i, PACK)
-            if t == 0:
-                diff[b] = held([P, PACK, PAIRS], F32, "w2_raw0%d" % b)
-            nc.vector.tensor_tensor(
-                diff[b][:, t, :], ann[i][:].indirect(pos2_sb[:]), second[i][:], SUBTRACT
-            )
+            diff[i] = ring.tile([P, PAIRS], F32, name="diff", bufs=2)
+            nc.vector.tensor_tensor(diff[i][:], ann[i][:].indirect(pos2_sb[:]), second[i][:], SUBTRACT)
 
-        def scale(i):
+        def square(i):
             b, t = divmod(i, PACK)
-            if t == 0:
-                scaled[b] = held([P, PACK, PAIRS], F32, "w2_raw1%d" % b)
             nc.vector.scalar_tensor_tensor(
-                scaled[b][:, t, :], diff[b][:, t, :], gain_sb[:, b, t : t + 1], gate[i][:], MULT, MULT
+                weighted[b][:, t, :], diff[i][:], gain_sb[:, b, t : t + 1], diff[i][:], MULT, MULT
             )
 
-        z_woven = {}
-        z_mx = {}
-
-        def make_z(b, half):
-            cols = slice(half * HALF, (half + 1) * HALF)
-            z_woven[b, half] = ring.tile([P, HALF, PACK], BF16, name="z_woven%d" % b, bufs=2 - b, align_bytes=64)
+        def make_z(values, gates, name):
+            width = values.shape[2]
+            woven = held([P, width, PACK], BF16, name + "_woven")
             nc.vector.tensor_tensor(
-                z_woven[b, half][:].rearrange("p (g i) t -> p g t i", i=4),
-                diff[b][:, :, cols].rearrange("p t (g i) -> p g t i", i=4),
-                scaled[b][:, :, cols].rearrange("p t (g i) -> p g t i", i=4),
+                woven[:].rearrange("p (g i) t -> p g t i", i=4),
+                values.rearrange("p t (g i) -> p g t i", i=4),
+                gates.rearrange("p t (g i) -> p g t i", i=4),
                 MULT,
             )
+            return woven
 
-        def quantize_z(b, half):
-            z_mx[b, half] = quantize(flat(z_woven[b, half]), HALF, "z%d%d" % (b, half))
-
-        def make_w2(a, b, engines):
-            woven = weave_sorted(engines, w2_raw[a, b])
-            w2_mx[a, b] = quantize(flat(woven), BANK, "w2_%d%d" % (a, b))
-
-        guide_mx = {}
-        w4_mx = {}
-
-        def make_w4(a, engine):
-            w4_mx[a] = quantize(flat(weave(engine, w4_raw[a], slice(0, N))), N, "w4_%d" % a)
-
-        def make_guide(a, half, engine):
-            cols = slice(half * HALF, (half + 1) * HALF)
-            guide_mx[a, half] = quantize(flat(weave(engine, guide_raw[a], cols)), HALF, "guide%d%d" % (a, half))
-
+        sort_w1(0, "w1_sorted0", "w1_sorted_plane0")
+        pick_words(0, 0)
         pick_words(0, 1)
-        make_w2(0, 0, ["scalar"])
-        make_w2(1, 0, ["vector"])
-        pick_words(1, 2)
-        sort_w1(0)
+        pick_words(1, 0)
+        pick_words(1, 1)
+        head_block(0, 0)
+
+        slots = [1, 2, 3, 0]
+        pieces = [(a, b) for b in range(2) for a in range(2)]
+        w2_raw = [load_rows(w2, a, slice(b * BANK, (b + 1) * BANK), "w2_raw%d%d" % (a, b), slot) for (a, b), slot in zip(pieces, slots)]
+        for n, (a, b) in enumerate(pieces):
+            woven = held([P, BANK, PACK], BF16, "woven%d" % n)
+            weave_sorted(w2_raw[n], woven)
+            w2_mx[a, b] = quantize(woven, "w2_%d%d" % (a, b))
+        sort_w1(1, "woven0", "woven1")
+
+        late = [(guide, 0), (guide, 1), (w4, 0), (w4, 1)]
+        late_raw = [load_rows(src, a, slice(0, BANK), "late_raw%d" % slot, slot) for (src, a), slot in zip(late, slots)]
+        w3_sb = held([P, 2, N], U32, "slot_e")
+        nc.sync.dma_start(
+            out=w3_sb[:].bitcast(I32), in_=w3_words.rearrange("a p c i -> p a (c i)").bitcast(I32)
+        )
+        late_woven = {}
+        late_mx = {}
+
         ann_tile(0)
-        ann_tile(1)
-        head_tile(0)
-        ann_tile(2)
-        ann_tile(3)
-        pick_second(0)
-        make_w2(0, 1, ["vector"])
-        pick_second(1)
-        make_w2(1, 1, ["vector"])
-        sort_w1(1)
-        head_tile(1)
-
-        tiles = 2 * PACK
-        for i in range(tiles):
+        for i in range(TILES):
+            if i + 1 < TILES:
+                ann_tile(i + 1)
+            pick_second(i)
+            if 2 <= i < 2 + PACK:
+                t = i - 2
+                nc.scalar.activation(gate[0][:, t, :], head[0, t][:].indirect(pos1_sb[:]), SIGMOID, scale=-1.0)
+            if i < len(late):
+                late_woven[i] = held([P, BANK, PACK], BF16, "woven%d" % (2 + i % 2))
+                weave(late_raw[i], late_woven[i])
             subtract(i)
+            if i < len(late):
+                late_mx[i] = quantize(late_woven[i], "late%d" % i)
             if i >= 1:
-                scale(i - 1)
-            if i + 2 < tiles:
-                head_tile(i + 2)
-            if PACK <= i + 4 < tiles:
-                ann_tile(i + 4)
-            if i + 2 < tiles:
-                pick_second(i + 2)
-            if i == PACK:
-                make_z(0, 0)
-                make_z(0, 1)
-                quantize_z(0, 0)
-                quantize_z(0, 1)
-            if i == 3:
-                make_w4(0, "scalar")
-            if i == 2:
-                make_guide(0, 0, "vector")
-                make_guide(0, 1, "scalar")
-            if i == 5:
-                make_w4(1, "scalar")
-            if i == 5:
-                make_guide(1, 0, "scalar")
-        scale(tiles - 1)
-        make_z(1, 0)
-        quantize_z(1, 0)
-        make_guide(1, 1, "scalar")
-        make_z(1, 1)
-        quantize_z(1, 1)
+                square(i - 1)
+            if i == TILES - 2:
+                z0_woven = make_z(weighted[0][:], gate[0][:], "z0")
+            if i == TILES - 1:
+                z0_mx = quantize(z0_woven, "z0")
+        square(TILES - 1)
 
-        for half in range(2):
-            cols = slice(half * HALF, (half + 1) * HALF)
-            result = held([P, N // P, HALF], F32, "result%d" % half)
+        head_block(1, 4 + 2 * TILES)
+        z1_mx = []
+        for h in range(2):
+            entries = pos1_sb[:, h * HALF // 16 : (h + 1) * HALF // 16]
+            for t in range(PACK):
+                nc.scalar.activation(gate_half[h][:, t, :], head[1, t][:].indirect(entries), SIGMOID, scale=-1.0)
+            woven = make_z(weighted[1][:, :, h * HALF : (h + 1) * HALF], gate_half[h][:], "z1%d" % h)
+            z1_mx.append(quantize(woven, "z1%d" % h))
+
+        for h in range(2):
+            cols = slice(h * HALF, (h + 1) * HALF)
+            result = staged([P, N // P, HALF], F32, "result%d" % h, slots[h] * SLOT)
             for n in range(N // P):
                 rows = slice(n * P, (n + 1) * P)
-                acc = next_bank(HALF)
-                guide_passes = [
-                    (w4_mx[a][0][:, rows], w4_mx[a][1][:, rows], guide_mx[a, half][0][:], guide_mx[a, half][1][:])
+                acc = psum.tile([P, HALF], F32, name="bank%d" % (PACK * h + n))
+                passes = [
+                    (late_mx[2 + a][0][:, rows], late_mx[2 + a][1][:, rows], late_mx[a][0][:, cols], late_mx[a][1][:, cols])
                     for a in range(2)
                 ]
-                z_passes = [
-                    (w3_sb[:, b, rows], w3_plane[4 * b : P, rows], z_mx[b, half][0][:], z_mx[b, half][1][:])
-                    for b in range(2)
-                ]
-                passes = [z_passes[0]] + guide_passes + [z_passes[1]]
+                passes.append((w3_sb[:, 0, rows], w3_plane[:, rows], z0_mx[0][:, cols], z0_mx[1][:, cols]))
+                passes.append((w3_sb[:, 1, rows], w3_plane[4:P, rows], z1_mx[h][0][:], z1_mx[h][1][:]))
                 for j, (lhs, lhs_plane, rhs, rhs_plane) in enumerate(passes):
                     nc.tensor.matmul_mx(
                         out=acc[:],
@@ -349,11 +311,11 @@ def tile_list_annotation_disagreement_kernel(
                         start=(j == 0),
                         stop=(j == len(passes) - 1),
                     )
-                engine = "vector" if half == 1 and n % 2 == 1 else "scalar"
-                cast(engine, result[:, n, :], acc[:])
-                if half == 1:
+                if h == 1 and n % 2 == 0:
+                    nc.vector.tensor_copy(result[:, n, :], acc[:])
+                else:
+                    nc.scalar.copy(result[:, n, :], acc[:])
+                if h == 1:
                     nc.sync.dma_start(out=out[rows, cols], in_=result[:, n, :])
-            if half == 0:
-                nc.sync.dma_start(
-                    out=out[:, cols].rearrange("(n p) m -> p n m", p=P), in_=result[:]
-                )
+            if h == 0:
+                nc.sync.dma_start(out=out[:, cols].rearrange("(n p) m -> p n m", p=P), in_=result[:])

@@ -45,9 +45,9 @@ def tile_list_annotation_disagreement_kernel(
         def staged(shape, dtype, name, offset):
             return stage.tile(shape, dtype, name=name, align_bytes=64, offset=offset)
 
-        def zeroed(shape, name):
+        def zeroed(engine, shape, name):
             plane = held(shape, U8, name)
-            nc.vector.memset(plane[:].bitcast(I32), 0)
+            engine.memset(plane[:].bitcast(I32), 0)
             return plane
 
         def load_list(src, name):
@@ -56,41 +56,41 @@ def tile_list_annotation_disagreement_kernel(
             return tile
 
         def load_rows(src, k_pass, cols, name, slot):
-            raw = staged([P, PACK, BANK], F32, name, slot * SLOT)
+            raw = staged([P, PACK, BANK], F32, name, slot)
             rows = src[k_pass * K_PASS : (k_pass + 1) * K_PASS, cols]
             nc.sync.dma_start(out=raw[:], in_=rows.rearrange("(p j) c -> p j c", j=PACK))
             return raw
 
         def load_tab(a, slot):
-            words = staged([P, T], U32, "tab%d" % a, slot * SLOT)
+            words = staged([P, T], U32, "tab%d" % a, slot)
             nc.sync.dma_start(
                 out=words[:].bitcast(I32), in_=tab_words[a].rearrange("p t i -> p (t i)").bitcast(I32)
             )
             return words
 
         offs_sb = load_list(offs, "offs_sb")
-        tab_rows = staged([P, T], U8, "tab_rows", SLOT - T // 2)
+        tab_rows = staged([P, T], U8, "tab_rows", SLOT)
         nc.sync.dma_start(
-            out=tab_rows[0:32, :].bitcast(I32), in_=tab_scales.rearrange("a q t -> q a t").bitcast(I32)
+            out=tab_rows[96:P, :].bitcast(I32), in_=tab_scales.rearrange("a q t -> q a t").bitcast(I32)
         )
-        w1_plane = zeroed([P, 2 * H], "w1_plane")
-        nc.vector.memset(tab_rows[32:64, :].bitcast(I32), 0)
-        nc.vector.memset(tab_rows[64:128, :].bitcast(I32), 0)
-        picked_plane = zeroed([P, 2 * S], "picked_plane")
-        w3_plane = zeroed([P, N], "w3_plane")
-        pos1_sb = load_list(pos1, "pos1_sb")
-        pos3_sb = load_list(pos3, "pos3_sb")
-        pos2_sb = load_list(pos2, "pos2_sb")
+        w1_plane = zeroed(nc.gpsimd, [P, 2 * H], "w1_plane")
+        nc.vector.memset(tab_rows[0:96, :].bitcast(I32), 0)
+        picked_plane = zeroed(nc.vector, [P, 2 * S], "picked_plane")
+        w3_plane = zeroed(nc.vector, [P, N], "w3_plane")
+        for q in range(4):
+            nc.sync.dma_start(
+                out=w1_plane[32 * q : 32 * q + 4, :].rearrange("r (a c) -> r a c", a=2).bitcast(I32),
+                in_=w1_scales[:, 4 * q : 4 * q + 4, :].rearrange("a r c -> r a c").bitcast(I32),
+            )
+        tab_sb = [load_tab(0, 3 * SLOT)]
         w1_sb = held([P, 2, 2 * H], U8, "slot_e")
         nc.sync.dma_start(
             out=w1_sb[:].bitcast(I32), in_=w1_words.rearrange("a p c -> p a c").bitcast(I32)
         )
-        tab_sb = [load_tab(0, 3)]
-        for q in range(4):
-            nc.scalar.dma_start(
-                out=w1_plane[32 * q : 32 * q + 4, :].rearrange("r (a c) -> r a c", a=2).bitcast(I32),
-                in_=w1_scales[:, 4 * q : 4 * q + 4, :].rearrange("a r c -> r a c").bitcast(I32),
-            )
+        pos1_sb = load_list(pos1, "pos1_sb")
+        tab_sb.append(load_tab(1, 0))
+        pos3_sb = load_list(pos3, "pos3_sb")
+        pos2_sb = load_list(pos2, "pos2_sb")
         gain_sb = held([P, 2, PACK], F32, "gain_sb")
         nc.gpsimd.dma_start(out=gain_sb[:], in_=gain.rearrange("(b p t) -> p b t", b=2, t=PACK))
         for q in range(4):
@@ -104,10 +104,9 @@ def tile_list_annotation_disagreement_kernel(
         for q in range(4):
             nc.sync.dma_start(
                 out=picked_plane[32 * q : 32 * q + 4, :].bitcast(I32),
-                in_=picked_rows[8 * q : 8 * q + 8, :].bitcast(I32),
+                in_=picked_rows[96 + 8 * q : 96 + 8 * q + 8, :].bitcast(I32),
             )
 
-        tab_sb.append(load_tab(1, 0))
         picked = [held([P, S], U32, "picked%d" % a) for a in range(2)]
 
         def pick_words(a, h):
@@ -119,10 +118,10 @@ def tile_list_annotation_disagreement_kernel(
         w1_sorted = {}
         w1_sorted_plane = {}
 
-        def sort_w1(b, words_slot, plane_slot):
+        def sort_w1(b, words, plane):
             cols = slice(b * BANK, (b + 1) * BANK)
-            w1_sorted[b] = held([P, 2, 2 * BANK], U8, words_slot)
-            w1_sorted_plane[b] = held([P, 2, BANK], U8, plane_slot)
+            w1_sorted[b] = words
+            w1_sorted_plane[b] = plane
             nc.vector.tensor_copy(
                 w1_sorted[b][:].bitcast(U16).rearrange("p a (t g m) -> p a g t m", t=PACK, m=8),
                 w1_sb[:].bitcast(U16)[:, :, cols].rearrange("p a (g m t) -> p a g t m", t=PACK, m=8),
@@ -185,7 +184,6 @@ def tile_list_annotation_disagreement_kernel(
             return codes[:, P * t : P * (t + 1)].bitcast(FP8X4), plane[:, P * t : P * (t + 1)]
 
         head = {}
-        gate = [held([P, PACK, PAIRS], F32, "gate0")]
         gate_half = [held([P, PACK, HALF], F32, "gate1%d" % h) for h in range(2)]
 
         def head_block(b, first_bank):
@@ -207,7 +205,7 @@ def tile_list_annotation_disagreement_kernel(
 
         def pick_second(i):
             second[i] = ring.tile([P, PAIRS], F32, name="second")
-            if i < TILES - 1:
+            if 0 < i < TILES - 1:
                 nc.scalar.activation(second[i][:], ann[i][:].indirect(pos3_sb[:]), COPY)
             else:
                 nc.vector.tensor_copy(second[i][:], ann[i][:].indirect(pos3_sb[:]))
@@ -233,21 +231,25 @@ def tile_list_annotation_disagreement_kernel(
             )
             return woven
 
-        sort_w1(0, "w1_sorted0", "w1_sorted_plane0")
         pick_words(0, 0)
         pick_words(0, 1)
+        sort_w1(0, held([P, 2, 2 * BANK], U8, "w1_sorted0"), staged([P, 2, BANK], U8, "w1_sorted_plane0", 3 * SLOT))
         pick_words(1, 0)
         pick_words(1, 1)
         head_block(0, 0)
 
-        slots = [1, 2, 3, 0]
+        slots = [SLOT, 2 * SLOT, 3 * SLOT + 2 * BANK, 0]
         pieces = [(a, b) for b in range(2) for a in range(2)]
         w2_raw = [load_rows(w2, a, slice(b * BANK, (b + 1) * BANK), "w2_raw%d%d" % (a, b), slot) for (a, b), slot in zip(pieces, slots)]
         for n, (a, b) in enumerate(pieces):
-            woven = held([P, BANK, PACK], BF16, "woven%d" % n)
+            if n < 3:
+                woven = held([P, BANK, PACK], BF16, "woven%d" % n)
+            else:
+                woven = staged([P, BANK, PACK], BF16, "woven3", 5 * SLOT)
             weave_sorted(w2_raw[n], woven)
             w2_mx[a, b] = quantize(woven, "w2_%d%d" % (a, b))
-        sort_w1(1, "woven0", "woven1")
+        sort_w1(1, held([P, 2, 2 * BANK], U8, "woven2"), staged([P, 2, BANK], U8, "w1_sorted_plane1", 5 * SLOT + 2 * BANK))
+        gate = [staged([P, PACK, PAIRS], F32, "gate0", 4 * SLOT + 2 * BANK)]
 
         late = [(guide, 0), (guide, 1), (w4, 0), (w4, 1)]
         late_raw = [load_rows(src, a, slice(0, BANK), "late_raw%d" % slot, slot) for (src, a), slot in zip(late, slots)]
@@ -267,7 +269,7 @@ def tile_list_annotation_disagreement_kernel(
                 t = i - 2
                 nc.scalar.activation(gate[0][:, t, :], head[0, t][:].indirect(pos1_sb[:]), SIGMOID, scale=-1.0)
             if i < len(late):
-                late_woven[i] = held([P, BANK, PACK], BF16, "woven%d" % (2 + i % 2))
+                late_woven[i] = held([P, BANK, PACK], BF16, "woven%d" % (i % 2))
                 weave(late_raw[i], late_woven[i])
             subtract(i)
             if i < len(late):
@@ -291,7 +293,7 @@ def tile_list_annotation_disagreement_kernel(
 
         for h in range(2):
             cols = slice(h * HALF, (h + 1) * HALF)
-            result = staged([P, N // P, HALF], F32, "result%d" % h, slots[h] * SLOT)
+            result = staged([P, N // P, HALF], F32, "result%d" % h, slots[h])
             for n in range(N // P):
                 rows = slice(n * P, (n + 1) * P)
                 acc = psum.tile([P, HALF], F32, name="bank%d" % (PACK * h + n))

@@ -68,6 +68,10 @@ def tile_list_annotation_disagreement_kernel(
             )
             return words
 
+        warm = held([P, 2], F32, "warm")
+        nc.gpsimd.memset(warm[:, 0:1], 0.0)
+        nc.scalar.activation(warm[:, 1:2], warm[:, 0:1], SIGMOID)
+
         offs_sb = load_list(offs, "offs_sb")
         tab_rows = staged([P, T], U8, "tab_rows", SLOT)
         nc.sync.dma_start(

@@ -23,7 +23,7 @@ PACK = 4
 K_PASS = P * PACK
 BANK = 512
 BANKS = 8
-HALF = PAIRS // 2
+ARC_PIECES = (slice(0, 256), slice(256, 384), slice(384, 512))
 TILES = H // P
 SLOT = 4 * T
 
@@ -130,7 +130,7 @@ def tile_list_annotation_disagreement_kernel(
                 w1_sorted[b][:].bitcast(U16).rearrange("p a (t g m) -> p a g t m", t=PACK, m=8),
                 w1_sb[:].bitcast(U16)[:, :, cols].rearrange("p a (g m t) -> p a g t m", t=PACK, m=8),
             )
-            nc.vector.tensor_copy(
+            nc.gpsimd.tensor_copy(
                 w1_sorted_plane[b][:].rearrange("p a (t g m) -> p a g t m", t=PACK, m=16),
                 w1_plane[:].rearrange("p (a c) -> p a c", a=2)[:, :, cols].rearrange(
                     "p a (g m t) -> p a g t m", t=PACK, m=16
@@ -161,7 +161,7 @@ def tile_list_annotation_disagreement_kernel(
         def product_half(stationary, i, h, bank, window):
             acc = psum.tile([P, BANK], F32, name="bank%d" % (bank % BANKS))
             cols = slice(h * BANK, (h + 1) * BANK)
-            order = (0, 1) if i < 2 else (1, 0)
+            order = (0, 1) if bank < 2 else (1, 0)
             for a in order:
                 codes, plane = stationary(a, i)
                 nc.tensor.matmul_mx(
@@ -188,14 +188,13 @@ def tile_list_annotation_disagreement_kernel(
             return codes[:, P * t : P * (t + 1)].bitcast(FP8X4), plane[:, P * t : P * (t + 1)]
 
         head = {}
-        gate_half = [held([P, PACK, HALF], F32, "gate1%d" % h) for h in range(2)]
 
         def head_block(b, first_bank):
             for t in range(PACK):
                 head[b, t] = ring.tile([P, S], F32, name="head")
             for h in range(2):
                 for t in range(PACK):
-                    product_half(w1_columns, PACK * b + t, h, first_bank + t, head[b, t])
+                    product_half(w1_columns, PACK * b + t, h, first_bank + PACK * h + t, head[b, t])
 
         ann = {}
         second = {}
@@ -205,7 +204,7 @@ def tile_list_annotation_disagreement_kernel(
         def ann_tile(i):
             ann[i] = held([P, S], F32, "ann%d" % i)
             for h in range(2):
-                product_half(w2_columns, i, h, 4 + 2 * i + h, ann[i])
+                product_half(w2_columns, i, h, BANKS + 2 * i + h, ann[i])
 
         def pick_second(i):
             second[i] = ring.tile([P, PAIRS], F32, name="second")
@@ -237,7 +236,7 @@ def tile_list_annotation_disagreement_kernel(
 
         pick_words(0, 0)
         pick_words(0, 1)
-        sort_w1(0, held([P, 2, 2 * BANK], U8, "w1_sorted0"), staged([P, 2, BANK], U8, "w1_sorted_plane0", 3 * SLOT))
+        sort_w1(0, held([P, 2, 2 * BANK], U8, "w1_sorted0"), held([P, 2, BANK], U8, "w1_sorted_plane0"))
         pick_words(1, 0)
         pick_words(1, 1)
         head_block(0, 0)
@@ -252,7 +251,7 @@ def tile_list_annotation_disagreement_kernel(
                 woven = staged([P, BANK, PACK], BF16, "woven3", 5 * SLOT)
             weave_sorted(w2_raw[n], woven)
             w2_mx[a, b] = quantize(woven, "w2_%d%d" % (a, b))
-        sort_w1(1, held([P, 2, 2 * BANK], U8, "woven2"), staged([P, 2, BANK], U8, "w1_sorted_plane1", 5 * SLOT + 2 * BANK))
+        sort_w1(1, held([P, 2, 2 * BANK], U8, "woven2"), held([P, 2, BANK], U8, "w1_sorted_plane1"))
         gate = [staged([P, PACK, PAIRS], F32, "gate0", 4 * SLOT + 2 * BANK)]
 
         late = [(guide, 0), (guide, 1), (w4, 0), (w4, 1)]
@@ -286,42 +285,49 @@ def tile_list_annotation_disagreement_kernel(
                 z0_mx = quantize(z0_woven, "z0")
         square(TILES - 1)
 
-        head_block(1, 4 + 2 * TILES)
+        head_block(1, BANKS + 2 * TILES)
         z1_mx = []
-        for h in range(2):
-            entries = pos1_sb[:, h * HALF // 16 : (h + 1) * HALF // 16]
+        for u, arcs in enumerate(ARC_PIECES):
+            width = arcs.stop - arcs.start
+            entries = pos1_sb[:, arcs.start // 16 : arcs.stop // 16]
+            gates = held([P, PACK, width], F32, "gate1%d" % u)
             for t in range(PACK):
-                nc.scalar.activation(gate_half[h][:, t, :], head[1, t][:].indirect(entries), SIGMOID, scale=-1.0)
-            woven = make_z(weighted[1][:, :, h * HALF : (h + 1) * HALF], gate_half[h][:], "z1%d" % h)
-            z1_mx.append(quantize(woven, "z1%d" % h))
+                nc.scalar.activation(gates[:, t, :], head[1, t][:].indirect(entries), SIGMOID, scale=-1.0)
+            z1_mx.append(quantize(make_z(weighted[1][:, :, arcs], gates[:], "z1%d" % u), "z1%d" % u))
 
-        for h in range(2):
-            cols = slice(h * HALF, (h + 1) * HALF)
-            result = staged([P, N // P, HALF], F32, "result%d" % h, slots[h])
-            for n in range(N // P):
-                rows = slice(n * P, (n + 1) * P)
-                acc = psum.tile([P, HALF], F32, name="bank%d" % (PACK * h + n))
-                passes = [
-                    (late_mx[2 + a][0][:, rows], late_mx[2 + a][1][:, rows], late_mx[a][0][:, cols], late_mx[a][1][:, cols])
-                    for a in range(2)
-                ]
-                passes.append((w3_sb[:, 0, rows], w3_plane[:, rows], z0_mx[0][:, cols], z0_mx[1][:, cols]))
-                passes.append((w3_sb[:, 1, rows], w3_plane[4:P, rows], z1_mx[h][0][:], z1_mx[h][1][:]))
-                for j, (lhs, lhs_plane, rhs, rhs_plane) in enumerate(passes):
-                    nc.tensor.matmul_mx(
-                        out=acc[:],
-                        lhsT=lhs.bitcast(FP8X4),
-                        lhsT_scale=lhs_plane,
-                        rhs=rhs.bitcast(FP8X4),
-                        rhs_scale=rhs_plane,
-                        start=(j == 0),
-                        stop=(j == len(passes) - 1),
-                    )
-                if h == 1 and n % 2 == 0:
-                    nc.vector.tensor_copy(result[:, n, :], acc[:])
+        bank = 0
+        for u, arcs in enumerate(ARC_PIECES):
+            width = arcs.stop - arcs.start
+            last = u == len(ARC_PIECES) - 1
+            per_bank = 2 if last else BANK // width
+            result = staged([P, N // P, width], F32, "result%d" % u, slots[u])
+            stored = out[:, arcs].rearrange("(n p) m -> p n m", p=P)
+            operands = [
+                (late_mx[2 + a][0], late_mx[2 + a][1], late_mx[a][0][:, arcs], late_mx[a][1][:, arcs]) for a in range(2)
+            ]
+            operands.append((w3_sb[:, 0, :], w3_plane, z0_mx[0][:, arcs], z0_mx[1][:, arcs]))
+            operands.append((w3_sb[:, 1, :], w3_plane[4:P, :], z1_mx[u][0][:], z1_mx[u][1][:]))
+            for first in range(0, N // P, per_bank):
+                acc = psum.tile([P, per_bank, width], F32, name="bank%d" % bank)
+                bank = bank + 1
+                for j, (lhs, lhs_plane, rhs, rhs_plane) in enumerate(operands):
+                    for n in range(per_bank):
+                        rows = slice((first + n) * P, (first + n + 1) * P)
+                        nc.tensor.matmul_mx(
+                            out=acc[:, n, :],
+                            lhsT=lhs[:, rows].bitcast(FP8X4),
+                            lhsT_scale=lhs_plane[:, rows],
+                            rhs=rhs.bitcast(FP8X4),
+                            rhs_scale=rhs_plane,
+                            start=(j == 0 and n == 0),
+                            stop=(j == len(operands) - 1 and n == per_bank - 1),
+                        )
+                part = slice(first, first + per_bank)
+                if u > 0 and first == 0:
+                    nc.vector.tensor_copy(result[:, part, :], acc[:])
                 else:
-                    nc.scalar.copy(result[:, n, :], acc[:])
-                if h == 1:
-                    nc.sync.dma_start(out=out[rows, cols], in_=result[:, n, :])
-            if h == 0:
-                nc.sync.dma_start(out=out[:, cols].rearrange("(n p) m -> p n m", p=P), in_=result[:])
+                    nc.scalar.copy(result[:, part, :], acc[:])
+                if last:
+                    nc.sync.dma_start(out=stored[:, part, :], in_=result[:, part, :])
+            if not last:
+                nc.sync.dma_start(out=stored, in_=result[:])

@@ -81,12 +81,12 @@ def tile_list_annotation_disagreement_kernel(
         nc.vector.memset(tab_rows[0:96, :].bitcast(I32), 0)
         picked_plane = zeroed(nc.vector, [P, 2 * S], "picked_plane")
         w3_plane = zeroed(nc.vector, [P, N], "w3_plane")
+        tab_sb = [load_tab(0, 3 * SLOT)]
         for q in range(4):
             nc.sync.dma_start(
                 out=w1_plane[32 * q : 32 * q + 4, :].rearrange("r (a c) -> r a c", a=2).bitcast(I32),
                 in_=w1_scales[:, 4 * q : 4 * q + 4, :].rearrange("a r c -> r a c").bitcast(I32),
             )
-        tab_sb = [load_tab(0, 3 * SLOT)]
         w1_sb = held([P, 2, 2 * H], U8, "slot_e")
         nc.sync.dma_start(
             out=w1_sb[:].bitcast(I32), in_=w1_words.rearrange("a p c -> p a c").bitcast(I32)
@@ -208,10 +208,7 @@ def tile_list_annotation_disagreement_kernel(
 
         def pick_second(i):
             second[i] = ring.tile([P, PAIRS], F32, name="second")
-            if 0 < i < TILES - 1:
-                nc.scalar.activation(second[i][:], ann[i][:].indirect(pos3_sb[:]), COPY)
-            else:
-                nc.vector.tensor_copy(second[i][:], ann[i][:].indirect(pos3_sb[:]))
+            nc.scalar.activation(second[i][:], ann[i][:].indirect(pos3_sb[:]), COPY)
 
         def subtract(i):
             diff[i] = ring.tile([P, PAIRS], F32, name="diff", bufs=2)

@@ -138,24 +138,29 @@ def tile_list_annotation_disagreement_kernel(
             )
 
         def weave(raw, woven):
-            nc.vector.tensor_copy(
-                woven[:].rearrange("p (g i) j -> p g j i", i=4),
-                raw[:].rearrange("p j (g i) -> p g j i", i=4),
-            )
+            for cols in (slice(0, BANK // 2), slice(BANK // 2, BANK)):
+                nc.vector.tensor_copy(
+                    woven[:, cols, :].rearrange("p (g i) j -> p g j i", i=4),
+                    raw[:, :, cols].rearrange("p j (g i) -> p g j i", i=4),
+                )
 
         def weave_sorted(raw, woven):
-            nc.vector.tensor_copy(
-                woven[:].rearrange("p (t m) j -> p m j t", t=PACK),
-                raw[:].rearrange("p j (m t) -> p m j t", t=PACK),
-            )
+            for pair in (slice(0, 2), slice(2, 4)):
+                nc.vector.tensor_copy(
+                    woven[:].rearrange("p (t m) j -> p m j t", t=PACK)[:, :, :, pair],
+                    raw[:].rearrange("p j (m t) -> p m j t", t=PACK)[:, :, :, pair],
+                )
 
         def quantize(woven, name):
             width = woven.shape[1]
             codes = held([P, width], U32, name + "_codes")
             plane = held([P, width], U8, name + "_plane")
-            nc.vector.quantize_mx(
-                out=codes[:].bitcast(FP8X4), scales=plane[:], in_=woven[:].rearrange("p c j -> p (c j)")
-            )
+            for cols in (slice(0, width // 2), slice(width // 2, width)):
+                nc.vector.quantize_mx(
+                    out=codes[:, cols].bitcast(FP8X4),
+                    scales=plane[:, cols],
+                    in_=woven[:, cols, :].rearrange("p c j -> p (c j)"),
+                )
             return codes, plane
 
         def product_half(stationary, i, h, bank, window):
@@ -223,12 +228,13 @@ def tile_list_annotation_disagreement_kernel(
         def make_z(values, gates, name):
             width = values.shape[2]
             woven = held([P, width, PACK], BF16, name + "_woven")
-            nc.vector.tensor_tensor(
-                woven[:].rearrange("p (g i) t -> p g t i", i=4),
-                values.rearrange("p t (g i) -> p g t i", i=4),
-                gates.rearrange("p t (g i) -> p g t i", i=4),
-                MULT,
-            )
+            for cols in (slice(0, width // 2), slice(width // 2, width)):
+                nc.vector.tensor_tensor(
+                    woven[:, cols, :].rearrange("p (g i) t -> p g t i", i=4),
+                    values[:, :, cols].rearrange("p t (g i) -> p g t i", i=4),
+                    gates[:, :, cols].rearrange("p t (g i) -> p g t i", i=4),
+                    MULT,
+                )
             return woven
 
         pick_words(0, 0)

@@ -217,13 +217,16 @@ def tile_list_annotation_disagreement_kernel(
 
         def subtract(i):
             diff[i] = ring.tile([P, PAIRS], F32, name="diff", bufs=2)
-            nc.vector.tensor_tensor(diff[i][:], ann[i][:].indirect(pos2_sb[:]), second[i][:], SUBTRACT)
+            for arcs in (slice(0, PAIRS // 2), slice(PAIRS // 2, PAIRS)):
+                entries = pos2_sb[:, arcs.start // 16 : arcs.stop // 16]
+                nc.vector.tensor_tensor(diff[i][:, arcs], ann[i][:].indirect(entries), second[i][:, arcs], SUBTRACT)
 
         def square(i):
             b, t = divmod(i, PACK)
-            nc.vector.scalar_tensor_tensor(
-                weighted[b][:, t, :], diff[i][:], gain_sb[:, b, t : t + 1], diff[i][:], MULT, MULT
-            )
+            for arcs in (slice(0, PAIRS // 2), slice(PAIRS // 2, PAIRS)):
+                nc.vector.scalar_tensor_tensor(
+                    weighted[b][:, t, arcs], diff[i][:, arcs], gain_sb[:, b, t : t + 1], diff[i][:, arcs], MULT, MULT
+                )
 
         def make_z(values, gates, name):
             width = values.shape[2]

@@ -130,7 +130,7 @@ def tile_list_annotation_disagreement_kernel(
                 w1_sorted[b][:].bitcast(U16).rearrange("p a (t g m) -> p a g t m", t=PACK, m=8),
                 w1_sb[:].bitcast(U16)[:, :, cols].rearrange("p a (g m t) -> p a g t m", t=PACK, m=8),
             )
-            nc.gpsimd.tensor_copy(
+            nc.vector.tensor_copy(
                 w1_sorted_plane[b][:].rearrange("p a (t g m) -> p a g t m", t=PACK, m=16),
                 w1_plane[:].rearrange("p (a c) -> p a c", a=2)[:, :, cols].rearrange(
                     "p a (g m t) -> p a g t m", t=PACK, m=16
@@ -213,7 +213,10 @@ def tile_list_annotation_disagreement_kernel(
 
         def pick_second(i):
             second[i] = ring.tile([P, PAIRS], F32, name="second")
-            nc.scalar.activation(second[i][:], ann[i][:].indirect(pos3_sb[:]), COPY)
+            if i > 0:
+                nc.scalar.activation(second[i][:], ann[i][:].indirect(pos3_sb[:]), COPY)
+            else:
+                nc.vector.tensor_copy(second[i][:], ann[i][:].indirect(pos3_sb[:]))
 
         def subtract(i):
             diff[i] = ring.tile([P, PAIRS], F32, name="diff", bufs=2)
@@ -242,7 +245,7 @@ def tile_list_annotation_disagreement_kernel(
 
         pick_words(0, 0)
         pick_words(0, 1)
-        sort_w1(0, held([P, 2, 2 * BANK], U8, "w1_sorted0"), held([P, 2, BANK], U8, "w1_sorted_plane0"))
+        sort_w1(0, held([P, 2, 2 * BANK], U8, "w1_sorted0"), staged([P, 2, BANK], U8, "w1_sorted_plane0", 3 * SLOT))
         pick_words(1, 0)
         pick_words(1, 1)
         head_block(0, 0)
@@ -257,7 +260,7 @@ def tile_list_annotation_disagreement_kernel(
                 woven = staged([P, BANK, PACK], BF16, "woven3", 5 * SLOT)
             weave_sorted(w2_raw[n], woven)
             w2_mx[a, b] = quantize(woven, "w2_%d%d" % (a, b))
-        sort_w1(1, held([P, 2, 2 * BANK], U8, "woven2"), held([P, 2, BANK], U8, "w1_sorted_plane1"))
+        sort_w1(1, held([P, 2, 2 * BANK], U8, "woven2"), staged([P, 2, BANK], U8, "w1_sorted_plane1", 5 * SLOT + 2 * BANK))
         gate = [staged([P, PACK, PAIRS], F32, "gate0", 4 * SLOT + 2 * BANK)]
 
         late = [(guide, 0), (guide, 1), (w4, 0), (w4, 1)]

@@ -80,28 +80,22 @@ def tile_list_annotation_disagreement_kernel(
         w1_plane = zeroed(nc.gpsimd, [P, 2 * H], "w1_plane")
         nc.vector.memset(tab_rows[0:96, :].bitcast(I32), 0)
         picked_plane = zeroed(nc.vector, [P, 2 * S], "picked_plane")
-        w3_plane = zeroed(nc.vector, [P, N], "w3_plane")
-        tab_sb = [load_tab(0, 3 * SLOT)]
+        w1_sb = held([P, 2, 2 * H], U8, "w1_sb")
+        nc.sync.dma_start(
+            out=w1_sb[:].bitcast(I32), in_=w1_words.rearrange("a p c -> p a c").bitcast(I32)
+        )
         for q in range(4):
             nc.sync.dma_start(
                 out=w1_plane[32 * q : 32 * q + 4, :].rearrange("r (a c) -> r a c", a=2).bitcast(I32),
                 in_=w1_scales[:, 4 * q : 4 * q + 4, :].rearrange("a r c -> r a c").bitcast(I32),
             )
-        w1_sb = held([P, 2, 2 * H], U8, "slot_e")
-        nc.sync.dma_start(
-            out=w1_sb[:].bitcast(I32), in_=w1_words.rearrange("a p c -> p a c").bitcast(I32)
-        )
+        tab_sb = [load_tab(0, 3 * SLOT)]
         pos1_sb = load_list(pos1, "pos1_sb")
         tab_sb.append(load_tab(1, 0))
         pos3_sb = load_list(pos3, "pos3_sb")
         pos2_sb = load_list(pos2, "pos2_sb")
         gain_sb = held([P, 2, PACK], F32, "gain_sb")
         nc.gpsimd.dma_start(out=gain_sb[:], in_=gain.rearrange("(b p t) -> p b t", b=2, t=PACK))
-        for q in range(4):
-            nc.gpsimd.dma_start(
-                out=w3_plane[32 * q : 32 * q + 8, :].bitcast(I32),
-                in_=w3_scales[:, 4 * q : 4 * q + 4, :].bitcast(I32),
-            )
 
         picked_rows = staged([P, S], U8, "picked_rows", 2 * SLOT)
         nc.vector.tensor_copy(picked_rows[:], tab_rows[:].indirect(offs_sb[:]))
@@ -122,15 +116,15 @@ def tile_list_annotation_disagreement_kernel(
         w1_sorted = {}
         w1_sorted_plane = {}
 
-        def sort_w1(b, words, plane):
+        def sort_w1(b):
             cols = slice(b * BANK, (b + 1) * BANK)
-            w1_sorted[b] = words
-            w1_sorted_plane[b] = plane
-            nc.vector.tensor_copy(
-                w1_sorted[b][:].bitcast(U16).rearrange("p a (t g m) -> p a g t m", t=PACK, m=8),
-                w1_sb[:].bitcast(U16)[:, :, cols].rearrange("p a (g m t) -> p a g t m", t=PACK, m=8),
+            w1_sorted[b] = held([P, 2, 2 * BANK], U8, "w1_sorted%d" % b)
+            w1_sorted_plane[b] = held([P, 2, BANK], U8, "w1_sorted_plane%d" % b)
+            nc.gpsimd.tensor_copy(
+                w1_sorted[b][:].rearrange("p a (t m e) -> p a t m e", t=PACK, e=2),
+                w1_sb[:, :, 2 * b * BANK : 2 * (b + 1) * BANK].rearrange("p a (m t e) -> p a t m e", t=PACK, e=2),
             )
-            nc.vector.tensor_copy(
+            nc.gpsimd.tensor_copy(
                 w1_sorted_plane[b][:].rearrange("p a (t g m) -> p a g t m", t=PACK, m=16),
                 w1_plane[:].rearrange("p (a c) -> p a c", a=2)[:, :, cols].rearrange(
                     "p a (g m t) -> p a g t m", t=PACK, m=16
@@ -245,12 +239,13 @@ def tile_list_annotation_disagreement_kernel(
 
         pick_words(0, 0)
         pick_words(0, 1)
-        sort_w1(0, held([P, 2, 2 * BANK], U8, "w1_sorted0"), staged([P, 2, BANK], U8, "w1_sorted_plane0", 3 * SLOT))
+        sort_w1(0)
+        sort_w1(1)
         pick_words(1, 0)
         pick_words(1, 1)
         head_block(0, 0)
 
-        slots = [SLOT, 2 * SLOT, 3 * SLOT + 2 * BANK, 0]
+        slots = [SLOT, 2 * SLOT, 3 * SLOT, 0]
         pieces = [(a, b) for b in range(2) for a in range(2)]
         w2_raw = [load_rows(w2, a, slice(b * BANK, (b + 1) * BANK), "w2_raw%d%d" % (a, b), slot) for (a, b), slot in zip(pieces, slots)]
         for n, (a, b) in enumerate(pieces):
@@ -260,12 +255,18 @@ def tile_list_annotation_disagreement_kernel(
                 woven = staged([P, BANK, PACK], BF16, "woven3", 5 * SLOT)
             weave_sorted(w2_raw[n], woven)
             w2_mx[a, b] = quantize(woven, "w2_%d%d" % (a, b))
-        sort_w1(1, held([P, 2, 2 * BANK], U8, "woven2"), staged([P, 2, BANK], U8, "w1_sorted_plane1", 5 * SLOT + 2 * BANK))
         gate = [staged([P, PACK, PAIRS], F32, "gate0", 4 * SLOT + 2 * BANK)]
 
         late = [(guide, 0), (guide, 1), (w4, 0), (w4, 1)]
         late_raw = [load_rows(src, a, slice(0, BANK), "late_raw%d" % slot, slot) for (src, a), slot in zip(late, slots)]
-        w3_sb = held([P, 2, N], U32, "slot_e")
+        w3_plane = staged([P, N], U8, "w3_plane", 5 * SLOT + 2 * BANK)
+        nc.vector.memset(w3_plane[:].bitcast(I32), 0)
+        for q in range(4):
+            nc.sync.dma_start(
+                out=w3_plane[32 * q : 32 * q + 8, :].bitcast(I32),
+                in_=w3_scales[:, 4 * q : 4 * q + 4, :].bitcast(I32),
+            )
+        w3_sb = held([P, 2, N], U32, "woven2")
         nc.sync.dma_start(
             out=w3_sb[:].bitcast(I32), in_=w3_words.rearrange("a p c i -> p a (c i)").bitcast(I32)
         )
@@ -274,9 +275,12 @@ def tile_list_annotation_disagreement_kernel(
 
         ann_tile(0)
         for i in range(TILES):
+            if i == 0:
+                pick_second(i)
             if i + 1 < TILES:
                 ann_tile(i + 1)
-            pick_second(i)
+            if i > 0:
+                pick_second(i)
             if 2 <= i < 2 + PACK:
                 t = i - 2
                 nc.scalar.activation(gate[0][:, t, :], head[0, t][:].indirect(pos1_sb[:]), SIGMOID, scale=-1.0)
@@ -337,6 +341,7 @@ def tile_list_annotation_disagreement_kernel(
                 else:
                     nc.scalar.copy(result[:, part, :], acc[:])
                 if last:
-                    nc.sync.dma_start(out=stored[:, part, :], in_=result[:, part, :])
+                    queue = nc.sync if first == 0 else nc.scalar
+                    queue.dma_start(out=stored[:, part, :], in_=result[:, part, :])
             if not last:
                 nc.sync.dma_start(out=stored, in_=result[:])

@@ -80,10 +80,14 @@ def tile_list_annotation_disagreement_kernel(
         w1_plane = zeroed(nc.gpsimd, [P, 2 * H], "w1_plane")
         nc.vector.memset(tab_rows[0:96, :].bitcast(I32), 0)
         picked_plane = zeroed(nc.vector, [P, 2 * S], "picked_plane")
-        w1_sb = held([P, 2, 2 * H], U8, "w1_sb")
-        nc.sync.dma_start(
-            out=w1_sb[:].bitcast(I32), in_=w1_words.rearrange("a p c -> p a c").bitcast(I32)
-        )
+
+        def load_w1(b):
+            words = held([P, 2, 2 * BANK], U8, "w1_sb%d" % b)
+            columns = w1_words[:, :, 2 * b * BANK : 2 * (b + 1) * BANK]
+            nc.sync.dma_start(out=words[:].bitcast(I32), in_=columns.rearrange("a p c -> p a c").bitcast(I32))
+            return words
+
+        w1_sb = [load_w1(0)]
         for q in range(4):
             nc.sync.dma_start(
                 out=w1_plane[32 * q : 32 * q + 4, :].rearrange("r (a c) -> r a c", a=2).bitcast(I32),
@@ -91,8 +95,9 @@ def tile_list_annotation_disagreement_kernel(
             )
         tab_sb = [load_tab(0, 3 * SLOT)]
         pos1_sb = load_list(pos1, "pos1_sb")
-        tab_sb.append(load_tab(1, 0))
         pos3_sb = load_list(pos3, "pos3_sb")
+        tab_sb.append(load_tab(1, 0))
+        w1_sb.append(load_w1(1))
         pos2_sb = load_list(pos2, "pos2_sb")
         gain_sb = held([P, 2, PACK], F32, "gain_sb")
         nc.gpsimd.dma_start(out=gain_sb[:], in_=gain.rearrange("(b p t) -> p b t", b=2, t=PACK))
@@ -122,7 +127,7 @@ def tile_list_annotation_disagreement_kernel(
             w1_sorted_plane[b] = held([P, 2, BANK], U8, "w1_sorted_plane%d" % b)
             nc.gpsimd.tensor_copy(
                 w1_sorted[b][:].rearrange("p a (t m e) -> p a t m e", t=PACK, e=2),
-                w1_sb[:, :, 2 * b * BANK : 2 * (b + 1) * BANK].rearrange("p a (m t e) -> p a t m e", t=PACK, e=2),
+                w1_sb[b][:].rearrange("p a (m t e) -> p a t m e", t=PACK, e=2),
             )
             nc.gpsimd.tensor_copy(
                 w1_sorted_plane[b][:].rearrange("p a (t g m) -> p a g t m", t=PACK, m=16),

@@ -40,10 +40,10 @@ def tile_list_annotation_disagreement_kernel(
         psum = ctx.enter_context(tc.psum_pool(name="psum", bufs=1))
 
         def held(shape, dtype, name):
-            return keep.tile(shape, dtype, name=name, align_bytes=64)
+            return keep.tile(shape, dtype, name=name, align_bytes=256)
 
         def staged(shape, dtype, name, offset):
-            return stage.tile(shape, dtype, name=name, align_bytes=64, offset=offset)
+            return stage.tile(shape, dtype, name=name, align_bytes=256, offset=offset)
 
         def zeroed(engine, shape, name):
             plane = held(shape, U8, name)
@@ -73,7 +73,7 @@ def tile_list_annotation_disagreement_kernel(
         nc.scalar.activation(warm[:, 1:2], warm[:, 0:1], SIGMOID)
 
         offs_sb = load_list(offs, "offs_sb")
-        tab_rows = staged([P, T], U8, "tab_rows", SLOT)
+        tab_rows = staged([P, T], U8, "tab_rows", 2 * SLOT - T // 2)
         nc.sync.dma_start(
             out=tab_rows[96:P, :].bitcast(I32), in_=tab_scales.rearrange("a q t -> q a t").bitcast(I32)
         )
@@ -88,12 +88,12 @@ def tile_list_annotation_disagreement_kernel(
             return words
 
         w1_sb = [load_w1(0)]
+        tab_sb = [load_tab(0, 3 * SLOT)]
         for q in range(4):
             nc.sync.dma_start(
                 out=w1_plane[32 * q : 32 * q + 4, :].rearrange("r (a c) -> r a c", a=2).bitcast(I32),
                 in_=w1_scales[:, 4 * q : 4 * q + 4, :].rearrange("a r c -> r a c").bitcast(I32),
             )
-        tab_sb = [load_tab(0, 3 * SLOT)]
         pos1_sb = load_list(pos1, "pos1_sb")
         pos3_sb = load_list(pos3, "pos3_sb")
         tab_sb.append(load_tab(1, 0))
@@ -102,7 +102,7 @@ def tile_list_annotation_disagreement_kernel(
         gain_sb = held([P, 2, PACK], F32, "gain_sb")
         nc.gpsimd.dma_start(out=gain_sb[:], in_=gain.rearrange("(b p t) -> p b t", b=2, t=PACK))
 
-        picked_rows = staged([P, S], U8, "picked_rows", 2 * SLOT)
+        picked_rows = held([P, S], U8, "picked_rows")
         nc.vector.tensor_copy(picked_rows[:], tab_rows[:].indirect(offs_sb[:]))
         for q in range(4):
             nc.sync.dma_start(

@@ -25,7 +25,7 @@ BANK = 512
 BANKS = 8
 ARC_PIECES = (slice(0, 256), slice(256, 384), slice(384, 512))
 TILES = H // P
-SLOT = 4 * T
+KIB = 1024
 
 
 def tile_list_annotation_disagreement_kernel(
@@ -73,7 +73,7 @@ def tile_list_annotation_disagreement_kernel(
         nc.scalar.activation(warm[:, 1:2], warm[:, 0:1], SIGMOID)
 
         offs_sb = load_list(offs, "offs_sb")
-        tab_rows = staged([P, T], U8, "tab_rows", 2 * SLOT - T // 2)
+        tab_rows = staged([P, T], U8, "tab_rows", 16 * KIB)
         nc.sync.dma_start(
             out=tab_rows[96:P, :].bitcast(I32), in_=tab_scales.rearrange("a q t -> q a t").bitcast(I32)
         )
@@ -81,14 +81,13 @@ def tile_list_annotation_disagreement_kernel(
         nc.vector.memset(tab_rows[0:96, :].bitcast(I32), 0)
         picked_plane = zeroed(nc.vector, [P, 2 * S], "picked_plane")
 
-        def load_w1(b):
-            words = held([P, 2, 2 * BANK], U8, "w1_sb%d" % b)
+        def load_w1(b, words):
             columns = w1_words[:, :, 2 * b * BANK : 2 * (b + 1) * BANK]
             nc.sync.dma_start(out=words[:].bitcast(I32), in_=columns.rearrange("a p c -> p a c").bitcast(I32))
             return words
 
-        w1_sb = [load_w1(0)]
-        tab_sb = [load_tab(0, 3 * SLOT)]
+        w1_sb = [load_w1(0, held([P, 2, 2 * BANK], U8, "w1_sb0"))]
+        tab_sb = [load_tab(0, 25 * KIB)]
         for q in range(4):
             nc.sync.dma_start(
                 out=w1_plane[32 * q : 32 * q + 4, :].rearrange("r (a c) -> r a c", a=2).bitcast(I32),
@@ -97,10 +96,7 @@ def tile_list_annotation_disagreement_kernel(
         pos1_sb = load_list(pos1, "pos1_sb")
         pos3_sb = load_list(pos3, "pos3_sb")
         tab_sb.append(load_tab(1, 0))
-        w1_sb.append(load_w1(1))
         pos2_sb = load_list(pos2, "pos2_sb")
-        gain_sb = held([P, 2, PACK], F32, "gain_sb")
-        nc.gpsimd.dma_start(out=gain_sb[:], in_=gain.rearrange("(b p t) -> p b t", b=2, t=PACK))
 
         picked_rows = held([P, S], U8, "picked_rows")
         nc.vector.tensor_copy(picked_rows[:], tab_rows[:].indirect(offs_sb[:]))
@@ -121,14 +117,22 @@ def tile_list_annotation_disagreement_kernel(
         w1_sorted = {}
         w1_sorted_plane = {}
 
-        def sort_w1(b):
-            cols = slice(b * BANK, (b + 1) * BANK)
+        def sort_words(b):
             w1_sorted[b] = held([P, 2, 2 * BANK], U8, "w1_sorted%d" % b)
+            if b == 0:
+                nc.gpsimd.tensor_copy(
+                    w1_sorted[b][:].rearrange("p a (t m e) -> p a t m e", t=PACK, e=2),
+                    w1_sb[b][:].rearrange("p a (m t e) -> p a t m e", t=PACK, e=2),
+                )
+            else:
+                nc.vector.tensor_copy(
+                    w1_sorted[b][:].bitcast(U16).rearrange("p a (t g m) -> p a g t m", t=PACK, m=8),
+                    w1_sb[b][:].bitcast(U16).rearrange("p a (g m t) -> p a g t m", t=PACK, m=8),
+                )
+
+        def sort_plane(b):
+            cols = slice(b * BANK, (b + 1) * BANK)
             w1_sorted_plane[b] = held([P, 2, BANK], U8, "w1_sorted_plane%d" % b)
-            nc.gpsimd.tensor_copy(
-                w1_sorted[b][:].rearrange("p a (t m e) -> p a t m e", t=PACK, e=2),
-                w1_sb[b][:].rearrange("p a (m t e) -> p a t m e", t=PACK, e=2),
-            )
             nc.gpsimd.tensor_copy(
                 w1_sorted_plane[b][:].rearrange("p a (t g m) -> p a g t m", t=PACK, m=16),
                 w1_plane[:].rearrange("p (a c) -> p a c", a=2)[:, :, cols].rearrange(
@@ -244,27 +248,32 @@ def tile_list_annotation_disagreement_kernel(
 
         pick_words(0, 0)
         pick_words(0, 1)
-        sort_w1(0)
-        sort_w1(1)
+        sort_words(0)
+        sort_plane(0)
+        sort_plane(1)
         pick_words(1, 0)
         pick_words(1, 1)
         head_block(0, 0)
 
-        slots = [SLOT, 2 * SLOT, 3 * SLOT, 0]
+        slots = [9 * KIB, 17 * KIB, 25 * KIB, KIB]
         pieces = [(a, b) for b in range(2) for a in range(2)]
         w2_raw = [load_rows(w2, a, slice(b * BANK, (b + 1) * BANK), "w2_raw%d%d" % (a, b), slot) for (a, b), slot in zip(pieces, slots)]
+        w1_sb.append(load_w1(1, held([P, 2, 2 * BANK], U8, "picked_rows")))
+        gain_sb = staged([P, 2, PACK], F32, "gain_sb", 0)
+        nc.sync.dma_start(out=gain_sb[:], in_=gain.rearrange("(b p t) -> p b t", b=2, t=PACK))
         for n, (a, b) in enumerate(pieces):
             if n < 3:
                 woven = held([P, BANK, PACK], BF16, "woven%d" % n)
             else:
-                woven = staged([P, BANK, PACK], BF16, "woven3", 5 * SLOT)
+                woven = staged([P, BANK, PACK], BF16, "woven3", 40 * KIB)
             weave_sorted(w2_raw[n], woven)
             w2_mx[a, b] = quantize(woven, "w2_%d%d" % (a, b))
-        gate = [staged([P, PACK, PAIRS], F32, "gate0", 4 * SLOT + 2 * BANK)]
+        sort_words(1)
+        gate = [staged([P, PACK, PAIRS], F32, "gate0", 33 * KIB)]
 
         late = [(guide, 0), (guide, 1), (w4, 0), (w4, 1)]
         late_raw = [load_rows(src, a, slice(0, BANK), "late_raw%d" % slot, slot) for (src, a), slot in zip(late, slots)]
-        w3_plane = staged([P, N], U8, "w3_plane", 5 * SLOT + 2 * BANK)
+        w3_plane = staged([P, N], U8, "w3_plane", 41 * KIB)
         nc.vector.memset(w3_plane[:].bitcast(I32), 0)
         for q in range(4):
             nc.sync.dma_start(

@@ -21,11 +21,35 @@ COPY = mybir.ActivationFunctionType.Copy
 P = 128
 PACK = 4
 K_PASS = P * PACK
+PASSES = K // K_PASS
 BANK = 512
 BANKS = 8
-ARC_PIECES = (slice(0, 256), slice(256, 384), slice(384, 512))
 TILES = H // P
+QUADRANT = 32
+STRIPE = 16
+ALIGN = 256
+SCALE_ROWS_AT = 96
+
+ARC_PIECES = (slice(0, 256), slice(256, 384), slice(384, 512))
+
+FIRST_GATE_STEP = 2
+
 KIB = 1024
+TAB_AT = (25 * KIB, 0)
+TAB_SCALES_AT = 16 * KIB
+GAIN_AT = 0
+ROWS_AT = (9 * KIB, 17 * KIB, 25 * KIB, KIB)
+LAST_W2_WOVEN_AT = 40 * KIB
+FIRST_GATES_AT = 33 * KIB
+W3_PLANE_AT = 41 * KIB
+
+
+def halves(width):
+    return slice(0, width // 2), slice(width // 2, width)
+
+
+def entries(tile, places):
+    return tile[:, places.start // STRIPE : places.stop // STRIPE]
 
 
 def tile_list_annotation_disagreement_kernel(
@@ -40,13 +64,13 @@ def tile_list_annotation_disagreement_kernel(
         psum = ctx.enter_context(tc.psum_pool(name="psum", bufs=1))
 
         def held(shape, dtype, name):
-            return keep.tile(shape, dtype, name=name, align_bytes=256)
+            return keep.tile(shape, dtype, name=name, align_bytes=ALIGN)
 
         def staged(shape, dtype, name, offset):
-            return stage.tile(shape, dtype, name=name, align_bytes=256, offset=offset)
+            return stage.tile(shape, dtype, name=name, align_bytes=ALIGN, offset=offset)
 
-        def zeroed(engine, shape, name):
-            plane = held(shape, U8, name)
+        def zeroed_plane(engine, width, name):
+            plane = held([P, width], U8, name)
             engine.memset(plane[:].bitcast(I32), 0)
             return plane
 
@@ -55,17 +79,22 @@ def tile_list_annotation_disagreement_kernel(
             nc.sync.dma_start(tile[:], src)
             return tile
 
-        def load_rows(src, k_pass, cols, name, slot):
-            raw = staged([P, PACK, BANK], F32, name, slot)
-            rows = src[k_pass * K_PASS : (k_pass + 1) * K_PASS, cols]
+        def load_rows(src, a, cols, name, offset):
+            raw = staged([P, PACK, BANK], F32, name, offset)
+            rows = src[a * K_PASS : (a + 1) * K_PASS, cols]
             nc.sync.dma_start(out=raw[:], in_=rows.rearrange("(p j) c -> p j c", j=PACK))
             return raw
 
-        def load_tab(a, slot):
-            words = staged([P, T], U32, "tab%d" % a, slot)
+        def load_tab(a):
+            words = staged([P, T], U32, "tab%d" % a, TAB_AT[a])
             nc.sync.dma_start(
                 out=words[:].bitcast(I32), in_=tab_words[a].rearrange("p t i -> p (t i)").bitcast(I32)
             )
+            return words
+
+        def load_w1(b, words):
+            columns = w1_words[:, :, 2 * b * K_PASS : 2 * (b + 1) * K_PASS]
+            nc.sync.dma_start(out=words[:].bitcast(I32), in_=columns.rearrange("a p c -> p a c").bitcast(I32))
             return words
 
         warm = held([P, 2], F32, "warm")
@@ -73,82 +102,77 @@ def tile_list_annotation_disagreement_kernel(
         nc.scalar.activation(warm[:, 1:2], warm[:, 0:1], SIGMOID)
 
         offs_sb = load_list(offs, "offs_sb")
-        tab_rows = staged([P, T], U8, "tab_rows", 16 * KIB)
+        tab_scale_rows = staged([P, T], U8, "tab_rows", TAB_SCALES_AT)
         nc.sync.dma_start(
-            out=tab_rows[96:P, :].bitcast(I32), in_=tab_scales.rearrange("a q t -> q a t").bitcast(I32)
+            out=tab_scale_rows[SCALE_ROWS_AT:P, :].bitcast(I32),
+            in_=tab_scales.rearrange("a q t -> q a t").bitcast(I32),
         )
-        w1_plane = zeroed(nc.gpsimd, [P, 2 * H], "w1_plane")
-        nc.vector.memset(tab_rows[0:96, :].bitcast(I32), 0)
-        picked_plane = zeroed(nc.vector, [P, 2 * S], "picked_plane")
-
-        def load_w1(b, words):
-            columns = w1_words[:, :, 2 * b * BANK : 2 * (b + 1) * BANK]
-            nc.sync.dma_start(out=words[:].bitcast(I32), in_=columns.rearrange("a p c -> p a c").bitcast(I32))
-            return words
-
-        w1_sb = [load_w1(0, held([P, 2, 2 * BANK], U8, "w1_sb0"))]
-        tab_sb = [load_tab(0, 25 * KIB)]
+        w1_plane = zeroed_plane(nc.gpsimd, PASSES * H, "w1_plane")
+        nc.vector.memset(tab_scale_rows[0:SCALE_ROWS_AT, :].bitcast(I32), 0)
+        picked_plane = zeroed_plane(nc.vector, PASSES * S, "picked_plane")
+        pos1_sb = load_list(pos1, "pos1_sb")
+        w1_sb = [load_w1(0, held([P, PASSES, 2 * K_PASS], U8, "w1_sb0"))]
+        tab_sb = [load_tab(0)]
         for q in range(4):
             nc.sync.dma_start(
-                out=w1_plane[32 * q : 32 * q + 4, :].rearrange("r (a c) -> r a c", a=2).bitcast(I32),
+                out=w1_plane[QUADRANT * q : QUADRANT * q + 4, :].rearrange("r (a c) -> r a c", a=PASSES).bitcast(I32),
                 in_=w1_scales[:, 4 * q : 4 * q + 4, :].rearrange("a r c -> r a c").bitcast(I32),
             )
-        pos1_sb = load_list(pos1, "pos1_sb")
         pos3_sb = load_list(pos3, "pos3_sb")
-        tab_sb.append(load_tab(1, 0))
+        tab_sb.append(load_tab(1))
         pos2_sb = load_list(pos2, "pos2_sb")
 
-        picked_rows = held([P, S], U8, "picked_rows")
-        nc.vector.tensor_copy(picked_rows[:], tab_rows[:].indirect(offs_sb[:]))
+        picked_scale_rows = held([P, S], U8, "picked_rows")
+        nc.vector.tensor_copy(picked_scale_rows[:], tab_scale_rows[:].indirect(offs_sb[:]))
         for q in range(4):
+            first_row = SCALE_ROWS_AT + 8 * q
             nc.sync.dma_start(
-                out=picked_plane[32 * q : 32 * q + 4, :].bitcast(I32),
-                in_=picked_rows[96 + 8 * q : 96 + 8 * q + 8, :].bitcast(I32),
+                out=picked_plane[QUADRANT * q : QUADRANT * q + 4, :].bitcast(I32),
+                in_=picked_scale_rows[first_row : first_row + 8, :].bitcast(I32),
             )
 
-        picked = [held([P, S], U32, "picked%d" % a) for a in range(2)]
+        picked = [held([P, S], U32, "picked%d" % a) for a in range(PASSES)]
 
-        def pick_words(a, h):
-            nc.vector.tensor_copy(
-                picked[a][:, h * BANK : (h + 1) * BANK],
-                tab_sb[a][:].indirect(offs_sb[:, h * BANK // 16 : (h + 1) * BANK // 16]),
-            )
+        def pick_words(a):
+            for places in halves(S):
+                nc.vector.tensor_copy(picked[a][:, places], tab_sb[a][:].indirect(entries(offs_sb, places)))
 
         w1_sorted = {}
         w1_sorted_plane = {}
 
-        def sort_words(b):
-            w1_sorted[b] = held([P, 2, 2 * BANK], U8, "w1_sorted%d" % b)
-            if b == 0:
-                nc.gpsimd.tensor_copy(
-                    w1_sorted[b][:].rearrange("p a (t m e) -> p a t m e", t=PACK, e=2),
-                    w1_sb[b][:].rearrange("p a (m t e) -> p a t m e", t=PACK, e=2),
-                )
-            else:
-                nc.vector.tensor_copy(
-                    w1_sorted[b][:].bitcast(U16).rearrange("p a (t g m) -> p a g t m", t=PACK, m=8),
-                    w1_sb[b][:].bitcast(U16).rearrange("p a (g m t) -> p a g t m", t=PACK, m=8),
-                )
+        def sort_first_words():
+            w1_sorted[0] = held([P, PASSES, 2 * K_PASS], U8, "w1_sorted0")
+            nc.gpsimd.tensor_copy(
+                w1_sorted[0][:].rearrange("p a (t m e) -> p a t m e", t=PACK, e=2),
+                w1_sb[0][:].rearrange("p a (m t e) -> p a t m e", t=PACK, e=2),
+            )
+
+        def sort_last_words():
+            w1_sorted[1] = held([P, PASSES, 2 * K_PASS], U8, "w1_sorted1")
+            nc.vector.tensor_copy(
+                w1_sorted[1][:].bitcast(U16).rearrange("p a (t g m) -> p a g t m", t=PACK, m=8),
+                w1_sb[1][:].bitcast(U16).rearrange("p a (g m t) -> p a g t m", t=PACK, m=8),
+            )
 
         def sort_plane(b):
-            cols = slice(b * BANK, (b + 1) * BANK)
-            w1_sorted_plane[b] = held([P, 2, BANK], U8, "w1_sorted_plane%d" % b)
+            cols = slice(b * K_PASS, (b + 1) * K_PASS)
+            w1_sorted_plane[b] = held([P, PASSES, K_PASS], U8, "w1_sorted_plane%d" % b)
             nc.gpsimd.tensor_copy(
                 w1_sorted_plane[b][:].rearrange("p a (t g m) -> p a g t m", t=PACK, m=16),
-                w1_plane[:].rearrange("p (a c) -> p a c", a=2)[:, :, cols].rearrange(
+                w1_plane[:].rearrange("p (a c) -> p a c", a=PASSES)[:, :, cols].rearrange(
                     "p a (g m t) -> p a g t m", t=PACK, m=16
                 ),
             )
 
         def weave(raw, woven):
-            for cols in (slice(0, BANK // 2), slice(BANK // 2, BANK)):
+            for cols in halves(BANK):
                 nc.vector.tensor_copy(
                     woven[:, cols, :].rearrange("p (g i) j -> p g j i", i=4),
                     raw[:, :, cols].rearrange("p j (g i) -> p g j i", i=4),
                 )
 
         def weave_sorted(raw, woven):
-            for pair in (slice(0, 2), slice(2, 4)):
+            for pair in halves(PACK):
                 nc.vector.tensor_copy(
                     woven[:].rearrange("p (t m) j -> p m j t", t=PACK)[:, :, :, pair],
                     raw[:].rearrange("p j (m t) -> p m j t", t=PACK)[:, :, :, pair],
@@ -158,7 +182,7 @@ def tile_list_annotation_disagreement_kernel(
             width = woven.shape[1]
             codes = held([P, width], U32, name + "_codes")
             plane = held([P, width], U8, name + "_plane")
-            for cols in (slice(0, width // 2), slice(width // 2, width)):
+            for cols in halves(width):
                 nc.vector.quantize_mx(
                     out=codes[:, cols].bitcast(FP8X4),
                     scales=plane[:, cols],
@@ -166,10 +190,10 @@ def tile_list_annotation_disagreement_kernel(
                 )
             return codes, plane
 
-        def product_half(stationary, i, h, bank, window):
-            acc = psum.tile([P, BANK], F32, name="bank%d" % (bank % BANKS))
+        def product_half(stationary, i, h, turn, window):
+            acc = psum.tile([P, BANK], F32, name="bank%d" % (turn % BANKS))
             cols = slice(h * BANK, (h + 1) * BANK)
-            order = (0, 1) if bank < 2 else (1, 0)
+            order = (0, 1) if turn < 2 else (1, 0)
             for a in order:
                 codes, plane = stationary(a, i)
                 nc.tensor.matmul_mx(
@@ -197,12 +221,12 @@ def tile_list_annotation_disagreement_kernel(
 
         head = {}
 
-        def head_block(b, first_bank):
+        def head_block(b, first_turn):
             for t in range(PACK):
                 head[b, t] = ring.tile([P, S], F32, name="head")
             for h in range(2):
                 for t in range(PACK):
-                    product_half(w1_columns, PACK * b + t, h, first_bank + PACK * h + t, head[b, t])
+                    product_half(w1_columns, PACK * b + t, h, first_turn + PACK * h + t, head[b, t])
 
         ann = {}
         second = {}
@@ -219,25 +243,30 @@ def tile_list_annotation_disagreement_kernel(
             if i > 0:
                 nc.scalar.activation(second[i][:], ann[i][:].indirect(pos3_sb[:]), COPY)
             else:
-                nc.vector.tensor_copy(second[i][:], ann[i][:].indirect(pos3_sb[:]))
+                for arcs in halves(PAIRS):
+                    nc.vector.tensor_copy(second[i][:, arcs], ann[i][:].indirect(entries(pos3_sb, arcs)))
 
         def subtract(i):
             diff[i] = ring.tile([P, PAIRS], F32, name="diff", bufs=2)
-            for arcs in (slice(0, PAIRS // 2), slice(PAIRS // 2, PAIRS)):
-                entries = pos2_sb[:, arcs.start // 16 : arcs.stop // 16]
-                nc.vector.tensor_tensor(diff[i][:, arcs], ann[i][:].indirect(entries), second[i][:, arcs], SUBTRACT)
+            for arcs in halves(PAIRS):
+                nc.vector.tensor_tensor(
+                    diff[i][:, arcs], ann[i][:].indirect(entries(pos2_sb, arcs)), second[i][:, arcs], SUBTRACT
+                )
 
         def square(i):
             b, t = divmod(i, PACK)
-            for arcs in (slice(0, PAIRS // 2), slice(PAIRS // 2, PAIRS)):
+            for arcs in halves(PAIRS):
                 nc.vector.scalar_tensor_tensor(
                     weighted[b][:, t, arcs], diff[i][:, arcs], gain_sb[:, b, t : t + 1], diff[i][:, arcs], MULT, MULT
                 )
 
+        def pick_gates(gates, window, offsets):
+            nc.scalar.activation(gates, window[:].indirect(offsets), SIGMOID, scale=-1.0)
+
         def make_z(values, gates, name):
             width = values.shape[2]
             woven = held([P, width, PACK], BF16, name + "_woven")
-            for cols in (slice(0, width // 2), slice(width // 2, width)):
+            for cols in halves(width):
                 nc.vector.tensor_tensor(
                     woven[:, cols, :].rearrange("p (g i) t -> p g t i", i=4),
                     values[:, :, cols].rearrange("p t (g i) -> p g t i", i=4),
@@ -246,38 +275,41 @@ def tile_list_annotation_disagreement_kernel(
                 )
             return woven
 
-        pick_words(0, 0)
-        pick_words(0, 1)
-        sort_words(0)
+        pick_words(0)
+        sort_first_words()
         sort_plane(0)
         sort_plane(1)
-        pick_words(1, 0)
-        pick_words(1, 1)
+        pick_words(1)
         head_block(0, 0)
 
-        slots = [9 * KIB, 17 * KIB, 25 * KIB, KIB]
-        pieces = [(a, b) for b in range(2) for a in range(2)]
-        w2_raw = [load_rows(w2, a, slice(b * BANK, (b + 1) * BANK), "w2_raw%d%d" % (a, b), slot) for (a, b), slot in zip(pieces, slots)]
-        w1_sb.append(load_w1(1, held([P, 2, 2 * BANK], U8, "picked_rows")))
-        gain_sb = staged([P, 2, PACK], F32, "gain_sb", 0)
+        w2_pieces = [(a, b) for b in range(2) for a in range(PASSES)]
+        w2_raw = [
+            load_rows(w2, a, slice(b * K_PASS, (b + 1) * K_PASS), "w2_raw%d%d" % (a, b), offset)
+            for (a, b), offset in zip(w2_pieces, ROWS_AT)
+        ]
+        w1_sb.append(load_w1(1, held([P, PASSES, 2 * K_PASS], U8, "picked_rows")))
+        gain_sb = staged([P, 2, PACK], F32, "gain_sb", GAIN_AT)
         nc.sync.dma_start(out=gain_sb[:], in_=gain.rearrange("(b p t) -> p b t", b=2, t=PACK))
-        for n, (a, b) in enumerate(pieces):
-            if n < 3:
+        for n, (a, b) in enumerate(w2_pieces):
+            if n < len(w2_pieces) - 1:
                 woven = held([P, BANK, PACK], BF16, "woven%d" % n)
             else:
-                woven = staged([P, BANK, PACK], BF16, "woven3", 40 * KIB)
+                woven = staged([P, BANK, PACK], BF16, "woven%d" % n, LAST_W2_WOVEN_AT)
             weave_sorted(w2_raw[n], woven)
             w2_mx[a, b] = quantize(woven, "w2_%d%d" % (a, b))
-        sort_words(1)
-        gate = [staged([P, PACK, PAIRS], F32, "gate0", 33 * KIB)]
+        sort_last_words()
+        first_gates = staged([P, PACK, PAIRS], F32, "gate0", FIRST_GATES_AT)
 
         late = [(guide, 0), (guide, 1), (w4, 0), (w4, 1)]
-        late_raw = [load_rows(src, a, slice(0, BANK), "late_raw%d" % slot, slot) for (src, a), slot in zip(late, slots)]
-        w3_plane = staged([P, N], U8, "w3_plane", 41 * KIB)
-        nc.vector.memset(w3_plane[:].bitcast(I32), 0)
+        late_raw = [
+            load_rows(src, a, slice(0, BANK), "late_raw%d" % offset, offset)
+            for (src, a), offset in zip(late, ROWS_AT)
+        ]
+        w3_plane = staged([P, N], U8, "w3_plane", W3_PLANE_AT)
+        nc.gpsimd.memset(w3_plane[:].bitcast(I32), 0)
         for q in range(4):
             nc.sync.dma_start(
-                out=w3_plane[32 * q : 32 * q + 8, :].bitcast(I32),
+                out=w3_plane[QUADRANT * q : QUADRANT * q + 8, :].bitcast(I32),
                 in_=w3_scales[:, 4 * q : 4 * q + 4, :].bitcast(I32),
             )
         w3_sb = held([P, 2, N], U32, "woven2")
@@ -288,16 +320,15 @@ def tile_list_annotation_disagreement_kernel(
         late_mx = {}
 
         ann_tile(0)
+        pick_second(0)
         for i in range(TILES):
-            if i == 0:
-                pick_second(i)
             if i + 1 < TILES:
                 ann_tile(i + 1)
             if i > 0:
                 pick_second(i)
-            if 2 <= i < 2 + PACK:
-                t = i - 2
-                nc.scalar.activation(gate[0][:, t, :], head[0, t][:].indirect(pos1_sb[:]), SIGMOID, scale=-1.0)
+            if FIRST_GATE_STEP <= i < FIRST_GATE_STEP + PACK:
+                t = i - FIRST_GATE_STEP
+                pick_gates(first_gates[:, t, :], head[0, t], pos1_sb[:])
             if i < len(late):
                 late_woven[i] = held([P, BANK, PACK], BF16, "woven%d" % (i % 2))
                 weave(late_raw[i], late_woven[i])
@@ -306,31 +337,30 @@ def tile_list_annotation_disagreement_kernel(
                 late_mx[i] = quantize(late_woven[i], "late%d" % i)
             if i >= 1:
                 square(i - 1)
-            if i == TILES - 2:
-                z0_woven = make_z(weighted[0][:], gate[0][:], "z0")
-            if i == TILES - 1:
+            if i == FIRST_GATE_STEP + PACK:
+                z0_woven = make_z(weighted[0][:], first_gates[:], "z0")
+            if i == FIRST_GATE_STEP + PACK + 1:
                 z0_mx = quantize(z0_woven, "z0")
         square(TILES - 1)
+        guide_mx, w4_mx = (late_mx[0], late_mx[1]), (late_mx[2], late_mx[3])
 
         head_block(1, BANKS + 2 * TILES)
         z1_mx = []
         for u, arcs in enumerate(ARC_PIECES):
-            width = arcs.stop - arcs.start
-            entries = pos1_sb[:, arcs.start // 16 : arcs.stop // 16]
-            gates = held([P, PACK, width], F32, "gate1%d" % u)
+            gates = held([P, PACK, arcs.stop - arcs.start], F32, "gate1%d" % u)
             for t in range(PACK):
-                nc.scalar.activation(gates[:, t, :], head[1, t][:].indirect(entries), SIGMOID, scale=-1.0)
+                pick_gates(gates[:, t, :], head[1, t], entries(pos1_sb, arcs))
             z1_mx.append(quantize(make_z(weighted[1][:, :, arcs], gates[:], "z1%d" % u), "z1%d" % u))
 
         bank = 0
         for u, arcs in enumerate(ARC_PIECES):
             width = arcs.stop - arcs.start
             last = u == len(ARC_PIECES) - 1
-            per_bank = 2 if last else BANK // width
-            result = staged([P, N // P, width], F32, "result%d" % u, slots[u])
+            per_bank = N // P // 2 if last else BANK // width
+            result = staged([P, N // P, width], F32, "result%d" % u, ROWS_AT[u])
             stored = out[:, arcs].rearrange("(n p) m -> p n m", p=P)
             operands = [
-                (late_mx[2 + a][0], late_mx[2 + a][1], late_mx[a][0][:, arcs], late_mx[a][1][:, arcs]) for a in range(2)
+                (w4_mx[a][0], w4_mx[a][1], guide_mx[a][0][:, arcs], guide_mx[a][1][:, arcs]) for a in range(PASSES)
             ]
             operands.append((w3_sb[:, 0, :], w3_plane, z0_mx[0][:, arcs], z0_mx[1][:, arcs]))
             operands.append((w3_sb[:, 1, :], w3_plane[4:P, :], z1_mx[u][0][:], z1_mx[u][1][:]))
@@ -350,7 +380,7 @@ def tile_list_annotation_disagreement_kernel(
                             stop=(j == len(operands) - 1 and n == per_bank - 1),
                         )
                 part = slice(first, first + per_bank)
-                if u > 0 and first == 0:
+                if last and first == 0:
                     nc.vector.tensor_copy(result[:, part, :], acc[:])
                 else:
                     nc.scalar.copy(result[:, part, :], acc[:])

@@ -113,10 +113,10 @@ def tile_list_annotation_disagreement_kernel(
         pos1_sb = load_list(pos1, "pos1_sb")
         w1_sb = [load_w1(0, held([P, PASSES, 2 * K_PASS], U8, "w1_sb0"))]
         tab_sb = [load_tab(0)]
-        for q in range(4):
+        for r in range(4):
             nc.sync.dma_start(
-                out=w1_plane[QUADRANT * q : QUADRANT * q + 4, :].rearrange("r (a c) -> r a c", a=PASSES).bitcast(I32),
-                in_=w1_scales[:, 4 * q : 4 * q + 4, :].rearrange("a r c -> r a c").bitcast(I32),
+                out=w1_plane[r:P:QUADRANT, :].rearrange("q (a c) -> q a c", a=PASSES).bitcast(I32),
+                in_=w1_scales[:, r:16:4, :].rearrange("a q c -> q a c").bitcast(I32),
             )
         pos3_sb = load_list(pos3, "pos3_sb")
         tab_sb.append(load_tab(1))
@@ -165,11 +165,9 @@ def tile_list_annotation_disagreement_kernel(
             )
 
         def weave(raw, woven):
-            for cols in halves(BANK):
-                nc.vector.tensor_copy(
-                    woven[:, cols, :].rearrange("p (g i) j -> p g j i", i=4),
-                    raw[:, :, cols].rearrange("p j (g i) -> p g j i", i=4),
-                )
+            nc.vector.tensor_copy(
+                woven[:].rearrange("p (g i) j -> p g j i", i=4), raw[:].rearrange("p j (g i) -> p g j i", i=4)
+            )
 
         def weave_sorted(raw, woven):
             for pair in halves(PACK):
@@ -190,7 +188,15 @@ def tile_list_annotation_disagreement_kernel(
                 )
             return codes, plane
 
-        def product_half(stationary, i, h, turn, window):
+        def quantize_late(n):
+            codes = held([P, BANK], U32, "late%d_codes" % n)
+            plane = held([P, BANK], U8, "late%d_plane" % n)
+            nc.vector.quantize_mx(
+                out=codes[:].bitcast(FP8X4), scales=plane[:], in_=late_woven[n][:].rearrange("p c j -> p (c j)")
+            )
+            return codes, plane
+
+        def product_half(stationary, i, h, turn):
             acc = psum.tile([P, BANK], F32, name="bank%d" % (turn % BANKS))
             cols = slice(h * BANK, (h + 1) * BANK)
             order = (0, 1) if turn < 2 else (1, 0)
@@ -205,7 +211,11 @@ def tile_list_annotation_disagreement_kernel(
                     start=(a == order[0]),
                     stop=(a == order[1]),
                 )
-            nc.scalar.copy(window[:, cols], acc[:])
+            return acc
+
+        def empty_pair(first, last):
+            for acc, window in (last, first):
+                nc.scalar.copy(window, acc[:])
 
         def w1_columns(a, i):
             b, t = divmod(i, PACK)
@@ -225,8 +235,15 @@ def tile_list_annotation_disagreement_kernel(
             for t in range(PACK):
                 head[b, t] = ring.tile([P, S], F32, name="head")
             for h in range(2):
+                cols = slice(h * BANK, (h + 1) * BANK)
                 for t in range(PACK):
-                    product_half(w1_columns, PACK * b + t, h, first_turn + PACK * h + t, head[b, t])
+                    acc = product_half(w1_columns, PACK * b + t, h, first_turn + PACK * h + t)
+                    if b == 0:
+                        nc.scalar.copy(head[b, t][:, cols], acc[:])
+                    elif t % 2 == 0:
+                        waiting = acc, head[b, t][:, cols]
+                    else:
+                        empty_pair(waiting, (acc, head[b, t][:, cols]))
 
         ann = {}
         second = {}
@@ -235,11 +252,11 @@ def tile_list_annotation_disagreement_kernel(
 
         def ann_tile(i):
             ann[i] = held([P, S], F32, "ann%d" % i)
-            for h in range(2):
-                product_half(w2_columns, i, h, BANKS + 2 * i + h, ann[i])
+            sums = [product_half(w2_columns, i, h, BANKS + 2 * i + h) for h in range(2)]
+            empty_pair((sums[0], ann[i][:, 0:BANK]), (sums[1], ann[i][:, BANK:S]))
 
         def pick_second(i):
-            second[i] = ring.tile([P, PAIRS], F32, name="second")
+            second[i] = held([P, PAIRS], F32, "second%d" % i)
             if i > 0:
                 nc.scalar.activation(second[i][:], ann[i][:].indirect(pos3_sb[:]), COPY)
             else:
@@ -248,14 +265,14 @@ def tile_list_annotation_disagreement_kernel(
 
         def subtract(i):
             diff[i] = ring.tile([P, PAIRS], F32, name="diff", bufs=2)
-            for arcs in halves(PAIRS):
+            for arcs in halves(PAIRS) if i >= PACK or i == 0 else [slice(0, PAIRS)]:
                 nc.vector.tensor_tensor(
                     diff[i][:, arcs], ann[i][:].indirect(entries(pos2_sb, arcs)), second[i][:, arcs], SUBTRACT
                 )
 
         def square(i):
             b, t = divmod(i, PACK)
-            for arcs in halves(PAIRS):
+            for arcs in halves(PAIRS) if i >= PACK else [slice(0, PAIRS)]:
                 nc.vector.scalar_tensor_tensor(
                     weighted[b][:, t, arcs], diff[i][:, arcs], gain_sb[:, b, t : t + 1], diff[i][:, arcs], MULT, MULT
                 )
@@ -334,7 +351,7 @@ def tile_list_annotation_disagreement_kernel(
                 weave(late_raw[i], late_woven[i])
             subtract(i)
             if i < len(late):
-                late_mx[i] = quantize(late_woven[i], "late%d" % i)
+                late_mx[i] = quantize_late(i)
             if i >= 1:
                 square(i - 1)
             if i == FIRST_GATE_STEP + PACK:

@@ -60,7 +60,6 @@ def tile_list_annotation_disagreement_kernel(
     with ExitStack() as ctx:
         keep = ctx.enter_context(tc.tile_pool(name="keep", bufs=1))
         stage = ctx.enter_context(tc.tile_pool(name="stage", bufs=1))
-        ring = ctx.enter_context(tc.tile_pool(name="ring", bufs=4))
         psum = ctx.enter_context(tc.psum_pool(name="psum", bufs=1))
 
         def held(shape, dtype, name):
@@ -233,7 +232,7 @@ def tile_list_annotation_disagreement_kernel(
 
         def head_block(b, first_turn):
             for t in range(PACK):
-                head[b, t] = ring.tile([P, S], F32, name="head")
+                head[b, t] = held([P, S], F32, "head%d%d" % (b, t))
             for h in range(2):
                 cols = slice(h * BANK, (h + 1) * BANK)
                 for t in range(PACK):
@@ -264,7 +263,7 @@ def tile_list_annotation_disagreement_kernel(
                     nc.vector.tensor_copy(second[i][:, arcs], ann[i][:].indirect(entries(pos3_sb, arcs)))
 
         def subtract(i):
-            diff[i] = ring.tile([P, PAIRS], F32, name="diff", bufs=2)
+            diff[i] = held([P, PAIRS], F32, "second%d" % (i - 2) if i >= 2 else "diff%d" % i)
             for arcs in halves(PAIRS) if i >= PACK or i == 0 else [slice(0, PAIRS)]:
                 nc.vector.tensor_tensor(
                     diff[i][:, arcs], ann[i][:].indirect(entries(pos2_sb, arcs)), second[i][:, arcs], SUBTRACT
@@ -374,7 +373,7 @@ def tile_list_annotation_disagreement_kernel(
             width = arcs.stop - arcs.start
             last = u == len(ARC_PIECES) - 1
             per_bank = N // P // 2 if last else BANK // width
-            result = staged([P, N // P, width], F32, "result%d" % u, ROWS_AT[u])
+            result = held([P, N // P, width], F32, "head0%d" % u)
             stored = out[:, arcs].rearrange("(n p) m -> p n m", p=P)
             operands = [
                 (w4_mx[a][0], w4_mx[a][1], guide_mx[a][0][:, arcs], guide_mx[a][1][:, arcs]) for a in range(PASSES)
@@ -401,8 +400,5 @@ def tile_list_annotation_disagreement_kernel(
                     nc.vector.tensor_copy(result[:, part, :], acc[:])
                 else:
                     nc.scalar.copy(result[:, part, :], acc[:])
-                if last:
-                    queue = nc.sync if first == 0 else nc.scalar
-                    queue.dma_start(out=stored[:, part, :], in_=result[:, part, :])
-            if not last:
-                nc.sync.dma_start(out=stored, in_=result[:])
+                queue = nc.scalar if last and first > 0 else nc.sync
+                queue.dma_start(out=stored[:, part, :], in_=result[:, part, :])

@@ -41,11 +41,14 @@ GAIN_AT = 0
 ROWS_AT = (9 * KIB, 17 * KIB, 25 * KIB, KIB)
 LAST_W2_WOVEN_AT = 40 * KIB
 FIRST_GATES_AT = 33 * KIB
-W3_PLANE_AT = 41 * KIB
 
 
 def halves(width):
     return slice(0, width // 2), slice(width // 2, width)
+
+
+def whole(width):
+    return (slice(0, width),)
 
 
 def entries(tile, places):
@@ -109,7 +112,7 @@ def tile_list_annotation_disagreement_kernel(
         w1_plane = zeroed_plane(nc.gpsimd, PASSES * H, "w1_plane")
         nc.vector.memset(tab_scale_rows[0:SCALE_ROWS_AT, :].bitcast(I32), 0)
         picked_plane = zeroed_plane(nc.vector, PASSES * S, "picked_plane")
-        pos1_sb = load_list(pos1, "pos1_sb")
+        pos3_sb = load_list(pos3, "pos3_sb")
         w1_sb = [load_w1(0, held([P, PASSES, 2 * K_PASS], U8, "w1_sb0"))]
         tab_sb = [load_tab(0)]
         for r in range(4):
@@ -117,7 +120,6 @@ def tile_list_annotation_disagreement_kernel(
                 out=w1_plane[r:P:QUADRANT, :].rearrange("q (a c) -> q a c", a=PASSES).bitcast(I32),
                 in_=w1_scales[:, r:16:4, :].rearrange("a q c -> q a c").bitcast(I32),
             )
-        pos3_sb = load_list(pos3, "pos3_sb")
         tab_sb.append(load_tab(1))
         pos2_sb = load_list(pos2, "pos2_sb")
 
@@ -175,24 +177,16 @@ def tile_list_annotation_disagreement_kernel(
                     raw[:].rearrange("p j (m t) -> p m j t", t=PACK)[:, :, :, pair],
                 )
 
-        def quantize(woven, name):
+        def quantize(woven, name, parts):
             width = woven.shape[1]
             codes = held([P, width], U32, name + "_codes")
             plane = held([P, width], U8, name + "_plane")
-            for cols in halves(width):
+            for cols in parts(width):
                 nc.vector.quantize_mx(
                     out=codes[:, cols].bitcast(FP8X4),
                     scales=plane[:, cols],
                     in_=woven[:, cols, :].rearrange("p c j -> p (c j)"),
                 )
-            return codes, plane
-
-        def quantize_late(n):
-            codes = held([P, BANK], U32, "late%d_codes" % n)
-            plane = held([P, BANK], U8, "late%d_plane" % n)
-            nc.vector.quantize_mx(
-                out=codes[:].bitcast(FP8X4), scales=plane[:], in_=late_woven[n][:].rearrange("p c j -> p (c j)")
-            )
             return codes, plane
 
         def product_half(stationary, i, h, turn):
@@ -262,16 +256,16 @@ def tile_list_annotation_disagreement_kernel(
                 for arcs in halves(PAIRS):
                     nc.vector.tensor_copy(second[i][:, arcs], ann[i][:].indirect(entries(pos3_sb, arcs)))
 
-        def subtract(i):
+        def subtract(i, parts):
             diff[i] = held([P, PAIRS], F32, "second%d" % (i - 2) if i >= 2 else "diff%d" % i)
-            for arcs in halves(PAIRS) if i >= PACK or i == 0 else [slice(0, PAIRS)]:
+            for arcs in parts(PAIRS):
                 nc.vector.tensor_tensor(
                     diff[i][:, arcs], ann[i][:].indirect(entries(pos2_sb, arcs)), second[i][:, arcs], SUBTRACT
                 )
 
-        def square(i):
+        def square(i, parts):
             b, t = divmod(i, PACK)
-            for arcs in halves(PAIRS) if i >= PACK else [slice(0, PAIRS)]:
+            for arcs in parts(PAIRS):
                 nc.vector.scalar_tensor_tensor(
                     weighted[b][:, t, arcs], diff[i][:, arcs], gain_sb[:, b, t : t + 1], diff[i][:, arcs], MULT, MULT
                 )
@@ -279,10 +273,10 @@ def tile_list_annotation_disagreement_kernel(
         def pick_gates(gates, window, offsets):
             nc.scalar.activation(gates, window[:].indirect(offsets), SIGMOID, scale=-1.0)
 
-        def make_z(values, gates, name):
+        def make_z(values, gates, name, parts):
             width = values.shape[2]
             woven = held([P, width, PACK], BF16, name + "_woven")
-            for cols in halves(width):
+            for cols in parts(width):
                 nc.vector.tensor_tensor(
                     woven[:, cols, :].rearrange("p (g i) t -> p g t i", i=4),
                     values[:, :, cols].rearrange("p t (g i) -> p g t i", i=4),
@@ -303,6 +297,7 @@ def tile_list_annotation_disagreement_kernel(
             load_rows(w2, a, slice(b * K_PASS, (b + 1) * K_PASS), "w2_raw%d%d" % (a, b), offset)
             for (a, b), offset in zip(w2_pieces, ROWS_AT)
         ]
+        pos1_sb = load_list(pos1, "pos1_sb")
         w1_sb.append(load_w1(1, held([P, PASSES, 2 * K_PASS], U8, "picked_rows")))
         gain_sb = staged([P, 2, PACK], F32, "gain_sb", GAIN_AT)
         nc.sync.dma_start(out=gain_sb[:], in_=gain.rearrange("(b p t) -> p b t", b=2, t=PACK))
@@ -312,7 +307,7 @@ def tile_list_annotation_disagreement_kernel(
             else:
                 woven = staged([P, BANK, PACK], BF16, "woven%d" % n, LAST_W2_WOVEN_AT)
             weave_sorted(w2_raw[n], woven)
-            w2_mx[a, b] = quantize(woven, "w2_%d%d" % (a, b))
+            w2_mx[a, b] = quantize(woven, "w2_%d%d" % (a, b), halves)
         sort_last_words()
         first_gates = staged([P, PACK, PAIRS], F32, "gate0", FIRST_GATES_AT)
 
@@ -321,13 +316,6 @@ def tile_list_annotation_disagreement_kernel(
             load_rows(src, a, slice(0, BANK), "late_raw%d" % offset, offset)
             for (src, a), offset in zip(late, ROWS_AT)
         ]
-        w3_plane = staged([P, N], U8, "w3_plane", W3_PLANE_AT)
-        nc.gpsimd.memset(w3_plane[:].bitcast(I32), 0)
-        for q in range(4):
-            nc.sync.dma_start(
-                out=w3_plane[QUADRANT * q : QUADRANT * q + 8, :].bitcast(I32),
-                in_=w3_scales[:, 4 * q : 4 * q + 4, :].bitcast(I32),
-            )
         w3_sb = held([P, 2, N], U32, "woven2")
         nc.sync.dma_start(
             out=w3_sb[:].bitcast(I32), in_=w3_words.rearrange("a p c i -> p a (c i)").bitcast(I32)
@@ -348,25 +336,31 @@ def tile_list_annotation_disagreement_kernel(
             if i < len(late):
                 late_woven[i] = held([P, BANK, PACK], BF16, "woven%d" % (i % 2))
                 weave(late_raw[i], late_woven[i])
-            subtract(i)
+            subtract(i, whole if i > 0 else halves)
             if i < len(late):
-                late_mx[i] = quantize_late(i)
+                late_mx[i] = quantize(late_woven[i], "late%d" % i, whole)
             if i >= 1:
-                square(i - 1)
+                square(i - 1, whole)
             if i == FIRST_GATE_STEP + PACK:
-                z0_woven = make_z(weighted[0][:], first_gates[:], "z0")
+                z0_woven = make_z(weighted[0][:], first_gates[:], "z0", whole)
             if i == FIRST_GATE_STEP + PACK + 1:
-                z0_mx = quantize(z0_woven, "z0")
-        square(TILES - 1)
+                z0_mx = quantize(z0_woven, "z0", whole)
+        square(TILES - 1, halves)
         guide_mx, w4_mx = (late_mx[0], late_mx[1]), (late_mx[2], late_mx[3])
 
         head_block(1, BANKS + 2 * TILES)
+        for q in range(4):
+            nc.sync.dma_start(
+                out=picked_plane[QUADRANT * q + 4 : QUADRANT * q + 12, 0:N].bitcast(I32),
+                in_=w3_scales[:, 4 * q : 4 * q + 4, :].bitcast(I32),
+            )
         z1_mx = []
         for u, arcs in enumerate(ARC_PIECES):
             gates = held([P, PACK, arcs.stop - arcs.start], F32, "gate1%d" % u)
             for t in range(PACK):
                 pick_gates(gates[:, t, :], head[1, t], entries(pos1_sb, arcs))
-            z1_mx.append(quantize(make_z(weighted[1][:, :, arcs], gates[:], "z1%d" % u), "z1%d" % u))
+            woven = make_z(weighted[1][:, :, arcs], gates[:], "z1%d" % u, halves)
+            z1_mx.append(quantize(woven, "z1%d" % u, halves))
 
         bank = 0
         for u, arcs in enumerate(ARC_PIECES):
@@ -378,8 +372,8 @@ def tile_list_annotation_disagreement_kernel(
             operands = [
                 (w4_mx[a][0], w4_mx[a][1], guide_mx[a][0][:, arcs], guide_mx[a][1][:, arcs]) for a in range(PASSES)
             ]
-            operands.append((w3_sb[:, 0, :], w3_plane, z0_mx[0][:, arcs], z0_mx[1][:, arcs]))
-            operands.append((w3_sb[:, 1, :], w3_plane[4:P, :], z1_mx[u][0][:], z1_mx[u][1][:]))
+            operands.append((w3_sb[:, 0, :], picked_plane[4:P, 0:N], z0_mx[0][:, arcs], z0_mx[1][:, arcs]))
+            operands.append((w3_sb[:, 1, :], picked_plane[8:P, 0:N], z1_mx[u][0][:], z1_mx[u][1][:]))
             for first in range(0, N // P, per_bank):
                 acc = psum.tile([P, per_bank, width], F32, name="bank%d" % bank)
                 bank = bank + 1

@@ -29,18 +29,18 @@ QUADRANT = 32
 STRIPE = 16
 ALIGN = 256
 SCALE_ROWS_AT = 96
-
 ARC_PIECES = (slice(0, 256), slice(256, 384), slice(384, 512))
-
-FIRST_GATE_STEP = 2
+FIRST_GROUPS = ((0, 0), (1, 0), (0, 1), (1, 1), (2, 0), (2, 1), (3, 0), (3, 1))
+VECTOR_GROUPS = (0, 4)
 
 KIB = 1024
-TAB_AT = (25 * KIB, 0)
-TAB_SCALES_AT = 16 * KIB
-GAIN_AT = 0
-ROWS_AT = (9 * KIB, 17 * KIB, 25 * KIB, KIB)
-LAST_W2_WOVEN_AT = 40 * KIB
-FIRST_GATES_AT = 33 * KIB
+LATE_ROWS_AT = 0
+TAB_AT = (57 * KIB, 31 * KIB)
+TAB_SCALES_AT = 48 * KIB
+GAIN_AT = 32 * KIB
+ROWS_AT = (41 * KIB, 49 * KIB, 33 * KIB, 57 * KIB + 512)
+PICKED_ROWS_AT = 65 * KIB
+W1_LAST_AT = 65 * KIB + 512
 
 
 def halves(width):
@@ -71,18 +71,13 @@ def tile_list_annotation_disagreement_kernel(
         def staged(shape, dtype, name, offset):
             return stage.tile(shape, dtype, name=name, align_bytes=ALIGN, offset=offset)
 
-        def zeroed_plane(engine, width, name):
-            plane = held([P, width], U8, name)
-            engine.memset(plane[:].bitcast(I32), 0)
-            return plane
-
         def load_list(src, name):
             tile = held(list(src.shape), U16, name)
             nc.sync.dma_start(tile[:], src)
             return tile
 
-        def load_rows(src, a, cols, name, offset):
-            raw = staged([P, PACK, BANK], F32, name, offset)
+        def load_rows(src, a, cols, name, slot):
+            raw = staged([P, PACK, BANK], F32, name, ROWS_AT[slot])
             rows = src[a * K_PASS : (a + 1) * K_PASS, cols]
             nc.sync.dma_start(out=raw[:], in_=rows.rearrange("(p j) c -> p j c", j=PACK))
             return raw
@@ -109,11 +104,13 @@ def tile_list_annotation_disagreement_kernel(
             out=tab_scale_rows[SCALE_ROWS_AT:P, :].bitcast(I32),
             in_=tab_scales.rearrange("a q t -> q a t").bitcast(I32),
         )
-        w1_plane = zeroed_plane(nc.gpsimd, PASSES * H, "w1_plane")
+        w1_plane = held([P, PASSES * H], U8, "w1_plane")
+        nc.gpsimd.memset(w1_plane[:].bitcast(I32), 0)
         nc.vector.memset(tab_scale_rows[0:SCALE_ROWS_AT, :].bitcast(I32), 0)
-        picked_plane = zeroed_plane(nc.vector, PASSES * S, "picked_plane")
-        pos3_sb = load_list(pos3, "pos3_sb")
-        w1_sb = [load_w1(0, held([P, PASSES, 2 * K_PASS], U8, "w1_sb0"))]
+        picked_plane = held([P, PASSES * S], U8, "picked_plane")
+        nc.vector.memset(picked_plane[:].bitcast(I32), 0)
+        pos1_sb = load_list(pos1, "pos1_sb")
+        w1_first = load_w1(0, held([P, PASSES, 2 * K_PASS], U8, "w1_first"))
         tab_sb = [load_tab(0)]
         for r in range(4):
             nc.sync.dma_start(
@@ -121,11 +118,10 @@ def tile_list_annotation_disagreement_kernel(
                 in_=w1_scales[:, r:16:4, :].rearrange("a q c -> q a c").bitcast(I32),
             )
         tab_sb.append(load_tab(1))
-        pos2_sb = load_list(pos2, "pos2_sb")
 
-        picked_scale_rows = held([P, S], U8, "picked_rows")
+        picked_scale_rows = staged([P, S], U8, "picked_rows", PICKED_ROWS_AT)
         nc.vector.tensor_copy(picked_scale_rows[:], tab_scale_rows[:].indirect(offs_sb[:]))
-        for q in range(4):
+        for q in (0, 2, 1, 3):
             first_row = SCALE_ROWS_AT + 8 * q
             nc.sync.dma_start(
                 out=picked_plane[QUADRANT * q : QUADRANT * q + 4, :].bitcast(I32),
@@ -138,26 +134,11 @@ def tile_list_annotation_disagreement_kernel(
             for places in halves(S):
                 nc.vector.tensor_copy(picked[a][:, places], tab_sb[a][:].indirect(entries(offs_sb, places)))
 
-        w1_sorted = {}
-        w1_sorted_plane = {}
-
-        def sort_first_words():
-            w1_sorted[0] = held([P, PASSES, 2 * K_PASS], U8, "w1_sorted0")
-            nc.gpsimd.tensor_copy(
-                w1_sorted[0][:].rearrange("p a (t m e) -> p a t m e", t=PACK, e=2),
-                w1_sb[0][:].rearrange("p a (m t e) -> p a t m e", t=PACK, e=2),
-            )
-
-        def sort_last_words():
-            w1_sorted[1] = held([P, PASSES, 2 * K_PASS], U8, "w1_sorted1")
-            nc.vector.tensor_copy(
-                w1_sorted[1][:].bitcast(U16).rearrange("p a (t g m) -> p a g t m", t=PACK, m=8),
-                w1_sb[1][:].bitcast(U16).rearrange("p a (g m t) -> p a g t m", t=PACK, m=8),
-            )
+        w1_sorted = [held([P, PASSES, 2 * K_PASS], U8, "w1_sorted%d" % b) for b in range(2)]
+        w1_sorted_plane = [held([P, PASSES, K_PASS], U8, "w1_sorted_plane%d" % b) for b in range(2)]
 
         def sort_plane(b):
             cols = slice(b * K_PASS, (b + 1) * K_PASS)
-            w1_sorted_plane[b] = held([P, PASSES, K_PASS], U8, "w1_sorted_plane%d" % b)
             nc.gpsimd.tensor_copy(
                 w1_sorted_plane[b][:].rearrange("p a (t g m) -> p a g t m", t=PACK, m=16),
                 w1_plane[:].rearrange("p (a c) -> p a c", a=PASSES)[:, :, cols].rearrange(
@@ -167,7 +148,7 @@ def tile_list_annotation_disagreement_kernel(
 
         def weave(raw, woven):
             nc.vector.tensor_copy(
-                woven[:].rearrange("p (g i) j -> p g j i", i=4), raw[:].rearrange("p j (g i) -> p g j i", i=4)
+                woven.rearrange("p (g i) j -> p g j i", i=4), raw.rearrange("p j (g i) -> p g j i", i=4)
             )
 
         def weave_sorted(raw, woven):
@@ -222,46 +203,26 @@ def tile_list_annotation_disagreement_kernel(
             codes, plane = w2_mx[a, b]
             return codes[:, P * t : P * (t + 1)].bitcast(FP8X4), plane[:, P * t : P * (t + 1)]
 
-        head = {}
-
-        def head_block(b, first_turn):
-            for t in range(PACK):
-                head[b, t] = held([P, S], F32, "head%d%d" % (b, t))
-            for h in range(2):
-                cols = slice(h * BANK, (h + 1) * BANK)
-                for t in range(PACK):
-                    acc = product_half(w1_columns, PACK * b + t, h, first_turn + PACK * h + t)
-                    if b == 0:
-                        nc.scalar.copy(head[b, t][:, cols], acc[:])
-                    elif t % 2 == 0:
-                        waiting = acc, head[b, t][:, cols]
-                    else:
-                        empty_pair(waiting, (acc, head[b, t][:, cols]))
-
-        ann = {}
+        head = {i: held([P, S], F32, "head%d" % i) for i in range(TILES) if i != 2}
+        ann = [held([P, S], F32, "ann%d" % i) for i in range(TILES)]
         second = {}
         diff = {}
-        weighted = [held([P, PACK, PAIRS], F32, "weighted%d" % b) for b in range(2)]
-
-        def ann_tile(i):
-            ann[i] = held([P, S], F32, "ann%d" % i)
-            sums = [product_half(w2_columns, i, h, BANKS + 2 * i + h) for h in range(2)]
-            empty_pair((sums[0], ann[i][:, 0:BANK]), (sums[1], ann[i][:, BANK:S]))
 
         def pick_second(i):
-            second[i] = held([P, PAIRS], F32, "second%d" % i)
-            if i > 0:
-                nc.scalar.activation(second[i][:], ann[i][:].indirect(pos3_sb[:]), COPY)
+            if i < 2:
+                second[i] = first_gates[:, 2 + i, :]
             else:
-                for arcs in halves(PAIRS):
-                    nc.vector.tensor_copy(second[i][:, arcs], ann[i][:].indirect(entries(pos3_sb, arcs)))
+                second[i] = held([P, PAIRS], F32, "second%d" % i)[:]
+            nc.scalar.activation(second[i], ann[i][:].indirect(pos3_sb[:]), COPY)
 
-        def subtract(i, parts):
-            diff[i] = held([P, PAIRS], F32, "second%d" % (i - 2) if i >= 2 else "diff%d" % i)
-            for arcs in parts(PAIRS):
-                nc.vector.tensor_tensor(
-                    diff[i][:, arcs], ann[i][:].indirect(entries(pos2_sb, arcs)), second[i][:, arcs], SUBTRACT
-                )
+        def subtract(i):
+            if i < 2:
+                diff[i] = staged([P, PAIRS], F32, "diff%d" % i, ROWS_AT[2] + 2 * KIB * i)[:]
+            elif i < 6:
+                diff[i] = late_rows[:, 2 * (i // 2 - 1), 1 + i % 2, :]
+            else:
+                diff[i] = held([P, PAIRS], F32, "second%d" % (i - 4))[:]
+            nc.vector.tensor_tensor(diff[i], ann[i][:].indirect(pos2_sb[:]), second[i], SUBTRACT)
 
         def square(i, parts):
             b, t = divmod(i, PACK)
@@ -273,82 +234,123 @@ def tile_list_annotation_disagreement_kernel(
         def pick_gates(gates, window, offsets):
             nc.scalar.activation(gates, window[:].indirect(offsets), SIGMOID, scale=-1.0)
 
-        def make_z(values, gates, name, parts):
-            width = values.shape[2]
-            woven = held([P, width, PACK], BF16, name + "_woven")
-            for cols in parts(width):
+        def make_z(values, gates, woven, parts):
+            for cols in parts(values.shape[2]):
                 nc.vector.tensor_tensor(
                     woven[:, cols, :].rearrange("p (g i) t -> p g t i", i=4),
                     values[:, :, cols].rearrange("p t (g i) -> p g t i", i=4),
                     gates[:, :, cols].rearrange("p t (g i) -> p g t i", i=4),
                     MULT,
                 )
-            return woven
 
         pick_words(0)
-        sort_first_words()
+        nc.gpsimd.tensor_copy(
+            w1_sorted[0][:].rearrange("p a (t m e) -> p a t m e", t=PACK, e=2),
+            w1_first[:].rearrange("p a (m t e) -> p a t m e", t=PACK, e=2),
+        )
         sort_plane(0)
         sort_plane(1)
         pick_words(1)
-        head_block(0, 0)
 
-        w2_pieces = [(a, b) for b in range(2) for a in range(PASSES)]
-        w2_raw = [
-            load_rows(w2, a, slice(b * K_PASS, (b + 1) * K_PASS), "w2_raw%d%d" % (a, b), offset)
-            for (a, b), offset in zip(w2_pieces, ROWS_AT)
-        ]
-        pos1_sb = load_list(pos1, "pos1_sb")
-        w1_sb.append(load_w1(1, held([P, PASSES, 2 * K_PASS], U8, "picked_rows")))
+        def w2_cols(b):
+            return slice(b * K_PASS, (b + 1) * K_PASS)
+
+        w2_raw = {(a, 0): load_rows(w2, a, w2_cols(0), "w2_raw%d0" % a, a) for a in range(PASSES)}
+        w1_last = load_w1(1, staged([P, PASSES, 2 * K_PASS], U8, "w1_last", W1_LAST_AT))
+        pos3_sb = load_list(pos3, "pos3_sb")
+        pos2_sb = load_list(pos2, "pos2_sb")
+        w2_raw[0, 1] = load_rows(w2, 0, w2_cols(1), "w2_raw01", 3)
+
+        def w2_piece(a, b, woven):
+            weave_sorted(w2_raw[a, b], woven)
+            w2_mx[a, b] = quantize(woven, "w2_%d%d" % (a, b), halves)
+
+        head[2] = staged([P, S], F32, "head2", ROWS_AT[0])
+        first_gates = held([P, PACK, PAIRS], F32, "gate0")
+        first_sums = [product_half(w1_columns, t, h, turn) for turn, (t, h) in enumerate(FIRST_GROUPS)]
+
+        def empty_first(turn):
+            t, h = FIRST_GROUPS[turn]
+            window = head[t][:, h * BANK : (h + 1) * BANK]
+            if turn in VECTOR_GROUPS:
+                nc.vector.tensor_copy(window, first_sums[turn][:])
+            else:
+                nc.scalar.copy(window, first_sums[turn][:])
+
+        for turn in range(4):
+            empty_first(turn)
+        pick_gates(first_gates[:, 0, :], head[0], pos1_sb[:])
+        w2_piece(0, 0, held([P, BANK, PACK], BF16, "woven0"))
+        for turn in range(4, 6):
+            empty_first(turn)
+        pick_gates(first_gates[:, 1, :], head[1], pos1_sb[:])
+        for turn in range(6, 8):
+            empty_first(turn)
+        w2_piece(1, 0, held([P, BANK, PACK], BF16, "woven1"))
+        w2_raw[1, 1] = load_rows(w2, 1, w2_cols(1), "w2_raw11", 2)
         gain_sb = staged([P, 2, PACK], F32, "gain_sb", GAIN_AT)
         nc.sync.dma_start(out=gain_sb[:], in_=gain.rearrange("(b p t) -> p b t", b=2, t=PACK))
-        for n, (a, b) in enumerate(w2_pieces):
-            if n < len(w2_pieces) - 1:
-                woven = held([P, BANK, PACK], BF16, "woven%d" % n)
-            else:
-                woven = staged([P, BANK, PACK], BF16, "woven%d" % n, LAST_W2_WOVEN_AT)
-            weave_sorted(w2_raw[n], woven)
-            w2_mx[a, b] = quantize(woven, "w2_%d%d" % (a, b), halves)
-        sort_last_words()
-        first_gates = staged([P, PACK, PAIRS], F32, "gate0", FIRST_GATES_AT)
-
-        late = [(guide, 0), (guide, 1), (w4, 0), (w4, 1)]
-        late_raw = [
-            load_rows(src, a, slice(0, BANK), "late_raw%d" % offset, offset)
-            for (src, a), offset in zip(late, ROWS_AT)
-        ]
-        w3_sb = held([P, 2, N], U32, "woven2")
-        nc.sync.dma_start(
-            out=w3_sb[:].bitcast(I32), in_=w3_words.rearrange("a p c i -> p a (c i)").bitcast(I32)
+        nc.vector.tensor_copy(
+            w1_sorted[1][:].bitcast(U16).rearrange("p a (t g m) -> p a g t m", t=PACK, m=8),
+            w1_last[:].bitcast(U16).rearrange("p a (g m t) -> p a g t m", t=PACK, m=8),
         )
-        late_woven = {}
-        late_mx = {}
+
+        def ann_tile(i):
+            sums = [product_half(w2_columns, i, h, BANKS + 2 * i + h) for h in range(2)]
+            if i == 0:
+                nc.scalar.copy(ann[i][:, 0:BANK], sums[0][:])
+                nc.vector.tensor_copy(ann[i][:, BANK:S], sums[1][:])
+            else:
+                empty_pair((sums[0], ann[i][:, 0:BANK]), (sums[1], ann[i][:, BANK:S]))
 
         ann_tile(0)
-        pick_second(0)
+        w2_piece(0, 1, held([P, BANK, PACK], BF16, "woven2"))
+        w2_piece(1, 1, held([P, BANK, PACK], BF16, "woven0"))
+
+        late_rows = staged([P, 2 * PASSES, PACK, BANK], F32, "late_rows", LATE_ROWS_AT)
+        for n, src in enumerate((guide, w4)):
+            nc.sync.dma_start(
+                out=late_rows[:, PASSES * n : PASSES * (n + 1), :, :],
+                in_=src.rearrange("(a p j) c -> p a j c", a=PASSES, j=PACK),
+            )
+        w3_sb = held([P, 2, N], U32, "woven2")
+        nc.sync.dma_start(out=w3_sb[:].bitcast(I32), in_=w3_words.rearrange("a p c i -> p a (c i)").bitcast(I32))
+        weighted = [late_rows[:, :, 0, :], held([P, PACK, PAIRS], F32, "weighted1")[:]]
+        late_mx = {}
+        z0_woven = staged([P, PAIRS, PACK], BF16, "z0_woven", ROWS_AT[2] + 4 * KIB)
+
         for i in range(TILES):
             if i + 1 < TILES:
                 ann_tile(i + 1)
-            if i > 0:
-                pick_second(i)
-            if FIRST_GATE_STEP <= i < FIRST_GATE_STEP + PACK:
-                t = i - FIRST_GATE_STEP
-                pick_gates(first_gates[:, t, :], head[0, t], pos1_sb[:])
-            if i < len(late):
-                late_woven[i] = held([P, BANK, PACK], BF16, "woven%d" % (i % 2))
-                weave(late_raw[i], late_woven[i])
-            subtract(i, whole if i > 0 else halves)
-            if i < len(late):
-                late_mx[i] = quantize(late_woven[i], "late%d" % i, whole)
-            if i >= 1:
-                square(i - 1, whole)
-            if i == FIRST_GATE_STEP + PACK:
-                z0_woven = make_z(weighted[0][:], first_gates[:], "z0", whole)
-            if i == FIRST_GATE_STEP + PACK + 1:
-                z0_mx = quantize(z0_woven, "z0", whole)
+            pick_second(i)
+            if i in (2, 3):
+                pick_gates(first_gates[:, i, :], head[i], pos1_sb[:])
+            if i in (2, 4):
+                n = i // 2 - 1
+                late_woven = staged([P, PASSES * BANK, PACK], BF16, "late_woven%d" % n, ROWS_AT[1 + 2 * n])
+                for a in range(PASSES):
+                    weave(late_rows[:, PASSES * n + a, :, :], late_woven[:, a * BANK : (a + 1) * BANK, :])
+            subtract(i)
+            if i in (2, 4):
+                late_mx[n] = quantize(late_woven, "late%d" % n, whole)
+            if i >= 2:
+                square(i - 2, whole)
+            if i == 6:
+                make_z(weighted[0], first_gates[:], z0_woven, whole)
+        square(TILES - 2, whole)
+        z0_mx = quantize(z0_woven, "z0", whole)
         square(TILES - 1, halves)
-        guide_mx, w4_mx = (late_mx[0], late_mx[1]), (late_mx[2], late_mx[3])
+        guide_mx, w4_mx = [
+            [(codes[:, a * BANK : (a + 1) * BANK], plane[:, a * BANK : (a + 1) * BANK]) for a in range(PASSES)]
+            for codes, plane in (late_mx[0], late_mx[1])
+        ]
 
-        head_block(1, BANKS + 2 * TILES)
+        for h in range(2):
+            cols = slice(h * BANK, (h + 1) * BANK)
+            for t in range(0, PACK, 2):
+                turn = BANKS + 2 * TILES + PACK * h + t
+                sums = [product_half(w1_columns, PACK + t + e, h, turn + e) for e in range(2)]
+                empty_pair((sums[0], head[PACK + t][:, cols]), (sums[1], head[PACK + t + 1][:, cols]))
         for q in range(4):
             nc.sync.dma_start(
                 out=picked_plane[QUADRANT * q + 4 : QUADRANT * q + 12, 0:N].bitcast(I32),
@@ -356,10 +358,15 @@ def tile_list_annotation_disagreement_kernel(
             )
         z1_mx = []
         for u, arcs in enumerate(ARC_PIECES):
-            gates = held([P, PACK, arcs.stop - arcs.start], F32, "gate1%d" % u)
+            width = arcs.stop - arcs.start
+            if u == 0:
+                gates = staged([P, PACK, width], F32, "gate10", ROWS_AT[0] + 4 * KIB)
+            else:
+                gates = held([P, PACK, width], F32, "gate1%d" % u)
             for t in range(PACK):
-                pick_gates(gates[:, t, :], head[1, t], entries(pos1_sb, arcs))
-            woven = make_z(weighted[1][:, :, arcs], gates[:], "z1%d" % u, halves)
+                pick_gates(gates[:, t, :], head[PACK + t], entries(pos1_sb, arcs))
+            woven = held([P, width, PACK], BF16, "z1%d_woven" % u)
+            make_z(weighted[1][:, :, arcs], gates[:], woven, halves)
             z1_mx.append(quantize(woven, "z1%d" % u, halves))
 
         bank = 0
@@ -367,7 +374,7 @@ def tile_list_annotation_disagreement_kernel(
             width = arcs.stop - arcs.start
             last = u == len(ARC_PIECES) - 1
             per_bank = N // P // 2 if last else BANK // width
-            result = held([P, N // P, width], F32, "head0%d" % u)
+            result = held([P, N // P, width], F32, "head%d" % (0, 1, 3)[u])
             stored = out[:, arcs].rearrange("(n p) m -> p n m", p=P)
             operands = [
                 (w4_mx[a][0], w4_mx[a][1], guide_mx[a][0][:, arcs], guide_mx[a][1][:, arcs]) for a in range(PASSES)

@@ -30,8 +30,8 @@ STRIPE = 16
 ALIGN = 256
 SCALE_ROWS_AT = 96
 ARC_PIECES = (slice(0, 256), slice(256, 384), slice(384, 512))
-FIRST_GROUPS = ((0, 0), (1, 0), (0, 1), (1, 1), (2, 0), (2, 1), (3, 0), (3, 1))
-VECTOR_GROUPS = (0, 4)
+FIRST_GROUPS = ((0, 0), (1, 0), (0, 1), (2, 0), (1, 1), (2, 1), (3, 0), (3, 1))
+VECTOR_GROUPS = (0, 3, 7)
 
 KIB = 1024
 LATE_ROWS_AT = 0
@@ -187,8 +187,8 @@ def tile_list_annotation_disagreement_kernel(
                 )
             return acc
 
-        def empty_pair(first, last):
-            for acc, window in (last, first):
+        def empty_banks(filled):
+            for acc, window in filled[-1:] + filled[:-1]:
                 nc.scalar.copy(window, acc[:])
 
         def w1_columns(a, i):
@@ -203,7 +203,7 @@ def tile_list_annotation_disagreement_kernel(
             codes, plane = w2_mx[a, b]
             return codes[:, P * t : P * (t + 1)].bitcast(FP8X4), plane[:, P * t : P * (t + 1)]
 
-        head = {i: held([P, S], F32, "head%d" % i) for i in range(TILES) if i != 2}
+        head = {i: held([P, S], F32, "head%d" % i) for i in range(TILES) if i not in (2, 3)}
         ann = [held([P, S], F32, "ann%d" % i) for i in range(TILES)]
         second = {}
         diff = {}
@@ -266,6 +266,7 @@ def tile_list_annotation_disagreement_kernel(
             w2_mx[a, b] = quantize(woven, "w2_%d%d" % (a, b), halves)
 
         head[2] = staged([P, S], F32, "head2", ROWS_AT[0])
+        head[3] = staged([P, S], F32, "head3", ROWS_AT[1])
         first_gates = held([P, PACK, PAIRS], F32, "gate0")
         first_sums = [product_half(w1_columns, t, h, turn) for turn, (t, h) in enumerate(FIRST_GROUPS)]
 
@@ -277,16 +278,17 @@ def tile_list_annotation_disagreement_kernel(
             else:
                 nc.scalar.copy(window, first_sums[turn][:])
 
-        for turn in range(4):
+        for turn in range(3):
+            empty_first(turn)
+        w2_piece(0, 0, held([P, BANK, PACK], BF16, "woven0"))
+        for turn in range(3, 5):
             empty_first(turn)
         pick_gates(first_gates[:, 0, :], head[0], pos1_sb[:])
-        w2_piece(0, 0, held([P, BANK, PACK], BF16, "woven0"))
-        for turn in range(4, 6):
-            empty_first(turn)
+        empty_first(5)
         pick_gates(first_gates[:, 1, :], head[1], pos1_sb[:])
+        w2_piece(1, 0, held([P, BANK, PACK], BF16, "woven1"))
         for turn in range(6, 8):
             empty_first(turn)
-        w2_piece(1, 0, held([P, BANK, PACK], BF16, "woven1"))
         w2_raw[1, 1] = load_rows(w2, 1, w2_cols(1), "w2_raw11", 2)
         gain_sb = staged([P, 2, PACK], F32, "gain_sb", GAIN_AT)
         nc.sync.dma_start(out=gain_sb[:], in_=gain.rearrange("(b p t) -> p b t", b=2, t=PACK))
@@ -295,15 +297,12 @@ def tile_list_annotation_disagreement_kernel(
             w1_last[:].bitcast(U16).rearrange("p a (g m t) -> p a g t m", t=PACK, m=8),
         )
 
-        def ann_tile(i):
-            sums = [product_half(w2_columns, i, h, BANKS + 2 * i + h) for h in range(2)]
-            if i == 0:
-                nc.scalar.copy(ann[i][:, 0:BANK], sums[0][:])
-                nc.vector.tensor_copy(ann[i][:, BANK:S], sums[1][:])
-            else:
-                empty_pair((sums[0], ann[i][:, 0:BANK]), (sums[1], ann[i][:, BANK:S]))
+        def ann_banks(i):
+            return [
+                (product_half(w2_columns, i, h, BANKS + 2 * i + h), ann[i][:, h * BANK : (h + 1) * BANK])
+                for h in range(2)
+            ]
 
-        ann_tile(0)
         w2_piece(0, 1, held([P, BANK, PACK], BF16, "woven2"))
         w2_piece(1, 1, held([P, BANK, PACK], BF16, "woven0"))
 
@@ -320,14 +319,18 @@ def tile_list_annotation_disagreement_kernel(
         z0_woven = staged([P, PAIRS, PACK], BF16, "z0_woven", ROWS_AT[2] + 4 * KIB)
 
         for i in range(TILES):
-            if i + 1 < TILES:
-                ann_tile(i + 1)
+            if i == 0:
+                empty_banks(ann_banks(0))
+                empty_banks(ann_banks(1))
+            elif i % 2 == 0:
+                empty_banks(ann_banks(i) + ann_banks(i + 1))
             pick_second(i)
-            if i in (2, 3):
-                pick_gates(first_gates[:, i, :], head[i], pos1_sb[:])
+            if i == 3:
+                for t in (2, 3):
+                    pick_gates(first_gates[:, t, :], head[t], pos1_sb[:])
             if i in (2, 4):
                 n = i // 2 - 1
-                late_woven = staged([P, PASSES * BANK, PACK], BF16, "late_woven%d" % n, ROWS_AT[1 + 2 * n])
+                late_woven = staged([P, PASSES * BANK, PACK], BF16, "late_woven%d" % n, ROWS_AT[3])
                 for a in range(PASSES):
                     weave(late_rows[:, PASSES * n + a, :, :], late_woven[:, a * BANK : (a + 1) * BANK, :])
             subtract(i)
@@ -347,10 +350,10 @@ def tile_list_annotation_disagreement_kernel(
 
         for h in range(2):
             cols = slice(h * BANK, (h + 1) * BANK)
-            for t in range(0, PACK, 2):
-                turn = BANKS + 2 * TILES + PACK * h + t
-                sums = [product_half(w1_columns, PACK + t + e, h, turn + e) for e in range(2)]
-                empty_pair((sums[0], head[PACK + t][:, cols]), (sums[1], head[PACK + t + 1][:, cols]))
+            turn = BANKS + 2 * TILES + PACK * h
+            empty_banks(
+                [(product_half(w1_columns, PACK + t, h, turn + t), head[PACK + t][:, cols]) for t in range(PACK)]
+            )
         for q in range(4):
             nc.sync.dma_start(
                 out=picked_plane[QUADRANT * q + 4 : QUADRANT * q + 12, 0:N].bitcast(I32),
@@ -374,7 +377,7 @@ def tile_list_annotation_disagreement_kernel(
             width = arcs.stop - arcs.start
             last = u == len(ARC_PIECES) - 1
             per_bank = N // P // 2 if last else BANK // width
-            result = held([P, N // P, width], F32, "head%d" % (0, 1, 3)[u])
+            result = held([P, N // P, width], F32, ("head0", "head1", "ann0")[u])
             stored = out[:, arcs].rearrange("(n p) m -> p n m", p=P)
             operands = [
                 (w4_mx[a][0], w4_mx[a][1], guide_mx[a][0][:, arcs], guide_mx[a][1][:, arcs]) for a in range(PASSES)

@@ -30,8 +30,8 @@ STRIPE = 16
 ALIGN = 256
 SCALE_ROWS_AT = 96
 ARC_PIECES = (slice(0, 256), slice(256, 384), slice(384, 512))
-FIRST_GROUPS = ((0, 0), (1, 0), (0, 1), (2, 0), (1, 1), (2, 1), (3, 0), (3, 1))
-VECTOR_GROUPS = (0, 3, 7)
+FIRST_GROUPS = ((0, 0), (1, 0), (2, 0), (0, 1), (1, 1), (2, 1), (3, 0), (3, 1))
+VECTOR_GROUPS = (7,)
 
 KIB = 1024
 LATE_ROWS_AT = 0
@@ -93,6 +93,18 @@ def tile_list_annotation_disagreement_kernel(
             columns = w1_words[:, :, 2 * b * K_PASS : 2 * (b + 1) * K_PASS]
             nc.sync.dma_start(out=words[:].bitcast(I32), in_=columns.rearrange("a p c -> p a c").bitcast(I32))
             return words
+
+        def quantize(woven, name, parts):
+            width = woven.shape[1]
+            codes = held([P, width], U32, name + "_codes")
+            plane = held([P, width], U8, name + "_plane")
+            for cols in parts(width):
+                nc.vector.quantize_mx(
+                    out=codes[:, cols].bitcast(FP8X4),
+                    scales=plane[:, cols],
+                    in_=woven[:, cols, :].rearrange("p c j -> p (c j)"),
+                )
+            return codes, plane
 
         warm = held([P, 2], F32, "warm")
         nc.gpsimd.memset(warm[:, 0:1], 0.0)
@@ -158,18 +170,6 @@ def tile_list_annotation_disagreement_kernel(
                     raw[:].rearrange("p j (m t) -> p m j t", t=PACK)[:, :, :, pair],
                 )
 
-        def quantize(woven, name, parts):
-            width = woven.shape[1]
-            codes = held([P, width], U32, name + "_codes")
-            plane = held([P, width], U8, name + "_plane")
-            for cols in parts(width):
-                nc.vector.quantize_mx(
-                    out=codes[:, cols].bitcast(FP8X4),
-                    scales=plane[:, cols],
-                    in_=woven[:, cols, :].rearrange("p c j -> p (c j)"),
-                )
-            return codes, plane
-
         def product_half(stationary, i, h, turn):
             acc = psum.tile([P, BANK], F32, name="bank%d" % (turn % BANKS))
             cols = slice(h * BANK, (h + 1) * BANK)
@@ -203,7 +203,7 @@ def tile_list_annotation_disagreement_kernel(
             codes, plane = w2_mx[a, b]
             return codes[:, P * t : P * (t + 1)].bitcast(FP8X4), plane[:, P * t : P * (t + 1)]
 
-        head = {i: held([P, S], F32, "head%d" % i) for i in range(TILES) if i not in (2, 3)}
+        head = {i: held([P, S], F32, "head%d" % i) for i in range(TILES) if i != 3}
         ann = [held([P, S], F32, "ann%d" % i) for i in range(TILES)]
         second = {}
         diff = {}
@@ -265,7 +265,6 @@ def tile_list_annotation_disagreement_kernel(
             weave_sorted(w2_raw[a, b], woven)
             w2_mx[a, b] = quantize(woven, "w2_%d%d" % (a, b), halves)
 
-        head[2] = staged([P, S], F32, "head2", ROWS_AT[0])
         head[3] = staged([P, S], F32, "head3", ROWS_AT[1])
         first_gates = held([P, PACK, PAIRS], F32, "gate0")
         first_sums = [product_half(w1_columns, t, h, turn) for turn, (t, h) in enumerate(FIRST_GROUPS)]
@@ -281,13 +280,13 @@ def tile_list_annotation_disagreement_kernel(
         for turn in range(3):
             empty_first(turn)
         w2_piece(0, 0, held([P, BANK, PACK], BF16, "woven0"))
-        for turn in range(3, 5):
+        for turn in (3, 4):
             empty_first(turn)
         pick_gates(first_gates[:, 0, :], head[0], pos1_sb[:])
         empty_first(5)
         pick_gates(first_gates[:, 1, :], head[1], pos1_sb[:])
         w2_piece(1, 0, held([P, BANK, PACK], BF16, "woven1"))
-        for turn in range(6, 8):
+        for turn in (6, 7):
             empty_first(turn)
         w2_raw[1, 1] = load_rows(w2, 1, w2_cols(1), "w2_raw11", 2)
         gain_sb = staged([P, 2, PACK], F32, "gain_sb", GAIN_AT)
@@ -363,7 +362,7 @@ def tile_list_annotation_disagreement_kernel(
         for u, arcs in enumerate(ARC_PIECES):
             width = arcs.stop - arcs.start
             if u == 0:
-                gates = staged([P, PACK, width], F32, "gate10", ROWS_AT[0] + 4 * KIB)
+                gates = staged([P, PACK, width], F32, "gate10", ROWS_AT[0])
             else:
                 gates = held([P, PACK, width], F32, "gate1%d" % u)
             for t in range(PACK):
@@ -377,7 +376,7 @@ def tile_list_annotation_disagreement_kernel(
             width = arcs.stop - arcs.start
             last = u == len(ARC_PIECES) - 1
             per_bank = N // P // 2 if last else BANK // width
-            result = held([P, N // P, width], F32, ("head0", "head1", "ann0")[u])
+            result = held([P, N // P, width], F32, "head%d" % u)
             stored = out[:, arcs].rearrange("(n p) m -> p n m", p=P)
             operands = [
                 (w4_mx[a][0], w4_mx[a][1], guide_mx[a][0][:, arcs], guide_mx[a][1][:, arcs]) for a in range(PASSES)

@@ -131,6 +131,21 @@ def tile_list_annotation_disagreement_kernel(
             )
         tab_sb.append(load_tab(1))
 
+        zeros = held([P, P, PACK], BF16, "zeros")
+        nc.vector.memset(zeros[:], 0.0)
+        zero_codes, zero_plane = quantize(zeros, "zero", whole)
+        idle_bank = psum.tile([P, BANK], F32, name="bank%d" % (BANKS - 1))
+        for turn in range(4):
+            nc.tensor.matmul_mx(
+                out=idle_bank[:],
+                lhsT=zero_codes[:].bitcast(FP8X4),
+                lhsT_scale=zero_plane[:],
+                rhs=w1_first[:, 0, :].bitcast(FP4X4),
+                rhs_scale=w1_plane[:, 0:BANK],
+                start=True,
+                stop=True,
+            )
+
         picked_scale_rows = staged([P, S], U8, "picked_rows", PICKED_ROWS_AT)
         nc.vector.tensor_copy(picked_scale_rows[:], tab_scale_rows[:].indirect(offs_sb[:]))
         for q in (0, 2, 1, 3):

@@ -31,7 +31,7 @@ ALIGN = 256
 SCALE_ROWS_AT = 96
 ARC_PIECES = (slice(0, 256), slice(256, 384), slice(384, 512))
 FIRST_GROUPS = ((0, 0), (1, 0), (2, 0), (0, 1), (1, 1), (2, 1), (3, 0), (3, 1))
-VECTOR_GROUPS = (7,)
+VECTOR_GROUPS = (6, 7)
 
 KIB = 1024
 LATE_ROWS_AT = 0
@@ -122,7 +122,6 @@ def tile_list_annotation_disagreement_kernel(
         picked_plane = held([P, PASSES * S], U8, "picked_plane")
         nc.vector.memset(picked_plane[:].bitcast(I32), 0)
         pos1_sb = load_list(pos1, "pos1_sb")
-        w1_first = load_w1(0, held([P, PASSES, 2 * K_PASS], U8, "w1_first"))
         tab_sb = [load_tab(0)]
         for r in range(4):
             nc.sync.dma_start(
@@ -130,17 +129,21 @@ def tile_list_annotation_disagreement_kernel(
                 in_=w1_scales[:, r:16:4, :].rearrange("a q c -> q a c").bitcast(I32),
             )
         tab_sb.append(load_tab(1))
+        w1_first = load_w1(0, held([P, PASSES, 2 * K_PASS], U8, "w1_first"))
 
-        zeros = held([P, P, PACK], BF16, "zeros")
-        nc.vector.memset(zeros[:], 0.0)
-        zero_codes, zero_plane = quantize(zeros, "zero", whole)
+        zeros = held([P, P * PACK], BF16, "woven2")
+        nc.vector.memset(zeros[:].bitcast(I32), 0)
+        zero_codes = held([P, BANK], U32, "woven1")
+        nc.gpsimd.memset(zero_codes[:, P:BANK].bitcast(I32), 0)
+        zero_plane = held([P, P], U8, "zero_plane")
+        nc.vector.quantize_mx(out=zero_codes[:, 0:P].bitcast(FP8X4), scales=zero_plane[:], in_=zeros[:])
         idle_bank = psum.tile([P, BANK], F32, name="bank%d" % (BANKS - 1))
-        for turn in range(4):
+        for turn in range(5):
             nc.tensor.matmul_mx(
                 out=idle_bank[:],
-                lhsT=zero_codes[:].bitcast(FP8X4),
+                lhsT=zero_codes[:, 0:P].bitcast(FP8X4),
                 lhsT_scale=zero_plane[:],
-                rhs=w1_first[:, 0, :].bitcast(FP4X4),
+                rhs=zero_codes[:].bitcast(FP8X4),
                 rhs_scale=w1_plane[:, 0:BANK],
                 start=True,
                 stop=True,
@@ -259,10 +262,11 @@ def tile_list_annotation_disagreement_kernel(
                 )
 
         pick_words(0)
-        nc.gpsimd.tensor_copy(
-            w1_sorted[0][:].rearrange("p a (t m e) -> p a t m e", t=PACK, e=2),
-            w1_first[:].rearrange("p a (m t e) -> p a t m e", t=PACK, e=2),
-        )
+        for t in range(PACK):
+            nc.scalar.copy(
+                w1_sorted[0][:].bitcast(U16).rearrange("p a (t m) -> p a t m", t=PACK)[:, :, t, :],
+                w1_first[:].bitcast(U16).rearrange("p a (m t) -> p a t m", t=PACK)[:, :, t, :],
+            )
         sort_plane(0)
         sort_plane(1)
         pick_words(1)

@@ -31,7 +31,7 @@ ALIGN = 256
 SCALE_ROWS_AT = 96
 ARC_PIECES = (slice(0, 256), slice(256, 384), slice(384, 512))
 FIRST_GROUPS = ((0, 0), (1, 0), (2, 0), (0, 1), (1, 1), (2, 1), (3, 0), (3, 1))
-VECTOR_GROUPS = (6, 7)
+VECTOR_COLUMNS = {6: BANK // 2, 7: BANK}
 
 KIB = 1024
 LATE_ROWS_AT = 0
@@ -291,10 +291,11 @@ def tile_list_annotation_disagreement_kernel(
         def empty_first(turn):
             t, h = FIRST_GROUPS[turn]
             window = head[t][:, h * BANK : (h + 1) * BANK]
-            if turn in VECTOR_GROUPS:
-                nc.vector.tensor_copy(window, first_sums[turn][:])
-            else:
-                nc.scalar.copy(window, first_sums[turn][:])
+            share = VECTOR_COLUMNS.get(turn, 0)
+            if share > 0:
+                nc.vector.tensor_copy(window[:, 0:share], first_sums[turn][:, 0:share])
+            if share < BANK:
+                nc.scalar.copy(window[:, share:BANK], first_sums[turn][:, share:BANK])
 
         for turn in range(3):
             empty_first(turn)

@@ -35,12 +35,12 @@ VECTOR_COLUMNS = {6: BANK // 2, 7: BANK}
 
 KIB = 1024
 LATE_ROWS_AT = 0
-TAB_AT = (57 * KIB, 31 * KIB)
-TAB_SCALES_AT = 48 * KIB
-GAIN_AT = 32 * KIB
-ROWS_AT = (41 * KIB, 49 * KIB, 33 * KIB, 57 * KIB + 512)
-PICKED_ROWS_AT = 65 * KIB
-W1_LAST_AT = 65 * KIB + 512
+TAB_AT = (59 * KIB, 33 * KIB)
+TAB_SCALES_AT = 50 * KIB
+GAIN_AT = 34 * KIB
+ROWS_AT = (43 * KIB, 51 * KIB, 35 * KIB, 59 * KIB + 512)
+PICKED_ROWS_AT = 67 * KIB
+W1_LAST_AT = 67 * KIB + 512
 
 
 def halves(width):
@@ -133,12 +133,12 @@ def tile_list_annotation_disagreement_kernel(
 
         zeros = held([P, P * PACK], BF16, "woven2")
         nc.vector.memset(zeros[:].bitcast(I32), 0)
-        zero_codes = held([P, BANK], U32, "woven1")
+        zero_codes = held([P, BANK], U32, "gate0")
         nc.gpsimd.memset(zero_codes[:, P:BANK].bitcast(I32), 0)
         zero_plane = held([P, P], U8, "zero_plane")
         nc.vector.quantize_mx(out=zero_codes[:, 0:P].bitcast(FP8X4), scales=zero_plane[:], in_=zeros[:])
         idle_bank = psum.tile([P, BANK], F32, name="bank%d" % (BANKS - 1))
-        for turn in range(5):
+        for turn in range(7):
             nc.tensor.matmul_mx(
                 out=idle_bank[:],
                 lhsT=zero_codes[:, 0:P].bitcast(FP8X4),
@@ -237,7 +237,7 @@ def tile_list_annotation_disagreement_kernel(
             if i < 2:
                 diff[i] = staged([P, PAIRS], F32, "diff%d" % i, ROWS_AT[2] + 2 * KIB * i)[:]
             elif i < 6:
-                diff[i] = late_rows[:, 2 * (i // 2 - 1), 1 + i % 2, :]
+                diff[i] = late_rows[:, 2 * (i // 2 - 1), i % 2, :]
             else:
                 diff[i] = held([P, PAIRS], F32, "second%d" % (i - 4))[:]
             nc.vector.tensor_tensor(diff[i], ann[i][:].indirect(pos2_sb[:]), second[i], SUBTRACT)
@@ -325,7 +325,9 @@ def tile_list_annotation_disagreement_kernel(
         w2_piece(0, 1, held([P, BANK, PACK], BF16, "woven2"))
         w2_piece(1, 1, held([P, BANK, PACK], BF16, "woven0"))
 
-        late_rows = staged([P, 2 * PASSES, PACK, BANK], F32, "late_rows", LATE_ROWS_AT)
+        late_tile = staged([P, (2 * PASSES * PACK + 1) * BANK], F32, "late_rows", LATE_ROWS_AT)
+        late_rows = late_tile[:, BANK:].rearrange("p (n j c) -> p n j c", j=PACK, c=BANK)
+        first_weighted = late_tile[:, 0 : 2 * PASSES * PACK * BANK].rearrange("p (t j c) -> p t j c", j=PACK, c=BANK)
         for n, src in enumerate((guide, w4)):
             nc.sync.dma_start(
                 out=late_rows[:, PASSES * n : PASSES * (n + 1), :, :],
@@ -333,35 +335,43 @@ def tile_list_annotation_disagreement_kernel(
             )
         w3_sb = held([P, 2, N], U32, "woven2")
         nc.sync.dma_start(out=w3_sb[:].bitcast(I32), in_=w3_words.rearrange("a p c i -> p a (c i)").bitcast(I32))
-        weighted = [late_rows[:, :, 0, :], held([P, PACK, PAIRS], F32, "weighted1")[:]]
+        weighted = [first_weighted[:, :, 0, :], held([P, PACK, PAIRS], F32, "weighted1")[:]]
         late_mx = {}
         z0_woven = staged([P, PAIRS, PACK], BF16, "z0_woven", ROWS_AT[2] + 4 * KIB)
 
-        for i in range(TILES):
-            if i == 0:
-                empty_banks(ann_banks(0))
-                empty_banks(ann_banks(1))
-            elif i % 2 == 0:
-                empty_banks(ann_banks(i) + ann_banks(i + 1))
-            pick_second(i)
-            if i == 3:
-                for t in (2, 3):
-                    pick_gates(first_gates[:, t, :], head[t], pos1_sb[:])
-            if i in (2, 4):
-                n = i // 2 - 1
+        for pair in range(TILES // 2):
+            low, high = 2 * pair, 2 * pair + 1
+            if pair == 0:
+                empty_banks(ann_banks(low))
+                empty_banks(ann_banks(high))
+            else:
+                empty_banks(ann_banks(low) + ann_banks(high))
+            pick_second(low)
+            pick_second(high)
+            if pair == 0:
+                subtract(low)
+                subtract(high)
+                square(low, whole)
+            elif pair < 3:
+                n = pair - 1
                 late_woven = staged([P, PASSES * BANK, PACK], BF16, "late_woven%d" % n, ROWS_AT[3])
                 for a in range(PASSES):
                     weave(late_rows[:, PASSES * n + a, :, :], late_woven[:, a * BANK : (a + 1) * BANK, :])
-            subtract(i)
-            if i in (2, 4):
+                subtract(high)
                 late_mx[n] = quantize(late_woven, "late%d" % n, whole)
-            if i >= 2:
-                square(i - 2, whole)
-            if i == 6:
+                subtract(low)
+                square(low - 1, whole)
+                square(low, whole)
+            else:
+                for t in (2, 3):
+                    pick_gates(first_gates[:, t, :], head[t], pos1_sb[:])
+                subtract(high)
+                square(low - 1, whole)
+                subtract(low)
                 make_z(weighted[0], first_gates[:], z0_woven, whole)
-        square(TILES - 2, whole)
-        z0_mx = quantize(z0_woven, "z0", whole)
-        square(TILES - 1, halves)
+                square(high, whole)
+                z0_mx = quantize(z0_woven, "z0", whole)
+                square(low, halves)
         guide_mx, w4_mx = [
             [(codes[:, a * BANK : (a + 1) * BANK], plane[:, a * BANK : (a + 1) * BANK]) for a in range(PASSES)]
             for codes, plane in (late_mx[0], late_mx[1])
@@ -384,7 +394,7 @@ def tile_list_annotation_disagreement_kernel(
             if u == 0:
                 gates = staged([P, PACK, width], F32, "gate10", ROWS_AT[0])
             else:
-                gates = held([P, PACK, width], F32, "gate1%d" % u)
+                gates = staged([P, PACK, width], F32, "gate1%d" % u, ROWS_AT[0] + (2 + 2 * u) * KIB)
             for t in range(PACK):
                 pick_gates(gates[:, t, :], head[PACK + t], entries(pos1_sb, arcs))
             woven = held([P, width, PACK], BF16, "z1%d_woven" % u)

@@ -30,6 +30,7 @@ STRIPE = 16
 ALIGN = 256
 SCALE_ROWS_AT = 96
 ARC_PIECES = (slice(0, 256), slice(256, 384), slice(384, 512))
+GATE_PARTS = (1, 1, 2)
 FIRST_GROUPS = ((0, 0), (1, 0), (2, 0), (0, 1), (1, 1), (2, 1), (3, 0), (3, 1))
 VECTOR_COLUMNS = {6: BANK // 2, 7: BANK}
 
@@ -121,7 +122,6 @@ def tile_list_annotation_disagreement_kernel(
         nc.vector.memset(tab_scale_rows[0:SCALE_ROWS_AT, :].bitcast(I32), 0)
         picked_plane = held([P, PASSES * S], U8, "picked_plane")
         nc.vector.memset(picked_plane[:].bitcast(I32), 0)
-        pos1_sb = load_list(pos1, "pos1_sb")
         tab_sb = [load_tab(0)]
         for r in range(4):
             nc.sync.dma_start(
@@ -130,6 +130,7 @@ def tile_list_annotation_disagreement_kernel(
             )
         tab_sb.append(load_tab(1))
         w1_first = load_w1(0, held([P, PASSES, 2 * K_PASS], U8, "w1_first"))
+        pos1_sb = load_list(pos1, "pos1_sb")
 
         zeros = held([P, P * PACK], BF16, "woven2")
         nc.vector.memset(zeros[:].bitcast(I32), 0)
@@ -391,14 +392,14 @@ def tile_list_annotation_disagreement_kernel(
         z1_mx = []
         for u, arcs in enumerate(ARC_PIECES):
             width = arcs.stop - arcs.start
-            if u == 0:
-                gates = staged([P, PACK, width], F32, "gate10", ROWS_AT[0])
-            else:
-                gates = staged([P, PACK, width], F32, "gate1%d" % u, ROWS_AT[0] + (2 + 2 * u) * KIB)
-            for t in range(PACK):
-                pick_gates(gates[:, t, :], head[PACK + t], entries(pos1_sb, arcs))
             woven = held([P, width, PACK], BF16, "z1%d_woven" % u)
-            make_z(weighted[1][:, :, arcs], gates[:], woven, halves)
+            step = width // GATE_PARTS[u]
+            for at in range(0, width, step):
+                places = slice(arcs.start + at, arcs.start + at + step)
+                gates = staged([P, PACK, step], F32, "gate1_%d" % places.start, ROWS_AT[0] + 16 * places.start)
+                for t in range(PACK):
+                    pick_gates(gates[:, t, :], head[PACK + t], entries(pos1_sb, places))
+                make_z(weighted[1][:, :, places], gates[:], woven[:, at : at + step, :], halves if step == width else whole)
             z1_mx.append(quantize(woven, "z1%d" % u, halves))
 
         bank = 0
@@ -429,7 +430,7 @@ def tile_list_annotation_disagreement_kernel(
                             stop=(j == len(operands) - 1 and n == per_bank - 1),
                         )
                 part = slice(first, first + per_bank)
-                if last and first == 0:
+                if u > 0 and first == 0:
                     nc.vector.tensor_copy(result[:, part, :], acc[:])
                 else:
                     nc.scalar.copy(result[:, part, :], acc[:])

@@ -139,7 +139,7 @@ def tile_list_annotation_disagreement_kernel(
         zero_plane = held([P, P], U8, "zero_plane")
         nc.vector.quantize_mx(out=zero_codes[:, 0:P].bitcast(FP8X4), scales=zero_plane[:], in_=zeros[:])
         idle_bank = psum.tile([P, BANK], F32, name="bank%d" % (BANKS - 1))
-        for turn in range(7):
+        for turn in range(5):
             nc.tensor.matmul_mx(
                 out=idle_bank[:],
                 lhsT=zero_codes[:, 0:P].bitcast(FP8X4),

@@ -2,8 +2,8 @@ from contextlib import ExitStack
 
 import concourse.mybir as mybir
 
-K, T, S, PAIRS, H, N = 1024, 2048, 1024, 512, 1024, 512
-FLOPS = 2 * K * H * S * 2 + 2 * H * N * PAIRS + 2 * K * N * PAIRS
+K, T, S, ARCS, H, N = 1024, 2048, 1024, 512, 1024, 512
+FLOPS = 2 * K * H * S * 2 + 2 * H * N * ARCS + 2 * K * N * ARCS
 
 F32 = mybir.dt.float32
 BF16 = mybir.dt.bfloat16
@@ -28,20 +28,23 @@ TILES = H // P
 QUADRANT = 32
 STRIPE = 16
 ALIGN = 256
+RUN = 4
 SCALE_ROWS_AT = 96
+WARM_PASSES = 5
 ARC_PIECES = (slice(0, 256), slice(256, 384), slice(384, 512))
 GATE_PARTS = (1, 1, 2)
-FIRST_GROUPS = ((0, 0), (1, 0), (2, 0), (0, 1), (1, 1), (2, 1), (3, 0), (3, 1))
-VECTOR_COLUMNS = {6: BANK // 2, 7: BANK}
+GAP_SHARE = 256
+LATE_SHARE = 128
+OUT_BANKS = (2, 7, 4, 5, 6)
 
 KIB = 1024
 LATE_ROWS_AT = 0
 TAB_AT = (59 * KIB, 33 * KIB)
-TAB_SCALES_AT = 50 * KIB
 GAIN_AT = 34 * KIB
-ROWS_AT = (43 * KIB, 51 * KIB, 35 * KIB, 59 * KIB + 512)
+TAB_SCALES_AT = 50 * KIB
+W1_SECOND_AT = 67 * KIB + 512
 PICKED_ROWS_AT = 67 * KIB
-W1_LAST_AT = 67 * KIB + 512
+W2_AT = {(0, 0): 43 * KIB, (1, 0): 51 * KIB, (0, 1): 59 * KIB + 512, (1, 1): 35 * KIB}
 
 
 def halves(width):
@@ -72,16 +75,13 @@ def tile_list_annotation_disagreement_kernel(
         def staged(shape, dtype, name, offset):
             return stage.tile(shape, dtype, name=name, align_bytes=ALIGN, offset=offset)
 
+        def bank_tile(number, shape):
+            return psum.tile(shape, F32, name="bank%d" % (number % BANKS))
+
         def load_list(src, name):
             tile = held(list(src.shape), U16, name)
             nc.sync.dma_start(tile[:], src)
             return tile
-
-        def load_rows(src, a, cols, name, slot):
-            raw = staged([P, PACK, BANK], F32, name, ROWS_AT[slot])
-            rows = src[a * K_PASS : (a + 1) * K_PASS, cols]
-            nc.sync.dma_start(out=raw[:], in_=rows.rearrange("(p j) c -> p j c", j=PACK))
-            return raw
 
         def load_tab(a):
             words = staged([P, T], U32, "tab%d" % a, TAB_AT[a])
@@ -95,6 +95,12 @@ def tile_list_annotation_disagreement_kernel(
             nc.sync.dma_start(out=words[:].bitcast(I32), in_=columns.rearrange("a p c -> p a c").bitcast(I32))
             return words
 
+        def load_w2(a, b):
+            raw = staged([P, PACK, K_PASS], F32, "w2_raw%d%d" % (a, b), W2_AT[a, b])
+            rows = w2[a * K_PASS : (a + 1) * K_PASS, b * K_PASS : (b + 1) * K_PASS]
+            nc.sync.dma_start(out=raw[:], in_=rows.rearrange("(p j) c -> p j c", j=PACK))
+            return raw
+
         def quantize(woven, name, parts):
             width = woven.shape[1]
             codes = held([P, width], U32, name + "_codes")
@@ -106,6 +112,13 @@ def tile_list_annotation_disagreement_kernel(
                     in_=woven[:, cols, :].rearrange("p c j -> p (c j)"),
                 )
             return codes, plane
+
+        def add_up(passes):
+            for j, (acc, lhs, lhs_plane, rhs, rhs_plane) in enumerate(passes):
+                nc.tensor.matmul_mx(
+                    out=acc, lhsT=lhs, lhsT_scale=lhs_plane, rhs=rhs, rhs_scale=rhs_plane,
+                    start=(j == 0), stop=(j == len(passes) - 1),
+                )
 
         warm = held([P, 2], F32, "warm")
         nc.gpsimd.memset(warm[:, 0:1], 0.0)
@@ -129,7 +142,7 @@ def tile_list_annotation_disagreement_kernel(
                 in_=w1_scales[:, r:16:4, :].rearrange("a q c -> q a c").bitcast(I32),
             )
         tab_sb.append(load_tab(1))
-        w1_first = load_w1(0, held([P, PASSES, 2 * K_PASS], U8, "w1_first"))
+        w1_raw = [load_w1(0, held([P, PASSES, 2 * K_PASS], U8, "w1_first"))]
         pos1_sb = load_list(pos1, "pos1_sb")
 
         zeros = held([P, P * PACK], BF16, "woven2")
@@ -138,17 +151,12 @@ def tile_list_annotation_disagreement_kernel(
         nc.gpsimd.memset(zero_codes[:, P:BANK].bitcast(I32), 0)
         zero_plane = held([P, P], U8, "zero_plane")
         nc.vector.quantize_mx(out=zero_codes[:, 0:P].bitcast(FP8X4), scales=zero_plane[:], in_=zeros[:])
-        idle_bank = psum.tile([P, BANK], F32, name="bank%d" % (BANKS - 1))
-        for turn in range(5):
-            nc.tensor.matmul_mx(
-                out=idle_bank[:],
-                lhsT=zero_codes[:, 0:P].bitcast(FP8X4),
-                lhsT_scale=zero_plane[:],
-                rhs=zero_codes[:].bitcast(FP8X4),
-                rhs_scale=w1_plane[:, 0:BANK],
-                start=True,
-                stop=True,
-            )
+        idle_bank = bank_tile(BANKS - 1, [P, BANK])
+        for turn in range(WARM_PASSES):
+            add_up([(
+                idle_bank[:], zero_codes[:, 0:P].bitcast(FP8X4), zero_plane[:],
+                zero_codes[:].bitcast(FP8X4), w1_plane[:, 0:BANK],
+            )])
 
         picked_scale_rows = staged([P, S], U8, "picked_rows", PICKED_ROWS_AT)
         nc.vector.tensor_copy(picked_scale_rows[:], tab_scale_rows[:].indirect(offs_sb[:]))
@@ -158,15 +166,19 @@ def tile_list_annotation_disagreement_kernel(
                 out=picked_plane[QUADRANT * q : QUADRANT * q + 4, :].bitcast(I32),
                 in_=picked_scale_rows[first_row : first_row + 8, :].bitcast(I32),
             )
+        w2_raw = {(a, 0): load_w2(a, 0) for a in range(PASSES)}
+        w1_raw.append(load_w1(1, staged([P, PASSES, 2 * K_PASS], U8, "w1_second", W1_SECOND_AT)))
+        pos3_sb = load_list(pos3, "pos3_sb")
+        pos2_sb = load_list(pos2, "pos2_sb")
+        w2_raw[0, 1] = load_w2(0, 1)
 
         picked = [held([P, S], U32, "picked%d" % a) for a in range(PASSES)]
-
-        def pick_words(a):
-            for places in halves(S):
-                nc.vector.tensor_copy(picked[a][:, places], tab_sb[a][:].indirect(entries(offs_sb, places)))
-
         w1_sorted = [held([P, PASSES, 2 * K_PASS], U8, "w1_sorted%d" % b) for b in range(2)]
         w1_sorted_plane = [held([P, PASSES, K_PASS], U8, "w1_sorted_plane%d" % b) for b in range(2)]
+
+        def pick_words(a, parts):
+            for places in parts:
+                nc.vector.tensor_copy(picked[a][:, places], tab_sb[a][:].indirect(entries(offs_sb, places)))
 
         def sort_plane(b):
             cols = slice(b * K_PASS, (b + 1) * K_PASS)
@@ -176,39 +188,6 @@ def tile_list_annotation_disagreement_kernel(
                     "p a (g m t) -> p a g t m", t=PACK, m=16
                 ),
             )
-
-        def weave(raw, woven):
-            nc.vector.tensor_copy(
-                woven.rearrange("p (g i) j -> p g j i", i=4), raw.rearrange("p j (g i) -> p g j i", i=4)
-            )
-
-        def weave_sorted(raw, woven):
-            for pair in halves(PACK):
-                nc.vector.tensor_copy(
-                    woven[:].rearrange("p (t m) j -> p m j t", t=PACK)[:, :, :, pair],
-                    raw[:].rearrange("p j (m t) -> p m j t", t=PACK)[:, :, :, pair],
-                )
-
-        def product_half(stationary, i, h, turn):
-            acc = psum.tile([P, BANK], F32, name="bank%d" % (turn % BANKS))
-            cols = slice(h * BANK, (h + 1) * BANK)
-            order = (0, 1) if turn < 2 else (1, 0)
-            for a in order:
-                codes, plane = stationary(a, i)
-                nc.tensor.matmul_mx(
-                    out=acc[:],
-                    lhsT=codes,
-                    lhsT_scale=plane,
-                    rhs=picked[a][:, cols].bitcast(FP8X4),
-                    rhs_scale=picked_plane[:, a * S + h * BANK : a * S + (h + 1) * BANK],
-                    start=(a == order[0]),
-                    stop=(a == order[1]),
-                )
-            return acc
-
-        def empty_banks(filled):
-            for acc, window in filled[-1:] + filled[:-1]:
-                nc.scalar.copy(window, acc[:])
 
         def w1_columns(a, i):
             b, t = divmod(i, PACK)
@@ -222,33 +201,43 @@ def tile_list_annotation_disagreement_kernel(
             codes, plane = w2_mx[a, b]
             return codes[:, P * t : P * (t + 1)].bitcast(FP8X4), plane[:, P * t : P * (t + 1)]
 
-        head = {i: held([P, S], F32, "head%d" % i) for i in range(TILES) if i != 3}
-        ann = [held([P, S], F32, "ann%d" % i) for i in range(TILES)]
-        second = {}
-        diff = {}
+        def picked_columns(a, cols):
+            return picked[a][:, cols].bitcast(FP8X4), picked_plane[:, a * S + cols.start : a * S + cols.stop]
 
-        def pick_second(i):
-            if i < 2:
-                second[i] = first_gates[:, 2 + i, :]
-            else:
-                second[i] = held([P, PAIRS], F32, "second%d" % i)[:]
-            nc.scalar.activation(second[i], ann[i][:].indirect(pos3_sb[:]), COPY)
+        def fill_bank(number, stationary, parts, order):
+            acc = bank_tile(number, [P, BANK])
+            width = BANK // len(parts)
+            sums = [acc[:, n * width : (n + 1) * width] for n in range(len(parts))]
+            add_up([
+                (sums[n],) + stationary(a, i) + picked_columns(a, cols)
+                for a in order
+                for n, (i, cols) in enumerate(parts)
+            ])
+            return sums
 
-        def subtract(i):
-            if i < 2:
-                diff[i] = staged([P, PAIRS], F32, "diff%d" % i, ROWS_AT[2] + 2 * KIB * i)[:]
-            elif i < 6:
-                diff[i] = late_rows[:, 2 * (i // 2 - 1), i % 2, :]
-            else:
-                diff[i] = held([P, PAIRS], F32, "second%d" % (i - 4))[:]
-            nc.vector.tensor_tensor(diff[i], ann[i][:].indirect(pos2_sb[:]), second[i], SUBTRACT)
+        def tile_banks(number, stationary, i, window):
+            return [
+                (fill_bank(number + h, stationary, [(i, cols)], (1, 0))[0], window[:, cols])
+                for h, cols in enumerate(halves(S))
+            ]
 
-        def square(i, parts):
-            b, t = divmod(i, PACK)
-            for arcs in parts(PAIRS):
-                nc.vector.scalar_tensor_tensor(
-                    weighted[b][:, t, arcs], diff[i][:, arcs], gain_sb[:, b, t : t + 1], diff[i][:, arcs], MULT, MULT
+        def empty_banks(filled):
+            for acc, window in filled[-1:] + filled[:-1]:
+                nc.scalar.copy(window, acc)
+
+        def weave(raw, woven):
+            nc.vector.tensor_copy(
+                woven.rearrange("p (g i) j -> p g j i", i=RUN), raw.rearrange("p j (g i) -> p g j i", i=RUN)
+            )
+
+        def w2_piece(a, b, name):
+            woven = held([P, K_PASS, PACK], BF16, name)
+            for pair in halves(PACK):
+                nc.vector.tensor_copy(
+                    woven[:].rearrange("p (t m) j -> p m j t", t=PACK)[:, :, :, pair],
+                    w2_raw[a, b][:].rearrange("p j (m t) -> p m j t", t=PACK)[:, :, :, pair],
                 )
+            w2_mx[a, b] = quantize(woven, "w2_%d%d" % (a, b), halves)
 
         def pick_gates(gates, window, offsets):
             nc.scalar.activation(gates, window[:].indirect(offsets), SIGMOID, scale=-1.0)
@@ -256,75 +245,59 @@ def tile_list_annotation_disagreement_kernel(
         def make_z(values, gates, woven, parts):
             for cols in parts(values.shape[2]):
                 nc.vector.tensor_tensor(
-                    woven[:, cols, :].rearrange("p (g i) t -> p g t i", i=4),
-                    values[:, :, cols].rearrange("p t (g i) -> p g t i", i=4),
-                    gates[:, :, cols].rearrange("p t (g i) -> p g t i", i=4),
+                    woven[:, cols, :].rearrange("p (g i) t -> p g t i", i=RUN),
+                    values[:, :, cols].rearrange("p t (g i) -> p g t i", i=RUN),
+                    gates[:, :, cols].rearrange("p t (g i) -> p g t i", i=RUN),
                     MULT,
                 )
 
-        pick_words(0)
+        pick_words(0, halves(S))
         for t in range(PACK):
             nc.scalar.copy(
                 w1_sorted[0][:].bitcast(U16).rearrange("p a (t m) -> p a t m", t=PACK)[:, :, t, :],
-                w1_first[:].bitcast(U16).rearrange("p a (m t) -> p a t m", t=PACK)[:, :, t, :],
+                w1_raw[0][:].bitcast(U16).rearrange("p a (m t) -> p a t m", t=PACK)[:, :, t, :],
             )
         sort_plane(0)
         sort_plane(1)
-        pick_words(1)
+        pick_words(1, halves(S))
 
-        def w2_cols(b):
-            return slice(b * K_PASS, (b + 1) * K_PASS)
+        head = {i: held([P, S], F32, "head%d" % i) for i in range(TILES) if i != 3}
+        head[3] = staged([P, S], F32, "head3", W2_AT[1, 0])
+        ann = [held([P, S], F32, "ann%d" % i) for i in range(TILES)]
+        first_gates = held([P, PACK, ARCS], F32, "gate0")
+        low, high = halves(S)
+        early = [(0, low), (1, low), (2, low), (0, high), (1, high), (2, high), (3, low), (3, high)]
+        early_sums = [
+            fill_bank(number, w1_columns, [part], (0, 1) if number < 2 else (1, 0))[0]
+            for number, part in enumerate(early)
+        ]
 
-        w2_raw = {(a, 0): load_rows(w2, a, w2_cols(0), "w2_raw%d0" % a, a) for a in range(PASSES)}
-        w1_last = load_w1(1, staged([P, PASSES, 2 * K_PASS], U8, "w1_last", W1_LAST_AT))
-        pos3_sb = load_list(pos3, "pos3_sb")
-        pos2_sb = load_list(pos2, "pos2_sb")
-        w2_raw[0, 1] = load_rows(w2, 0, w2_cols(1), "w2_raw01", 3)
+        def empty_early(number, copy, share=slice(0, BANK)):
+            i, cols = early[number]
+            copy(head[i][:, cols][:, share], early_sums[number][:, share])
 
-        def w2_piece(a, b, woven):
-            weave_sorted(w2_raw[a, b], woven)
-            w2_mx[a, b] = quantize(woven, "w2_%d%d" % (a, b), halves)
-
-        head[3] = staged([P, S], F32, "head3", ROWS_AT[1])
-        first_gates = held([P, PACK, PAIRS], F32, "gate0")
-        first_sums = [product_half(w1_columns, t, h, turn) for turn, (t, h) in enumerate(FIRST_GROUPS)]
-
-        def empty_first(turn):
-            t, h = FIRST_GROUPS[turn]
-            window = head[t][:, h * BANK : (h + 1) * BANK]
-            share = VECTOR_COLUMNS.get(turn, 0)
-            if share > 0:
-                nc.vector.tensor_copy(window[:, 0:share], first_sums[turn][:, 0:share])
-            if share < BANK:
-                nc.scalar.copy(window[:, share:BANK], first_sums[turn][:, share:BANK])
-
-        for turn in range(3):
-            empty_first(turn)
-        w2_piece(0, 0, held([P, BANK, PACK], BF16, "woven0"))
-        for turn in (3, 4):
-            empty_first(turn)
+        for number in (0, 1, 2):
+            empty_early(number, nc.scalar.copy)
+        w2_piece(0, 0, "woven0")
+        empty_early(3, nc.scalar.copy)
+        empty_early(4, nc.scalar.copy, slice(GAP_SHARE, BANK))
+        empty_early(4, nc.vector.tensor_copy, slice(0, GAP_SHARE))
         pick_gates(first_gates[:, 0, :], head[0], pos1_sb[:])
-        empty_first(5)
+        empty_early(5, nc.scalar.copy)
         pick_gates(first_gates[:, 1, :], head[1], pos1_sb[:])
-        w2_piece(1, 0, held([P, BANK, PACK], BF16, "woven1"))
-        for turn in (6, 7):
-            empty_first(turn)
-        w2_raw[1, 1] = load_rows(w2, 1, w2_cols(1), "w2_raw11", 2)
+        w2_piece(1, 0, "woven1")
+        empty_early(6, nc.vector.tensor_copy, slice(0, LATE_SHARE))
+        empty_early(6, nc.scalar.copy, slice(LATE_SHARE, BANK))
+        empty_early(7, nc.vector.tensor_copy)
+        w2_raw[1, 1] = load_w2(1, 1)
         gain_sb = staged([P, 2, PACK], F32, "gain_sb", GAIN_AT)
         nc.sync.dma_start(out=gain_sb[:], in_=gain.rearrange("(b p t) -> p b t", b=2, t=PACK))
         nc.vector.tensor_copy(
             w1_sorted[1][:].bitcast(U16).rearrange("p a (t g m) -> p a g t m", t=PACK, m=8),
-            w1_last[:].bitcast(U16).rearrange("p a (g m t) -> p a g t m", t=PACK, m=8),
+            w1_raw[1][:].bitcast(U16).rearrange("p a (g m t) -> p a g t m", t=PACK, m=8),
         )
-
-        def ann_banks(i):
-            return [
-                (product_half(w2_columns, i, h, BANKS + 2 * i + h), ann[i][:, h * BANK : (h + 1) * BANK])
-                for h in range(2)
-            ]
-
-        w2_piece(0, 1, held([P, BANK, PACK], BF16, "woven2"))
-        w2_piece(1, 1, held([P, BANK, PACK], BF16, "woven0"))
+        w2_piece(0, 1, "woven2")
+        w2_piece(1, 1, "woven0")
 
         late_tile = staged([P, (2 * PASSES * PACK + 1) * BANK], F32, "late_rows", LATE_ROWS_AT)
         late_rows = late_tile[:, BANK:].rearrange("p (n j c) -> p n j c", j=PACK, c=BANK)
@@ -336,54 +309,75 @@ def tile_list_annotation_disagreement_kernel(
             )
         w3_sb = held([P, 2, N], U32, "woven2")
         nc.sync.dma_start(out=w3_sb[:].bitcast(I32), in_=w3_words.rearrange("a p c i -> p a (c i)").bitcast(I32))
-        weighted = [first_weighted[:, :, 0, :], held([P, PACK, PAIRS], F32, "weighted1")[:]]
+        weighted = [first_weighted[:, :, 0, :], held([P, PACK, ARCS], F32, "weighted1")[:]]
+        z0_woven = staged([P, ARCS, PACK], BF16, "z0_woven", W2_AT[1, 1] + 4 * KIB)
+        third = {}
+        diff = {}
         late_mx = {}
-        z0_woven = staged([P, PAIRS, PACK], BF16, "z0_woven", ROWS_AT[2] + 4 * KIB)
+
+        def pick_third(i):
+            if i < 2:
+                third[i] = first_gates[:, 2 + i, :]
+            else:
+                third[i] = held([P, ARCS], F32, "third%d" % i)[:]
+            nc.scalar.activation(third[i], ann[i][:].indirect(pos3_sb[:]), COPY)
+
+        def subtract(i):
+            if i < 2:
+                diff[i] = staged([P, ARCS], F32, "diff%d" % i, W2_AT[1, 1] + 2 * KIB * i)[:]
+            elif i < 6:
+                diff[i] = late_rows[:, 2 * (i // 2 - 1), i % 2, :]
+            else:
+                diff[i] = held([P, ARCS], F32, "third%d" % (i - 4))[:]
+            nc.vector.tensor_tensor(diff[i], ann[i][:].indirect(pos2_sb[:]), third[i], SUBTRACT)
+
+        def square(i, parts):
+            b, t = divmod(i, PACK)
+            for arcs in parts(ARCS):
+                nc.vector.scalar_tensor_tensor(
+                    weighted[b][:, t, arcs], diff[i][:, arcs], gain_sb[:, b, t : t + 1], diff[i][:, arcs], MULT, MULT
+                )
 
         for pair in range(TILES // 2):
-            low, high = 2 * pair, 2 * pair + 1
+            even, odd = 2 * pair, 2 * pair + 1
+            filled = [tile_banks(2 * i, w2_columns, i, ann[i]) for i in (even, odd)]
             if pair == 0:
-                empty_banks(ann_banks(low))
-                empty_banks(ann_banks(high))
+                empty_banks(filled[0])
+                empty_banks(filled[1])
             else:
-                empty_banks(ann_banks(low) + ann_banks(high))
-            pick_second(low)
-            pick_second(high)
+                empty_banks(filled[0] + filled[1])
+            pick_third(even)
+            pick_third(odd)
             if pair == 0:
-                subtract(low)
-                subtract(high)
-                square(low, whole)
+                subtract(even)
+                subtract(odd)
+                square(even, whole)
             elif pair < 3:
                 n = pair - 1
-                late_woven = staged([P, PASSES * BANK, PACK], BF16, "late_woven%d" % n, ROWS_AT[3])
+                late_woven = staged([P, PASSES * BANK, PACK], BF16, "late_woven%d" % n, W2_AT[0, 1])
                 for a in range(PASSES):
                     weave(late_rows[:, PASSES * n + a, :, :], late_woven[:, a * BANK : (a + 1) * BANK, :])
-                subtract(high)
+                subtract(odd)
                 late_mx[n] = quantize(late_woven, "late%d" % n, whole)
-                subtract(low)
-                square(low - 1, whole)
-                square(low, whole)
+                subtract(even)
+                square(even - 1, whole)
+                square(even, whole)
             else:
                 for t in (2, 3):
                     pick_gates(first_gates[:, t, :], head[t], pos1_sb[:])
-                subtract(high)
-                square(low - 1, whole)
-                subtract(low)
+                subtract(odd)
+                square(even - 1, whole)
+                subtract(even)
                 make_z(weighted[0], first_gates[:], z0_woven, whole)
-                square(high, whole)
+                square(odd, whole)
                 z0_mx = quantize(z0_woven, "z0", whole)
-                square(low, halves)
-        guide_mx, w4_mx = [
-            [(codes[:, a * BANK : (a + 1) * BANK], plane[:, a * BANK : (a + 1) * BANK]) for a in range(PASSES)]
-            for codes, plane in (late_mx[0], late_mx[1])
-        ]
+                square(even, halves)
 
-        for h in range(2):
-            cols = slice(h * BANK, (h + 1) * BANK)
-            turn = BANKS + 2 * TILES + PACK * h
-            empty_banks(
-                [(product_half(w1_columns, PACK + t, h, turn + t), head[PACK + t][:, cols]) for t in range(PACK)]
-            )
+        for h, cols in enumerate(halves(S)):
+            empty_banks([
+                (fill_bank(PACK * h + t, w1_columns, [(PACK + t, cols)], (1, 0))[0], head[PACK + t][:, cols])
+                for t in range(PACK)
+            ])
         for q in range(4):
             nc.sync.dma_start(
                 out=picked_plane[QUADRANT * q + 4 : QUADRANT * q + 12, 0:N].bitcast(I32),
@@ -396,43 +390,41 @@ def tile_list_annotation_disagreement_kernel(
             step = width // GATE_PARTS[u]
             for at in range(0, width, step):
                 places = slice(arcs.start + at, arcs.start + at + step)
-                gates = staged([P, PACK, step], F32, "gate1_%d" % places.start, ROWS_AT[0] + 16 * places.start)
+                gates = staged([P, PACK, step], F32, "gate1_%d" % places.start, W2_AT[0, 0] + 16 * places.start)
                 for t in range(PACK):
                     pick_gates(gates[:, t, :], head[PACK + t], entries(pos1_sb, places))
                 make_z(weighted[1][:, :, places], gates[:], woven[:, at : at + step, :], halves if step == width else whole)
             z1_mx.append(quantize(woven, "z1%d" % u, halves))
 
-        bank = 0
+        (guide_codes, guide_plane), (w4_codes, w4_plane) = late_mx[0], late_mx[1]
+        number = 0
         for u, arcs in enumerate(ARC_PIECES):
             width = arcs.stop - arcs.start
             last = u == len(ARC_PIECES) - 1
             per_bank = N // P // 2 if last else BANK // width
             result = held([P, N // P, width], F32, "head%d" % u)
             stored = out[:, arcs].rearrange("(n p) m -> p n m", p=P)
-            operands = [
-                (w4_mx[a][0], w4_mx[a][1], guide_mx[a][0][:, arcs], guide_mx[a][1][:, arcs]) for a in range(PASSES)
-            ]
+            operands = []
+            for a in range(PASSES):
+                own, cols = slice(a * N, (a + 1) * N), slice(a * ARCS + arcs.start, a * ARCS + arcs.stop)
+                operands.append((w4_codes[:, own], w4_plane[:, own], guide_codes[:, cols], guide_plane[:, cols]))
             operands.append((w3_sb[:, 0, :], picked_plane[4:P, 0:N], z0_mx[0][:, arcs], z0_mx[1][:, arcs]))
             operands.append((w3_sb[:, 1, :], picked_plane[8:P, 0:N], z1_mx[u][0][:], z1_mx[u][1][:]))
-            for first in range(0, N // P, per_bank):
-                acc = psum.tile([P, per_bank, width], F32, name="bank%d" % bank)
-                bank = bank + 1
-                for j, (lhs, lhs_plane, rhs, rhs_plane) in enumerate(operands):
-                    for n in range(per_bank):
-                        rows = slice((first + n) * P, (first + n + 1) * P)
-                        nc.tensor.matmul_mx(
-                            out=acc[:, n, :],
-                            lhsT=lhs[:, rows].bitcast(FP8X4),
-                            lhsT_scale=lhs_plane[:, rows],
-                            rhs=rhs.bitcast(FP8X4),
-                            rhs_scale=rhs_plane,
-                            start=(j == 0 and n == 0),
-                            stop=(j == len(operands) - 1 and n == per_bank - 1),
-                        )
-                part = slice(first, first + per_bank)
-                if u > 0 and first == 0:
+            for at in range(0, N // P, per_bank):
+                acc = bank_tile(OUT_BANKS[number], [P, per_bank, width])
+                number = number + 1
+                add_up([
+                    (
+                        acc[:, n, :], lhs[:, (at + n) * P : (at + n + 1) * P].bitcast(FP8X4),
+                        lhs_plane[:, (at + n) * P : (at + n + 1) * P], rhs.bitcast(FP8X4), rhs_plane,
+                    )
+                    for lhs, lhs_plane, rhs, rhs_plane in operands
+                    for n in range(per_bank)
+                ])
+                part = slice(at, at + per_bank)
+                if u > 0 and at == 0:
                     nc.vector.tensor_copy(result[:, part, :], acc[:])
                 else:
                     nc.scalar.copy(result[:, part, :], acc[:])
-                queue = nc.scalar if last and first > 0 else nc.sync
+                queue = nc.scalar if last and at > 0 else nc.sync
                 queue.dma_start(out=stored[:, part, :], in_=result[:, part, :])

from contextlib import ExitStack

import concourse.mybir as mybir

K, T, S, ARCS, H, N = 1024, 2048, 1024, 512, 1024, 512
FLOPS = 2 * K * H * S * 2 + 2 * H * N * ARCS + 2 * K * N * ARCS

F32 = mybir.dt.float32
BF16 = mybir.dt.bfloat16
I32 = mybir.dt.int32
U32 = mybir.dt.uint32
U16 = mybir.dt.uint16
U8 = mybir.dt.uint8
FP8X4 = mybir.dt.float8_e4m3fn_x4
FP4X4 = mybir.dt.float4_e2m1fn_x4
MULT = mybir.AluOpType.mult
SUBTRACT = mybir.AluOpType.subtract
SIGMOID = mybir.ActivationFunctionType.Sigmoid
COPY = mybir.ActivationFunctionType.Copy

P = 128
PACK = 4
K_PASS = P * PACK
PASSES = K // K_PASS
BANK = 512
BANKS = 8
TILES = H // P
QUADRANT = 32
STRIPE = 16
ALIGN = 256
RUN = 4
SCALE_ROWS_AT = 96
WARM_PASSES = 5
ARC_PIECES = (slice(0, 256), slice(256, 384), slice(384, 512))
GATE_PARTS = (1, 1, 2)
GAP_SHARE = 256
LATE_SHARE = 128
OUT_BANKS = (2, 7, 4, 5, 6)

KIB = 1024
LATE_ROWS_AT = 0
TAB_AT = (59 * KIB, 33 * KIB)
GAIN_AT = 34 * KIB
TAB_SCALES_AT = 50 * KIB
W1_SECOND_AT = 67 * KIB + 512
PICKED_ROWS_AT = 67 * KIB
W2_AT = {(0, 0): 43 * KIB, (1, 0): 51 * KIB, (0, 1): 59 * KIB + 512, (1, 1): 35 * KIB}


def halves(width):
    return slice(0, width // 2), slice(width // 2, width)


def whole(width):
    return (slice(0, width),)


def entries(tile, places):
    return tile[:, places.start // STRIPE : places.stop // STRIPE]


def tile_list_annotation_disagreement_kernel(
    tc, tab_words, tab_scales, offs, pos1, pos2, pos3, w1_words, w1_scales,
    w2, gain, w3_words, w3_scales, guide, w4, out,
):
    nc = tc.nc
    with ExitStack() as ctx:
        keep = ctx.enter_context(tc.tile_pool(name="keep", bufs=1))
        stage = ctx.enter_context(tc.tile_pool(name="stage", bufs=1))
        psum = ctx.enter_context(tc.psum_pool(name="psum", bufs=1))

        def held(shape, dtype, name):
            return keep.tile(shape, dtype, name=name, align_bytes=ALIGN)

        def staged(shape, dtype, name, offset):
            return stage.tile(shape, dtype, name=name, align_bytes=ALIGN, offset=offset)

        def bank_tile(number, shape):
            return psum.tile(shape, F32, name="bank%d" % (number % BANKS))

        def load_list(src, name):
            tile = held(list(src.shape), U16, name)
            nc.sync.dma_start(tile[:], src)
            return tile

        def load_tab(a):
            words = staged([P, T], U32, "tab%d" % a, TAB_AT[a])
            nc.sync.dma_start(
                out=words[:].bitcast(I32), in_=tab_words[a].rearrange("p t i -> p (t i)").bitcast(I32)
            )
            return words

        def load_w1(b, words):
            columns = w1_words[:, :, 2 * b * K_PASS : 2 * (b + 1) * K_PASS]
            nc.sync.dma_start(out=words[:].bitcast(I32), in_=columns.rearrange("a p c -> p a c").bitcast(I32))
            return words

        def load_w2(a, b):
            raw = staged([P, PACK, K_PASS], F32, "w2_raw%d%d" % (a, b), W2_AT[a, b])
            rows = w2[a * K_PASS : (a + 1) * K_PASS, b * K_PASS : (b + 1) * K_PASS]
            nc.sync.dma_start(out=raw[:], in_=rows.rearrange("(p j) c -> p j c", j=PACK))
            return raw

        def quantize(woven, name, parts):
            width = woven.shape[1]
            codes = held([P, width], U32, name + "_codes")
            plane = held([P, width], U8, name + "_plane")
            for cols in parts(width):
                nc.vector.quantize_mx(
                    out=codes[:, cols].bitcast(FP8X4),
                    scales=plane[:, cols],
                    in_=woven[:, cols, :].rearrange("p c j -> p (c j)"),
                )
            return codes, plane

        def add_up(passes):
            for j, (acc, lhs, lhs_plane, rhs, rhs_plane) in enumerate(passes):
                nc.tensor.matmul_mx(
                    out=acc, lhsT=lhs, lhsT_scale=lhs_plane, rhs=rhs, rhs_scale=rhs_plane,
                    start=(j == 0), stop=(j == len(passes) - 1),
                )

        warm = held([P, 2], F32, "warm")
        nc.gpsimd.memset(warm[:, 0:1], 0.0)
        nc.scalar.activation(warm[:, 1:2], warm[:, 0:1], SIGMOID)

        offs_sb = load_list(offs, "offs_sb")
        tab_scale_rows = staged([P, T], U8, "tab_rows", TAB_SCALES_AT)
        nc.sync.dma_start(
            out=tab_scale_rows[SCALE_ROWS_AT:P, :].bitcast(I32),
            in_=tab_scales.rearrange("a q t -> q a t").bitcast(I32),
        )
        w1_plane = held([P, PASSES * H], U8, "w1_plane")
        nc.gpsimd.memset(w1_plane[:].bitcast(I32), 0)
        nc.vector.memset(tab_scale_rows[0:SCALE_ROWS_AT, :].bitcast(I32), 0)
        picked_plane = held([P, PASSES * S], U8, "picked_plane")
        nc.vector.memset(picked_plane[:].bitcast(I32), 0)
        tab_sb = [load_tab(0)]
        for r in range(4):
            nc.sync.dma_start(
                out=w1_plane[r:P:QUADRANT, :].rearrange("q (a c) -> q a c", a=PASSES).bitcast(I32),
                in_=w1_scales[:, r:16:4, :].rearrange("a q c -> q a c").bitcast(I32),
            )
        tab_sb.append(load_tab(1))
        w1_raw = [load_w1(0, held([P, PASSES, 2 * K_PASS], U8, "w1_first"))]
        pos1_sb = load_list(pos1, "pos1_sb")

        zeros = held([P, P * PACK], BF16, "woven2")
        nc.vector.memset(zeros[:].bitcast(I32), 0)
        zero_codes = held([P, BANK], U32, "gate0")
        nc.gpsimd.memset(zero_codes[:, P:BANK].bitcast(I32), 0)
        zero_plane = held([P, P], U8, "zero_plane")
        nc.vector.quantize_mx(out=zero_codes[:, 0:P].bitcast(FP8X4), scales=zero_plane[:], in_=zeros[:])
        idle_bank = bank_tile(BANKS - 1, [P, BANK])
        for turn in range(WARM_PASSES):
            add_up([(
                idle_bank[:], zero_codes[:, 0:P].bitcast(FP8X4), zero_plane[:],
                zero_codes[:].bitcast(FP8X4), w1_plane[:, 0:BANK],
            )])

        picked_scale_rows = staged([P, S], U8, "picked_rows", PICKED_ROWS_AT)
        nc.vector.tensor_copy(picked_scale_rows[:], tab_scale_rows[:].indirect(offs_sb[:]))
        for q in (0, 2, 1, 3):
            first_row = SCALE_ROWS_AT + 8 * q
            nc.sync.dma_start(
                out=picked_plane[QUADRANT * q : QUADRANT * q + 4, :].bitcast(I32),
                in_=picked_scale_rows[first_row : first_row + 8, :].bitcast(I32),
            )
        w2_raw = {(a, 0): load_w2(a, 0) for a in range(PASSES)}
        w1_raw.append(load_w1(1, staged([P, PASSES, 2 * K_PASS], U8, "w1_second", W1_SECOND_AT)))
        pos3_sb = load_list(pos3, "pos3_sb")
        pos2_sb = load_list(pos2, "pos2_sb")
        w2_raw[0, 1] = load_w2(0, 1)

        picked = [held([P, S], U32, "picked%d" % a) for a in range(PASSES)]
        w1_sorted = [held([P, PASSES, 2 * K_PASS], U8, "w1_sorted%d" % b) for b in range(2)]
        w1_sorted_plane = [held([P, PASSES, K_PASS], U8, "w1_sorted_plane%d" % b) for b in range(2)]

        def pick_words(a, parts):
            for places in parts:
                nc.vector.tensor_copy(picked[a][:, places], tab_sb[a][:].indirect(entries(offs_sb, places)))

        def sort_plane(b):
            cols = slice(b * K_PASS, (b + 1) * K_PASS)
            nc.gpsimd.tensor_copy(
                w1_sorted_plane[b][:].rearrange("p a (t g m) -> p a g t m", t=PACK, m=16),
                w1_plane[:].rearrange("p (a c) -> p a c", a=PASSES)[:, :, cols].rearrange(
                    "p a (g m t) -> p a g t m", t=PACK, m=16
                ),
            )

        def w1_columns(a, i):
            b, t = divmod(i, PACK)
            codes = w1_sorted[b][:, a, 2 * P * t : 2 * P * (t + 1)].bitcast(FP4X4)
            return codes, w1_sorted_plane[b][:, a, P * t : P * (t + 1)]

        w2_mx = {}

        def w2_columns(a, i):
            b, t = divmod(i, PACK)
            codes, plane = w2_mx[a, b]
            return codes[:, P * t : P * (t + 1)].bitcast(FP8X4), plane[:, P * t : P * (t + 1)]

        def picked_columns(a, cols):
            return picked[a][:, cols].bitcast(FP8X4), picked_plane[:, a * S + cols.start : a * S + cols.stop]

        def fill_bank(number, stationary, parts, order):
            acc = bank_tile(number, [P, BANK])
            width = BANK // len(parts)
            sums = [acc[:, n * width : (n + 1) * width] for n in range(len(parts))]
            add_up([
                (sums[n],) + stationary(a, i) + picked_columns(a, cols)
                for a in order
                for n, (i, cols) in enumerate(parts)
            ])
            return sums

        def tile_banks(number, stationary, i, window):
            return [
                (fill_bank(number + h, stationary, [(i, cols)], (1, 0))[0], window[:, cols])
                for h, cols in enumerate(halves(S))
            ]

        def empty_banks(filled):
            for acc, window in filled[-1:] + filled[:-1]:
                nc.scalar.copy(window, acc)

        def weave(raw, woven):
            nc.vector.tensor_copy(
                woven.rearrange("p (g i) j -> p g j i", i=RUN), raw.rearrange("p j (g i) -> p g j i", i=RUN)
            )

        def w2_piece(a, b, name):
            woven = held([P, K_PASS, PACK], BF16, name)
            for pair in halves(PACK):
                nc.vector.tensor_copy(
                    woven[:].rearrange("p (t m) j -> p m j t", t=PACK)[:, :, :, pair],
                    w2_raw[a, b][:].rearrange("p j (m t) -> p m j t", t=PACK)[:, :, :, pair],
                )
            w2_mx[a, b] = quantize(woven, "w2_%d%d" % (a, b), halves)

        def pick_gates(gates, window, offsets):
            nc.scalar.activation(gates, window[:].indirect(offsets), SIGMOID, scale=-1.0)

        def make_z(values, gates, woven, parts):
            for cols in parts(values.shape[2]):
                nc.vector.tensor_tensor(
                    woven[:, cols, :].rearrange("p (g i) t -> p g t i", i=RUN),
                    values[:, :, cols].rearrange("p t (g i) -> p g t i", i=RUN),
                    gates[:, :, cols].rearrange("p t (g i) -> p g t i", i=RUN),
                    MULT,
                )

        pick_words(0, halves(S))
        for t in range(PACK):
            nc.scalar.copy(
                w1_sorted[0][:].bitcast(U16).rearrange("p a (t m) -> p a t m", t=PACK)[:, :, t, :],
                w1_raw[0][:].bitcast(U16).rearrange("p a (m t) -> p a t m", t=PACK)[:, :, t, :],
            )
        sort_plane(0)
        sort_plane(1)
        pick_words(1, halves(S))

        head = {i: held([P, S], F32, "head%d" % i) for i in range(TILES) if i != 3}
        head[3] = staged([P, S], F32, "head3", W2_AT[1, 0])
        ann = [held([P, S], F32, "ann%d" % i) for i in range(TILES)]
        first_gates = held([P, PACK, ARCS], F32, "gate0")
        low, high = halves(S)
        early = [(0, low), (1, low), (2, low), (0, high), (1, high), (2, high), (3, low), (3, high)]
        early_sums = [
            fill_bank(number, w1_columns, [part], (0, 1) if number < 2 else (1, 0))[0]
            for number, part in enumerate(early)
        ]

        def empty_early(number, copy, share=slice(0, BANK)):
            i, cols = early[number]
            copy(head[i][:, cols][:, share], early_sums[number][:, share])

        for number in (0, 1, 2):
            empty_early(number, nc.scalar.copy)
        w2_piece(0, 0, "woven0")
        empty_early(3, nc.scalar.copy)
        empty_early(4, nc.scalar.copy, slice(GAP_SHARE, BANK))
        empty_early(4, nc.vector.tensor_copy, slice(0, GAP_SHARE))
        pick_gates(first_gates[:, 0, :], head[0], pos1_sb[:])
        empty_early(5, nc.scalar.copy)
        pick_gates(first_gates[:, 1, :], head[1], pos1_sb[:])
        w2_piece(1, 0, "woven1")
        empty_early(6, nc.vector.tensor_copy, slice(0, LATE_SHARE))
        empty_early(6, nc.scalar.copy, slice(LATE_SHARE, BANK))
        empty_early(7, nc.vector.tensor_copy)
        w2_raw[1, 1] = load_w2(1, 1)
        gain_sb = staged([P, 2, PACK], F32, "gain_sb", GAIN_AT)
        nc.sync.dma_start(out=gain_sb[:], in_=gain.rearrange("(b p t) -> p b t", b=2, t=PACK))
        nc.vector.tensor_copy(
            w1_sorted[1][:].bitcast(U16).rearrange("p a (t g m) -> p a g t m", t=PACK, m=8),
            w1_raw[1][:].bitcast(U16).rearrange("p a (g m t) -> p a g t m", t=PACK, m=8),
        )
        w2_piece(0, 1, "woven2")
        w2_piece(1, 1, "woven0")

        late_tile = staged([P, (2 * PASSES * PACK + 1) * BANK], F32, "late_rows", LATE_ROWS_AT)
        late_rows = late_tile[:, BANK:].rearrange("p (n j c) -> p n j c", j=PACK, c=BANK)
        first_weighted = late_tile[:, 0 : 2 * PASSES * PACK * BANK].rearrange("p (t j c) -> p t j c", j=PACK, c=BANK)
        for n, src in enumerate((guide, w4)):
            nc.sync.dma_start(
                out=late_rows[:, PASSES * n : PASSES * (n + 1), :, :],
                in_=src.rearrange("(a p j) c -> p a j c", a=PASSES, j=PACK),
            )
        w3_sb = held([P, 2, N], U32, "woven2")
        nc.sync.dma_start(out=w3_sb[:].bitcast(I32), in_=w3_words.rearrange("a p c i -> p a (c i)").bitcast(I32))
        weighted = [first_weighted[:, :, 0, :], held([P, PACK, ARCS], F32, "weighted1")[:]]
        z0_woven = staged([P, ARCS, PACK], BF16, "z0_woven", W2_AT[1, 1] + 4 * KIB)
        third = {}
        diff = {}
        late_mx = {}

        def pick_third(i):
            if i < 2:
                third[i] = first_gates[:, 2 + i, :]
            else:
                third[i] = held([P, ARCS], F32, "third%d" % i)[:]
            nc.scalar.activation(third[i], ann[i][:].indirect(pos3_sb[:]), COPY)

        def subtract(i):
            if i < 2:
                diff[i] = staged([P, ARCS], F32, "diff%d" % i, W2_AT[1, 1] + 2 * KIB * i)[:]
            elif i < 6:
                diff[i] = late_rows[:, 2 * (i // 2 - 1), i % 2, :]
            else:
                diff[i] = held([P, ARCS], F32, "third%d" % (i - 4))[:]
            nc.vector.tensor_tensor(diff[i], ann[i][:].indirect(pos2_sb[:]), third[i], SUBTRACT)

        def square(i, parts):
            b, t = divmod(i, PACK)
            for arcs in parts(ARCS):
                nc.vector.scalar_tensor_tensor(
                    weighted[b][:, t, arcs], diff[i][:, arcs], gain_sb[:, b, t : t + 1], diff[i][:, arcs], MULT, MULT
                )

        for pair in range(TILES // 2):
            even, odd = 2 * pair, 2 * pair + 1
            filled = [tile_banks(2 * i, w2_columns, i, ann[i]) for i in (even, odd)]
            if pair == 0:
                empty_banks(filled[0])
                empty_banks(filled[1])
            else:
                empty_banks(filled[0] + filled[1])
            pick_third(even)
            pick_third(odd)
            if pair == 0:
                subtract(even)
                subtract(odd)
                square(even, whole)
            elif pair < 3:
                n = pair - 1
                late_woven = staged([P, PASSES * BANK, PACK], BF16, "late_woven%d" % n, W2_AT[0, 1])
                for a in range(PASSES):
                    weave(late_rows[:, PASSES * n + a, :, :], late_woven[:, a * BANK : (a + 1) * BANK, :])
                subtract(odd)
                late_mx[n] = quantize(late_woven, "late%d" % n, whole)
                subtract(even)
                square(even - 1, whole)
                square(even, whole)
            else:
                for t in (2, 3):
                    pick_gates(first_gates[:, t, :], head[t], pos1_sb[:])
                subtract(odd)
                square(even - 1, whole)
                subtract(even)
                make_z(weighted[0], first_gates[:], z0_woven, whole)
                square(odd, whole)
                z0_mx = quantize(z0_woven, "z0", whole)
                square(even, halves)

        for h, cols in enumerate(halves(S)):
            empty_banks([
                (fill_bank(PACK * h + t, w1_columns, [(PACK + t, cols)], (1, 0))[0], head[PACK + t][:, cols])
                for t in range(PACK)
            ])
        for q in range(4):
            nc.sync.dma_start(
                out=picked_plane[QUADRANT * q + 4 : QUADRANT * q + 12, 0:N].bitcast(I32),
                in_=w3_scales[:, 4 * q : 4 * q + 4, :].bitcast(I32),
            )
        z1_mx = []
        for u, arcs in enumerate(ARC_PIECES):
            width = arcs.stop - arcs.start
            woven = held([P, width, PACK], BF16, "z1%d_woven" % u)
            step = width // GATE_PARTS[u]
            for at in range(0, width, step):
                places = slice(arcs.start + at, arcs.start + at + step)
                gates = staged([P, PACK, step], F32, "gate1_%d" % places.start, W2_AT[0, 0] + 16 * places.start)
                for t in range(PACK):
                    pick_gates(gates[:, t, :], head[PACK + t], entries(pos1_sb, places))
                make_z(weighted[1][:, :, places], gates[:], woven[:, at : at + step, :], halves if step == width else whole)
            z1_mx.append(quantize(woven, "z1%d" % u, halves))

        (guide_codes, guide_plane), (w4_codes, w4_plane) = late_mx[0], late_mx[1]
        number = 0
        for u, arcs in enumerate(ARC_PIECES):
            width = arcs.stop - arcs.start
            last = u == len(ARC_PIECES) - 1
            per_bank = N // P // 2 if last else BANK // width
            result = held([P, N // P, width], F32, "head%d" % u)
            stored = out[:, arcs].rearrange("(n p) m -> p n m", p=P)
            operands = []
            for a in range(PASSES):
                own, cols = slice(a * N, (a + 1) * N), slice(a * ARCS + arcs.start, a * ARCS + arcs.stop)
                operands.append((w4_codes[:, own], w4_plane[:, own], guide_codes[:, cols], guide_plane[:, cols]))
            operands.append((w3_sb[:, 0, :], picked_plane[4:P, 0:N], z0_mx[0][:, arcs], z0_mx[1][:, arcs]))
            operands.append((w3_sb[:, 1, :], picked_plane[8:P, 0:N], z1_mx[u][0][:], z1_mx[u][1][:]))
            for at in range(0, N // P, per_bank):
                acc = bank_tile(OUT_BANKS[number], [P, per_bank, width])
                number = number + 1
                add_up([
                    (
                        acc[:, n, :], lhs[:, (at + n) * P : (at + n + 1) * P].bitcast(FP8X4),
                        lhs_plane[:, (at + n) * P : (at + n + 1) * P], rhs.bitcast(FP8X4), rhs_plane,
                    )
                    for lhs, lhs_plane, rhs, rhs_plane in operands
                    for n in range(per_bank)
                ])
                part = slice(at, at + per_bank)
                if u > 0 and at == 0:
                    nc.vector.tensor_copy(result[:, part, :], acc[:])
                else:
                    nc.scalar.copy(result[:, part, :], acc[:])
                queue = nc.scalar if last and at > 0 else nc.sync
                queue.dma_start(out=stored[:, part, :], in_=result[:, part, :])
